import numpy as np, ml_dtypes
CORES = [25,29,65,69,153,157,193,197]
N = 8
import mx_ref
BF = ml_dtypes.bfloat16
def gentries(a):
    return np.ascontiguousarray(a.reshape(8, 16, -1).transpose(0, 2, 1)).reshape(8, -1)
def gtable(e):
    e = np.asarray(e); return np.ascontiguousarray(e.reshape(8, -1, 16).transpose(0, 2, 1)).reshape(128, -1).astype(np.int32)
def gcols(t, e):
    v = np.concatenate([t.reshape(8, 16, -1, 4), np.zeros((8, 16, 1, 4), BF)], axis=2)
    return np.ascontiguousarray(np.stack([v[g][:, e[g]] for g in range(8)])).reshape(128, -1)
def tile(rs):
    return np.stack(rs, axis=2).reshape(128, -1).astype(BF)
def pick(q, e):
    c = np.concatenate([q[0].reshape(128, -1, 4), np.zeros((128, 1, 4), np.uint8)], axis=1); s = np.concatenate([q[1], np.ones((16, 1), np.uint8)], axis=1)
    return (np.ascontiguousarray(c[:, e].reshape(128, -1)), np.ascontiguousarray(s[:, e]))
def join(*qs):
    return (np.concatenate([q[0] for q in qs], axis=1), np.concatenate([q[1] for q in qs], axis=1))
def put(q, e, v):
    c, s = q[0].reshape(128, -1, 4).copy(), q[1].copy(); c[:, e] = v[0].reshape(128, -1, 4); s[:, e] = v[1]
    return (c.reshape(128, -1), s)
def pk(c, s):
    return (np.ascontiguousarray(c), mx_ref.live(s))
def emit(q):
    return q[0], q[1]
def packed(v, rng):
    q = [mx_ref.quantize(np.ascontiguousarray(v[r])) for r in range(N)]
    return np.stack([a for a, b in q]), np.stack([mx_ref.plane(b, rng) for a, b in q])
def values_of_codes():
    e, c = np.zeros((128, 128, 4), np.float32), np.zeros((128, 2, 4), np.uint8)
    e[np.arange(128), np.arange(128), 0] = 1
    c[:127, :, 0] = np.arange(256).reshape(2, 128).T[:127]
    return mx_ref.matmul(mx_ref.quantize(e.reshape(128, 512).astype(BF)), (c.reshape(128, 8), np.full((16, 2), 127, np.uint8))).T.reshape(-1).astype(np.float64)
CODE_VALUE, SCALE_VALUE = values_of_codes(), 2.0 ** (np.arange(256) - 127.0)
def decode(q):
    return (CODE_VALUE[q[0]].reshape(16, 8, -1, 4) * SCALE_VALUE[q[1]][:, None, :, None] + 0.0).reshape(128, -1).astype(np.float32)
def f(rng, *shape):
    return mx_ref.flush((rng.standard_normal(shape, dtype=np.float32) * np.exp2(rng.integers(-2, 3, shape[:-1] + (1,)))).astype(BF))
def wide(rng, *shape, cols=0):
    v = rng.standard_normal(shape, dtype=np.float32) * np.exp2(rng.integers(-12, 13, shape)).astype(np.float32)
    if cols: v *= np.repeat(np.exp2(rng.integers(-cols, cols + 1, shape[:-2] + (1, shape[-1] // 4))) * (rng.random(shape[:-2] + (1, shape[-1] // 4)) > 0.0625), 4, axis=-1).astype(np.float32)
    return mx_ref.flush(v.astype(BF))
C = 288
STEP = [4, 1, 2]
def take(a, e):
    return np.take_along_axis(a, e, axis=-1)
def effective(back):
    e = np.ones(back.shape, bool)
    for j in range(C - 1, -1, -1):
        up = back[..., j]
        e[..., j] = (up <= j) | ~take(e, up[..., None])[..., 0]
    return e
def numbers_of(rng):
    return {"x": np.array(f(rng, N, 128, 4 * C)), "u": np.array(f(rng, N, 128, 512)), "v": np.array(f(rng, N, 128, 512))}
def stored(back, ring, mate):
    return {k: np.stack([gtable(e[r]) for r in range(N)]) for k, e in (("ud", np.argsort(back, axis=-1)), ("iv", back), ("hp", ring), ("mt", mate))}
def shuffled(rng):
    return rng.permuted(np.tile(np.arange(C), (N, 8, 1)), axis=2)
def linked(order):
    e = np.zeros_like(order)
    np.put_along_axis(e, order, np.roll(order, -1, axis=-1), axis=-1)
    return e
def mates(rng):
    a = shuffled(rng)
    e = np.zeros_like(a)
    np.put_along_axis(e, a[..., ::2], a[..., 1::2], axis=-1)
    np.put_along_axis(e, a[..., 1::2], a[..., ::2], axis=-1)
    return e
def runs(rng, back):
    return linked(np.argsort(effective(back) + rng.random(back.shape), axis=-1))
def lists(rng):
    return stored(shuffled(rng), linked(shuffled(rng)), mates(rng))
def layers(rng, still=()):
    w = np.array(f(rng, N, 128, 2048)).reshape(N, 8, 16, 4, 8, 16, 4)
    for i in still:
        w[:, :, i] = 0
        w[:, :, :, :, :, i] = 0
    return w
def weights(rng, w):
    c, s = packed(np.ascontiguousarray(w).reshape(N, 128, 2048), rng)
    return {"wc": c, "ws": s}
def setup_inputs(rng):
    return {**numbers_of(rng), **lists(rng), **weights(rng, layers(rng))}
def setup_inputs_ties(rng):
    d = numbers_of(rng)
    o = rng.permutation(N)
    k = rng.choice([-1.0, 0.0, 1.0, 1.0], (N, 8, C))
    k[o[0]] = 0
    k[o[1]] = 1
    k[o[2]] = (rng.permutation(8) % 2 * 2.0 - 1.0)[:, None]
    x = d["x"].reshape(N, 8, 16, C, 4)
    x[:, :, 0] = 0
    x[:, :, 0, :, 0] = k.astype(np.float32).astype(BF)
    u = d["u"].reshape(N, 128, 128, 4)
    u[:, :, ::16] = 0
    for h in range(0, 128, 16): u[:, h, h, 0] = 1
    back = np.zeros((N, 8, C), np.int64)
    for r in range(N):
        for g, m in enumerate(rng.permutation([1, 1, 1, 2, 2, 3, C // 8, 0])):
            a = rng.integers(0, m, C) if m else np.arange(C)
            for i in np.unique(a):
                e = np.flatnonzero(a == i)
                back[r, g, e] = np.roll(e, -1)
    mate = mates(rng)
    tau = np.where((k > 0) & (take(k, mate) > 0), mate, np.arange(C))
    return {"x": x.reshape(N, 128, 4 * C), "u": u.reshape(N, 128, 512), "v": d["v"], **stored(take(tau, back), runs(rng, back), mate), **weights(rng, layers(rng, [0]))}
def setup_inputs_near(rng):
    d = numbers_of(rng)
    i = np.arange(N)
    first = np.minimum(i, i ^ STEP[0])
    small = np.isin(first, rng.permutation(np.unique(first))[:N // 4])
    k = np.where(small, 2.0 ** -30, 1.0)
    x = d["x"].astype(np.float32).reshape(N, 8, 16, C, 4)
    x[:, :, :8] = 0
    s = rng.choice([-1.0, 0.0, 1.0, 1.0], (N, 8, C)) * k[:, None, None]
    x[:, :, 0, :, 0] = 1.125 * s
    x[:, :, 1, :, 0] = -1.25 * s
    x[:, :, 3, :, 0] = np.where(small[:, None, None], rng.choice([-1.0, 1.0], (N, 8, C)) * 2.0 ** -30, 0.0)
    x[:, :, 4, :, 0] = np.where(small, 2.0 ** -27, 0.0)[:, None, None]
    u = d["u"].reshape(N, 128, 128, 4)
    u[:, :, ::16] = 0
    w = layers(rng, range(8))
    for r in range(N):
        at = [0, C - 1, int(rng.integers(C)), int(rng.integers(C))]
        for g, j in zip(rng.permutation(8)[:4], at): x[r, g, 0, j, 0] = 2.0 ** 30 * rng.choice([-1.0, 1.0])
        for g in range(8):
            h = 16 * g
            u[r, h, h, 0] = 1.125 * k[r]
            u[r, h + 1, h, 0] = k[r]
            u[r, h + 2, h, 0] = 1.125 * k[r]
            u[r, h + 5, h, 0] = k[r]
            if small[r]:
                w[r, g, 3, 0, g, 2, 0] = 2.0 ** -7
                w[r, g, 3, 0, g, 5, 0] = -2.0 ** -7
    return {"x": x.reshape(N, 128, 4 * C).astype(BF), "u": u.reshape(N, 128, 512), "v": d["v"], **lists(rng), **weights(rng, w)}
def setup_inputs_odd(rng):
    d = numbers_of(rng)
    x = (1.0 + (2 * rng.integers(0, 64, (N, 16, 8, C, 4)) + 1) * 2.0 ** -7) * np.exp2(-rng.integers(0, 7, (N, 16, 8, C, 4)).astype(np.float64)) * rng.choice([-1.0, 1.0], (N, 16, 8, C, 4))
    x[:, ::2] = 0
    x[:, :, 0, :, 0] = 1.96875 * 2.0 ** 8 * rng.choice([-1.0, 1.0], (N, 16, C))
    x[:, ::2, 1, :, 0] = (1.0 + 0.125 * (rng.random((N, 8, C)) < 0.75)) * 2.0 ** -5
    x[:, ::2, 2, :, 0] = (1.0 + 0.125 * (rng.random((N, 8, C)) < 0.25)) * 2.0 ** -5
    x[:, 14, 0, :, 1] = 16.0
    u = d["u"].reshape(N, 128, 128, 4)
    u[:, :, ::16] = 0
    for h in range(0, 128, 16):
        u[:, h + 1, h, 0] = 1
        u[:, h + 2, h, 0] = -1
        u[:, h + 3, h, 0] = 1
    w = layers(rng, [0, 1, 2, 8])
    w[:, 7, 0, 0, :, 0, 1] = -16.0
    return {"x": x.astype(np.float32).reshape(N, 128, 4 * C).astype(BF), "u": u.reshape(N, 128, 512), "v": d["v"], **lists(rng), **weights(rng, w)}
def setup_inputs_ends(rng):
    d = numbers_of(rng)
    x = np.zeros((N, 8, 16, C, 4))
    u = d["u"].astype(np.float32).reshape(N, 128, 128, 4)
    v = d["v"].astype(np.float32)
    w = np.zeros((N, 128, 4, 128, 4), np.float32)
    o, kinds = np.zeros(N, np.int64), rng.permutation(4)
    left = rng.permutation(np.unique(np.minimum(np.arange(N), np.arange(N) ^ STEP[0])))
    o[left] = kinds[:N // 2]
    o[left ^ STEP[0]] = kinds[(np.arange(N // 2) + 2) % 4]
    i, j = np.arange(128), np.arange(C)
    turns = np.stack([j ^ 1, C - 1 - j, (j + C // 2) % C])
    ways = np.stack([np.roll(j, -1), j, C - 1 - j, np.roll(j, 1)])
    mate = np.stack([turns[rng.permutation(8) % 3] for r in range(N)])
    plan = np.stack([ways[rng.permutation(8) % 4] for r in range(N)])
    ring, back = runs(rng, plan), plan.copy()
    for r in range(N):
        h = rng.permutation(8)
        sign = np.where(h < 2, 0.0, h % 2 * 2.0 - 1.0)
        c = sign[None, :, None]
        e = rng.permutation(8)
        ring[r, e[:2]] = np.roll(j, -1)
        ring[r, e[2:4]] = np.roll(j, 1)
        if o[r] in (0, 2): back[r, sign < 0] = take(mate[r], plan[r])[sign < 0]
        low = -(0.9 + 0.1 * rng.random((8, 16, C, 4))) * 2.0 ** 30
        if o[r] == 0: x[r] = low
        if o[r] == 1: x[r] = np.where((rng.random(C) < 0.5)[:, None], (1.0 + 0.4 * rng.random((8, 16, C, 4))) * 2.0 ** 27, low)
        if o[r] == 2: x[r] = -(1.0 + 0.125 * rng.integers(0, 8, (8, 16, C, 4))) * 2.0 ** -30
        if o[r] == 3: x[r] = d["x"][r].astype(np.float32).reshape(8, 16, C, 4)[:, :, :1]
        if o[r] < 2:
            x[r, 7, 15, :, 3] *= 2.0 ** -6
            u[r, :, ::16] = c * (0.9 + 0.1 * rng.random((128, 8, 4))) * 2.0 ** 30
            v[r] = rng.choice([-1.0, 1.0], (128, 512)) * (0.9 + 0.1 * rng.random((128, 512))) * 2.0 ** 30
        if o[r] == 2:
            u[r, :, ::16] = c * (1.0 + 0.125 * rng.integers(0, 8, (128, 8, 4))) * 2.0 ** -30
            v[r] = rng.choice([-1.0, 1.0], (128, 512)) * (1.0 + 0.125 * rng.integers(0, 8, (128, 512))) * 2.0 ** -30
        if o[r] == 3: u[r, :, ::16] *= np.abs(c).astype(np.float32)
        k = np.array([8.0, 16.0, 32.0])[rng.permutation(8) % 3]
        for b in range(4): w[r, i, b, i, b] = k[i // 16]
        if o[r] == 2:
            w[r, 127, 3, 127, 3] = 256.0
            w[r, 126, 3, 126, 3] = 2.0 ** -8
    return {"x": x.astype(np.float32).reshape(N, 128, 4 * C).astype(BF), "u": u.reshape(N, 128, 512).astype(BF), "v": v.astype(BF), **stored(back, ring, mate), **weights(rng, w.astype(BF))}
def setup_inputs_spread(rng):
    d = setup_inputs(rng)
    d["x"] = wide(rng, N, 128, 4 * C, cols=6)
    return d
def check_inputs(d):
    b = []
    for k in ("x", "u", "v"):
        a = np.abs(d[k].astype(np.float32))
        if not (np.isfinite(a).all() and ((a == 0) | (a >= 2.0 ** -30) & (a <= 2.0 ** 30)).all()): b.append("a value of " + k)
    none, least, most = [emit(mx_ref.quantize(np.full((128, 16), k, np.float32).astype(BF)))[1][0, 0] for k in (0.0, 2.0 ** -8, 2.0 ** 8)]
    own = np.arange(C)
    for r in range(N):
        ud, iv, hp, mt = [gentries(d[k][r]) for k in ("ud", "iv", "hp", "mt")]
        if any(((a < 0) | (a >= C)).any() for a in (ud, iv, hp, mt)): b.append("an entry of a list")
        else:
            if (np.sort(ud, axis=1) != own).any(): b.append("ud: a permutation")
            if (take(ud, iv) != own).any(): b.append("iv: the inverse of ud")
            if (take(mt, mt) != own).any() or (mt == own).any(): b.append("mt: pairs of columns")
            at, seen = np.zeros((8, 1), np.int64), np.zeros((8, C), bool)
            for j in range(C):
                at = take(hp, at)
                np.put_along_axis(seen, at, True, axis=1)
            if not seen.all(): b.append("hp: a ring")
        if ((d["wc"][r] == 0x7F) | (d["wc"][r] == 0xFF)).any(): b.append("wc: a code that is no number")
        s = mx_ref.live(d["ws"][r])
        if ((s != none) & ((s < least) | (s > most))).any(): b.append("ws: a scale out of range")
    return b
def halfsum(s, t):
    return ((s.astype(np.float32) + t.astype(np.float32)) * np.float32(0.5)).astype(BF)
def reference(x, u, v, ud, iv, hp, mt, wc, ws):
    qu = [mx_ref.quantize(u[r]) for r in range(N)]
    lay = [pk(wc[r], ws[r]) for r in range(N)]
    to, back, ring, mate = [[gentries(a[r]) for r in range(N)] for a in (ud, iv, hp, mt)]
    now = [x[r] for r in range(N)]
    for step in STEP:
        t, past, sent = [], [], []
        for r in range(N):
            q = mx_ref.quantize(now[r])
            s = mx_ref.matmul(qu[r], q)[::16] > 0
            t.append(decode(q).astype(BF))
            tau = np.where(s & take(s, mate[r]), mate[r], np.arange(C))
            to[r], back[r] = take(to[r], tau), take(tau, back[r])
            e, b = effective(back[r]), ring[r]
            while not take(e, b).all(): b = np.where(take(e, b), b, take(ring[r], b))
            past.append(b)
            sent.append(mx_ref.quantize(halfsum(gcols(t[r], b), gcols(t[r], back[r]))))
        for r in range(N):
            p = r ^ step
            h = tile([mx_ref.matmul(pick(lay[r], np.arange(128 * b, 128 * b + 128)), sent[p]) * np.float32(0.03125) for b in range(4)])
            now[r] = halfsum(gcols(t[r], to[r]), gcols(h, take(past[p], back[r])))
    y, uo = np.zeros((N, 128, C), np.float32), np.zeros((N, 8, C), np.float32)
    oc, osc = np.zeros((N, 128, 4 * C), np.uint8), np.zeros((N, 16, C), np.uint8)
    for r in range(N):
        q = mx_ref.quantize(now[r])
        y[r] = mx_ref.matmul(mx_ref.quantize(v[r]), q)
        uo[r] = to[r]
        oc[r], osc[r] = emit(q)
    return {"y": y, "uo": uo, "oc": oc, "osc": osc}

@@ -1,0 +1,491 @@
+from concourse.mybir import dt, AluOpType, ActivationFunctionType
+
+C, KW = 288, 18
+STEP = (4, 1, 2)
+MID = 145
+BIG = 512.0
+SCAN = "float16"
+EARLY = (0, 1)
+CUT = 10
+
+SCRATCH = {}
+for _n in ("xin", "xt", "zt", "th", "tp", "tu", "gv", "hh"):
+    SCRATCH[_n] = ("sbuf", [128, 4 * C], "bfloat16")
+for _n in ("ut", "vt"):
+    SCRATCH[_n] = ("sbuf", [128, 512], "bfloat16")
+SCRATCH["et"] = ("sbuf", [128, 520], "bfloat16")
+for _n, _w in (("x0", C), ("x1", C), ("x2", C), ("x3", C), ("p0", C), ("p1", C), ("p2", C), ("z", C),
+               ("u", 128), ("ur", 128), ("v", 128), ("e", 512), ("w", 512)):
+    SCRATCH[_n + "q"] = ("sbuf", [128, _w], "float8_e4m3fn_x4")
+    SCRATCH[_n + "sc"] = ("sbuf", [128, _w], "uint8")
+for _n in ("iota", "win", "h1", "h2", "h4", "h8", "fl"):
+    SCRATCH[_n] = ("sbuf", [128, 304], "bfloat16")
+for _n in ("iom", "pat", "patf", "pp", "r1", "r2", "r3", "hx", "nf", "fo", "sa", "sb", "br", "uda", "udb", "mtr", "mr", "oo"):
+    SCRATCH[_n] = ("sbuf", [128, C], "bfloat16")
+SCRATCH["hpr"] = ("sbuf", [128, 9 * C], "bfloat16")
+for _n in ("c0", "c1", "c2", "c3"):
+    SCRATCH[_n] = ("sbuf", [128, C], SCAN)
+SCRATCH["pati"] = ("sbuf", [128, C], "int32")
+for _n in ("ivl", "mtl", "udl", "hpl"):
+    SCRATCH[_n] = ("sbuf", [128, KW], "int32")
+SCRATCH["qi"] = ("sbuf", [128, 8], "int32")
+for _n in ("corr", "thr", "qz"):
+    SCRATCH[_n] = ("sbuf", [128, 8], "float32")
+for _n in ("k16", "kb", "jw", "mtw", "dtw", "t1", "t3", "bj", "dj", "tf", "diw", "di2"):
+    SCRATCH[_n] = ("sbuf", [128, KW], "float32")
+for _n in ("jw2", "im0", "im1", "ta", "tb", "nim", "fm0", "fm1", "fmo"):
+    SCRATCH[_n] = ("sbuf", [128, 2 * KW], "float32")
+LOCAL = ("iv0", "mi", "mto", "udo", "wino", "off1", "poso", "tauo", "udi")
+SCRATCH["lloc"] = ("sbuf", [128, len(LOCAL) * KW], "uint16")
+for _n in ("iv1", "iv2", "iv3", "bo0", "bo1", "bo2", "eo0", "eo1", "eo2",
+           "ivp0", "ivp1", "ivp2", "bp0", "bp1", "bp2", "ep0", "ep1", "ep2", "hoff", "foff", "ordo"):
+    SCRATCH["l" + _n] = ("sbuf", [128, 4 * KW if _n == "hoff" else KW], "uint16")
+SCRATCH["lhp"] = ("sbuf", [128, 8 * KW], "uint16")
+SCRATCH["luo"] = ("sbuf", [128, 8], "uint16")
+SCRATCH["uoi"] = ("sbuf", [128, 8], "int32")
+SCRATCH["udf"] = ("sbuf", [128, C], "float32")
+SCRATCH["yf"] = ("sbuf", [128, C], "float32")
+SCRATCH["ps"] = ("psum", [128, 4096], "float32")
+
+SEMAPHORES = ["cv", "cs", "ct", "cg", "snt"] + ["d%d" % i for i in range(20)]
+SEMAPHORES += ["%s%d" % (a, i) for a in ("rx", "ri", "rb", "re") for i in range(3)]
+
+MUL, ADD, SUB, MAX, MIN = AluOpType.mult, AluOpType.add, AluOpType.subtract, AluOpType.max, AluOpType.min
+GT, GE, EQ = AluOpType.is_gt, AluOpType.is_ge, AluOpType.is_equal
+COPY, IDENT, SIGN = ActivationFunctionType.Copy, ActivationFunctionType.Identity, ActivationFunctionType.Sign
+
+
+def relays(topo, src, dst):
+    if topo.may_write(src, dst):
+        return None
+    c = [a for a in topo.cores_of(src) if a != src and topo.may_write(a, dst)]
+    near = [a for a in c if topo.die(a) == topo.die(src)]
+    far = [a for a in c if topo.die(a) != topo.die(src)]
+    return (near + far)[:2]
+
+
+def rank_program(g, core, T, topo):
+    rank = T.rank_of(core)
+    sent = [0]
+
+    def put(dst, out, in_, sem):
+        e = topo.engines(core, dst)[:8]
+        rid, pid = topo.addr(dst, core)
+        m = 0
+        for a in e:
+            m |= 1 << a
+        g.remote_dma(out, in_, T.sem[sem], T.sem.snt, pid, rid, m)
+        sent[0] += len(e)
+        return len(e)
+
+    def width(a, b):
+        return len(topo.engines(a, b)[:8])
+
+    def u8(ap):
+        return ap.bitcast(dt.uint8)
+
+    HALF = C // 2
+    if rank is None:
+        for rd, step in enumerate(STEP):
+            for r, src in enumerate(T.cores):
+                dst = T.cores[r ^ step]
+                rel = relays(topo, src, dst)
+                if not rel or core not in rel:
+                    continue
+                n = width(src, core)
+                if core == rel[0]:
+                    g.wait_ge(T.sem["rx%d" % rd], 2 * n)
+                    put(dst, u8(T["p%dq" % rd][:, 0:HALF]), u8(T["p%dq" % rd][:, 0:HALF]), "rx%d" % rd)
+                    put(dst, T["p%dsc" % rd][:], T["p%dsc" % rd][:], "rx%d" % rd)
+                else:
+                    g.wait_ge(T.sem["rx%d" % rd], n)
+                    put(dst, u8(T["p%dq" % rd][:, HALF:C]), u8(T["p%dq" % rd][:, HALF:C]), "rx%d" % rd)
+                    for s, b in (("ri", "livp"), ("rb", "lbp"), ("re", "lep")):
+                        g.wait_ge(T.sem["%s%d" % (s, rd)], n)
+                        put(dst, T["%s%d" % (b, rd)][:], T["%s%d" % (b, rd)][:], "%s%d" % (s, rd))
+        if sent[0]:
+            g.wait_ge(T.sem.snt, sent[0])
+        return
+
+    Q = {"v": g.vector, "s": g.scalar, "t": g.tensor, "g": g, "y": g.sync}
+    SEM = {"v": "cv", "s": "cs", "t": "ct", "g": "cg"}
+    cnt = {"v": 0, "s": 0, "t": 0, "g": 0}
+    clock = {q: {} for q in Q}
+    wr, rdr = {}, {}
+    nd = [0]
+    dsems = []
+
+    def sync(q, reads, writes):
+        need = []
+        for k in reads:
+            if k in wr:
+                need.append(wr[k])
+        for k in writes:
+            if k in wr:
+                need.append(wr[k])
+            need += rdr.get(k, [])
+        need.sort(key=lambda t: -t[1])
+        for sem, val, clk in need:
+            if clock[q].get(sem, 0) < val:
+                Q[q].wait_ge(T.sem[sem], val)
+                for a, b in clk.items():
+                    if clock[q].get(a, 0) < b:
+                        clock[q][a] = b
+
+    def done(q, sem, val, reads, writes):
+        clk = dict(clock[q])
+        clk[sem] = val
+        tok = (sem, val, clk)
+        for k in reads:
+            rdr.setdefault(k, []).append(tok)
+        for k in writes:
+            wr[k] = tok
+            rdr[k] = []
+
+    def op(q, call, reads, writes):
+        sync(q, reads, writes)
+        i = call(Q[q])
+        cnt[q] += 1
+        i.then_inc(T.sem[SEM[q]], 1)
+        done(q, SEM[q], cnt[q], reads, writes)
+
+    def dma(q, out, in_, reads, writes):
+        sem = "d%d" % nd[0]
+        nd[0] += 1
+        sync(q, reads, writes)
+        Q[q].dma_start(out, in_).then_inc(T.sem[sem], 16)
+        dsems.append(sem)
+        done(q, sem, 16, reads, writes)
+
+    def tt(out, a, b, o, reads, writes):
+        op("v", lambda e: e.tensor_tensor(out, a, b, o), reads, writes)
+
+    def ts(out, a, s1, o1, reads, writes, s2=None, o2=None):
+        if o2 is None:
+            op("v", lambda e: e.tensor_scalar(out, a, s1, None, o1), reads, writes)
+        else:
+            op("v", lambda e: e.tensor_scalar(out, a, s1, s2, o1, o2), reads, writes)
+
+    def cp(out, in_, reads, writes, q="v"):
+        if q == "v":
+            op("v", lambda e: e.tensor_copy(out, in_), reads, writes)
+        else:
+            op("s", lambda e: e.activation(out, in_, COPY), reads, writes)
+
+    def pick(out, win, off, reads, key, k=CUT):
+        if k < KW:
+            op("s", lambda e: e.activation(T[out][:, 16 * k:C], win.indirect(off(k, KW)), COPY), reads, [key + "s"])
+        op("v", lambda e: e.tensor_copy(T[out][:, 0:16 * k], win.indirect(off(0, k))), reads, [key])
+
+    rot = [0]
+
+    def scan(row, n, key, pat="pat"):
+        b = "c%d" % (rot[0] % 4)
+        rot[0] += 1
+        op("v", lambda e: e.tensor_tensor_scan(T[b][:, 0:n], row, T[pat][:, 0:n], -2 * BIG, MAX, ADD),
+           [key, key + "s", pat], [b])
+        return b, T[b][:, 15:n:16]
+
+    def wraps(jobs):
+        es = [scan(j[0], j[1], j[2], j[5] if len(j) > 5 else "pat") for j in jobs]
+        for (b, e), j in zip(es, jobs):
+            ts(j[3], e, T.corr[:, 0:1], ADD, [b, "corr"], [j[4]])
+
+    def wrap(*job):
+        wraps([job])
+
+    def lst(name, a=0, b=KW):
+        if name in LOCAL:
+            o = KW * LOCAL.index(name)
+            return T.lloc[:, o + a:o + b]
+        return T["l" + name][:, a:b]
+
+    dma("s", T.hpl[:], T.hp[:], [], ["hpl"])
+    dma("y", T.ut[:], T.u[:], [], ["ut"])
+    dma("s", T.ivl[:], T.iv[:], [], ["ivl"])
+    dma("s", T.mtl[:], T.mt[:], [], ["mtl"])
+    dma("y", T.xin[:], T.x[:], [], ["xin"])
+    dma("s", T.udl[:], T.ud[:], [], ["udl"])
+    dma("y", u8(T.wq[:]), T.wc[:], [], ["wq"])
+    dma("y", T.wsc[:], T.ws[:], [], ["wsc"])
+    dma("y", T.vt[:], T.v[:], [], ["vt"])
+
+    op("v", lambda e: e.memset(T.lordo[:], C - 1), [], ["lordo"])
+    op("g", lambda e: e.iota(T.qi[:], [[0, 8]], 0, 1), [], ["qi"])
+    op("g", lambda e: e.iota(T.pati[:], [[1, C]], 1024, -1), [], ["pati"])
+    op("g", lambda e: e.iota(T.iota[:], [[1, 304]], -MID, 0, allow_small_or_imprecise_dtypes=True), [], ["iota"])
+    op("v", lambda e: e.memset(T.et[:], 0.5), [], ["et"])
+    op("g", lambda e: e.iota(T.k16[:], [[16, KW]], 0, 0, allow_small_or_imprecise_dtypes=True), [], ["k16"])
+    op("g", lambda e: e.iota(T.kb[:], [[-32, KW // 2], [0, 2]], -32, 0, allow_small_or_imprecise_dtypes=True), [], ["kb"])
+    op("g", lambda e: e.iota(T.uoi[:], [[16, 8]], 0, 0), [], ["uoi"])
+    op("g", lambda e: e.iota(T.iom[:], [[1, C]], -1 - MID, 0, allow_small_or_imprecise_dtypes=True), [], ["iom"])
+    op("g", lambda e: e.affine_select(T.et[:], T.et[:], [[1, 520]], EQ, 0.0, -3, -4), ["et"], ["et"])
+    ts(T.qi[:], T.qi[:], 15, AluOpType.bitwise_and, ["qi"], ["qi"])
+    ts(T.qz[:], T.qi[:], 0.0, EQ, ["qi"], ["qz"])
+    ts(T.corr[:], T.qz[:], 2 * BIG, MUL, ["qz"], ["corr"], MID - BIG, ADD)
+    ts(T.pati[:], T.pati[:], 15, AluOpType.bitwise_and, ["pati"], ["pati"])
+    ts(T.pat[:], T.pati[:], 0.0, EQ, ["pati"], ["pat"], BIG, MUL)
+    ts(T.hx[:], T.pati[:], 15.0, EQ, ["pati"], ["hx"], -2 * BIG, MUL)
+    cp(T.lhp[:, 0:KW], T.hpl[:], ["hpl"], ["lhp0"])
+    cp(T.hpr[:, 0:C], T.iota[:, 0:C].indirect(T.lhp[:, 0:KW]), ["iota", "lhp0"], ["hpr0"], "s")
+    tt(T.pat[:], T.pat[:], T.hx[:], ADD, ["pat", "hx"], ["pat"])
+    cp(lst("iv0"), T.ivl[:], ["ivl"], ["liv0"])
+    cp(lst("mto"), T.mtl[:], ["mtl"], ["lmto"])
+    ts(T.thr[:], T.qz[:], -4 * BIG, MUL, ["qz"], ["thr"], 1.5 + 2 * BIG, ADD)
+    cp(T.jw[:, 0:1], T.qi[:, 0:1], ["qi"], ["jwq"])
+    ts(T.jw2[:, 0:KW], T.k16[:], T.jw[:, 0:1], ADD, ["k16", "jwq"], ["jwa"])
+    ts(T.jw2[:, KW:2 * KW], T.k16[:], T.jw[:, 0:1], ADD, ["k16", "jwq"], ["jwb"])
+    JW = T.jw2[:, 0:KW]
+    JK = ["jwa", "jwb"]
+
+    def square(k):
+        if k < 8:
+            cp(T.hpr[:, (k + 1) * C:(k + 2) * C], T.hpr[:, k * C:(k + 1) * C].indirect(T.lhp[:, k * KW:(k + 1) * KW]),
+               ["hpr%d" % k, "lhp%d" % k], ["hpr%d" % (k + 1)], "s")
+
+    def places(k):
+        a, b = (16, 18) if k < 6 or k == 8 else (14, 18) if k == 6 else (10, 18)
+        o = 0 if k == 8 else 16 * a - (1 << k)
+        if k == 0:
+            cp(T.oo[:, 256:C], T.hpr[:, 0:C].indirect(T.lordo[:, a:b]), ["hpr0", "lordo"], ["oo"], "s")
+            cp(T.oo[:, 255:C - 1], T.hpr[:, C:2 * C].indirect(T.lordo[:, a:b]), ["hpr1", "lordo", "oo"], ["oo"], "s")
+        else:
+            cp(T.oo[:, o:o + 16 * (b - a)], T.hpr[:, k * C:(k + 1) * C].indirect(T.lordo[:, a:b]), ["hpr%d" % k, "lordo"], ["oo"], "s")
+        return (256, 288) if k < 5 else (o, o + 16 * (b - a))
+
+    def ring(k, jobs=()):
+        jobs = list(jobs)
+        square(k)
+        s0, s1 = places(k)
+        if k < 7:
+            jobs.append((T.hpr[:, (k + 1) * C:(k + 2) * C], C, "hpr%d" % (k + 1), T.lhp[:, (k + 1) * KW:(k + 2) * KW],
+                         "lhp%d" % (k + 1)))
+        jobs.append((T.oo[:, s0:s1], s1 - s0, "oo", T.lordo[:, s0 // 16:s1 // 16], "lordo"))
+        wraps(jobs)
+
+    op("v", lambda e: e.tensor_copy(T.luo[:], T.uoi[:]), ["uoi"], ["luo"])
+    op("v", lambda e: e.memset(T.fm0[:], 0.0), [], ["fm0"])
+    op("v", lambda e: e.memset(T.fl[:, C + 1:C + 2], 0.0), [], ["fle"])
+    op("v", lambda e: e.memset(T.fl[:, C:C + 1], 1.0), [], ["fl"])
+    cp(T.patf[:], T.pat[:], ["pat"], ["patf"])
+    tt(T.patf[:, 15:C:16], T.pat[:, 15:C:16], T.kb[:], ADD, ["pat", "kb", "patf"], ["patf"])
+    cp(T.im0[:, 0:KW], T.ivl[:], ["ivl"], ["im0"])
+    cp(T.mtw[:], T.mtl[:], ["mtl"], ["mtw"])
+    ring(0)
+    cp(T.mtr[:], T.iota[:, 0:C].indirect(lst("mto")), ["iota", "lmto"], ["mtr"], "s")
+    cp(T.mr[:], T.mtr[:].indirect(lst("iv0")), ["mtr", "liv0"], ["mr"], "s")
+    tt(T.dtw[:], T.mtw[:], JW, SUB, ["mtw"] + JK, ["dtw"])
+    cp(lst("udi"), T.udl[:], ["udl"], ["ludi"])
+
+    def prepare(rd):
+        im = "im%d" % (rd % 2)
+        b, e = scan(T.mr[:], C, "mr")
+        ts(T[im][:, KW:2 * KW], e, T.corr[:, 0:1], ADD, [b, "corr"], [im + "m"])
+        cp(lst("mi"), T[im][:, KW:2 * KW], [im + "m"], ["lmi"])
+        tt(T.ta[:], T[im][:], T.jw2[:], GT, [im, im + "m"] + JK, ["ta"])
+        ts(T.tb[:], T[im][:], float(C + 1), SUB, [im, im + "m"], ["tb"])
+        tt(T.diw[:], T[im][:, KW:2 * KW], T[im][:, 0:KW], SUB, [im, im + "m"], ["diw"])
+        tt(T.nim[:], T.ta[:], T.tb[:], MUL, ["ta", "tb"], ["nim"])
+        tt(T.fm0[:, 1:2 * KW:2], T.nim[:, KW:2 * KW], T.nim[:, 0:KW], SUB, ["nim"], ["fm0"])
+        ts(T.fm1[:, 1:2 * KW:2], T.nim[:, 0:KW], float(C + 1), ADD, ["nim"], ["fm1"])
+
+    for b in ("win", "h1", "h2", "h4", "h8"):
+        cp(T[b][:, C:C + 2], T.iota[:, C:C + 2], ["iota"], [b + "e"])
+    op("v", lambda e: e.memset(T.iom[:, 0:1], float(C - 1 - MID)), ["iom"], ["iom"])
+    op("v", lambda e: e.quantize_mx(T.uq[:], T.usc[:], T.ut[:]), ["ut"], ["u"])
+    op("v", lambda e: e.tensor_copy(T.urq[:, 0:128].bitcast(dt.uint32), T.uq[:, 0:128].bitcast(dt.uint32).indirect(T.luo[:, 0:8])),
+       ["u", "luo"], ["urq"])
+    op("s", lambda e: e.activation(T.ursc[:, 0:128], T.usc[:, 0:128].indirect(T.luo[:, 0:8]), COPY), ["u", "luo"], ["ursc"])
+    prepare(0)
+    op("v", lambda e: e.quantize_mx(T.x0q[:], T.x0sc[:], T.xin[:]), ["xin"], ["x0"])
+    ring(1)
+
+    def mm(bank, l, ls, a, r, rs, reads, c=0, d=C):
+        op("t", lambda e: e.matmul_mx(T.ps[:, 512 * bank:512 * bank + d - c], T[l][:, a:a + 128], T[ls][:, a:a + 128], T[r][:, c:d],
+                                      T[rs][:, c:d], True, True), reads, ["b%d" % bank])
+
+    def bank(k):
+        return T.ps[:, 512 * k:512 * k + C]
+
+    def pl(name, b):
+        return T[name][:, b * C:(b + 1) * C]
+
+    def constants(b):
+        op("v", lambda e: e.quantize_mx(T.eq[:, 128 * b:128 * b + 128], T.esc[:, 128 * b:128 * b + 128], T.et[:, 3 - b:515 - b]),
+           ["et"], ["e%d" % b])
+
+    ud = ["uda", "udb"]
+    for rd, step in enumerate(STEP):
+        xq, xs = "x%dq" % rd, "x%dsc" % rd
+        dst = T.cores[rank ^ step]
+        rel = relays(topo, core, dst)
+        backrel = relays(topo, dst, core)
+        RX, RI, RB, RE = ["%s%d" % (a, rd) for a in ("rx", "ri", "rb", "re")]
+        pq, pks = "p%dq" % rd, "p%dsc" % rd
+
+        def extra(k):
+            if rd == 0:
+                ring(k)
+
+        sync("g", ["x%d" % rd], [])
+        if rel:
+            put(rel[0], u8(T[pq][:, 0:HALF]), u8(T[xq][:, 0:HALF]), RX)
+            put(rel[1], u8(T[pq][:, HALF:C]), u8(T[xq][:, HALF:C]), RX)
+            put(rel[0], T[pks][:], T[xs][:], RX)
+        else:
+            put(dst, u8(T[pq][:]), u8(T[xq][:]), RX)
+            put(dst, T[pks][:], T[xs][:], RX)
+        listto = rel[1] if rel else dst
+        if backrel:
+            wr["p%d" % rd] = (RX, 2 * width(backrel[0], core) + width(backrel[1], core), {})
+            nl = width(backrel[1], core)
+        else:
+            wr["p%d" % rd] = (RX, 2 * width(dst, core), {})
+            nl = width(dst, core)
+        wr["livp%d" % rd] = (RI, nl, {RI: nl})
+        wr["lbp%d" % rd] = (RB, nl, {RB: nl})
+        wr["lep%d" % rd] = (RE, nl, {RE: nl})
+        wr["p%d" % rd][2][RX] = wr["p%d" % rd][1]
+
+        mm(0, "urq", "ursc", 0, xq, xs, ["urq", "ursc", "x%d" % rd], 0, HALF)
+        mm(5, "urq", "ursc", 0, xq, xs, ["urq", "ursc", "x%d" % rd], HALF, C)
+        ts(T.pp[:, 0:HALF], T.ps[:, 0:HALF], 0.0, GT, ["b0"], ["pp"])
+        if rd == 0:
+            constants(0)
+            constants(1)
+        op("s", lambda e: e.activation(T.pp[:, HALF:C], T.ps[:, 2560:2560 + HALF], SIGN), ["b5"], ["pps"])
+        cp(T.r1[:], T.pp[:].indirect(lst("iv%d" % rd)), ["pp", "pps", "liv%d" % rd], ["r1"], "s")
+        cp(T.r3[:], T.pp[:].indirect(lst("mto")), ["pp", "pps", "lmto"], ["r3"], "s")
+        cp(T.r2[:], T.pp[:].indirect(lst("mi")), ["pp", "pps", "lmi"], ["r2"])
+        c2, e2 = scan(T.r2[:], C, "r2")
+        c1, e1 = scan(T.r1[:], C, "r1")
+        tt(T.t1[:], e1, e2, ADD, [c1, c2], ["t1"])
+        ts(T.fm1[:, 0:2 * KW:2], T.t1[:], T.thr[:, 0:1], GE, ["t1", "thr"], ["bo"])
+        op("v", lambda e: e.tensor_tensor_scan(T.fmo[:], T.fm0[:], T.fm1[:], 0.0, MUL, ADD), ["bo", "fm0", "fm1"], ["fmo"])
+        tw = T.fmo[:, 1:2 * KW:2]
+        cp(lst("wino"), tw, ["fmo"], ["lwino"])
+        op("s", lambda e: e.activation(T.win[:, 96:C], T.iota[:, 0:C + 2].indirect(lst("wino", 6, KW)), COPY), ["iota", "lwino"], ["wins"])
+        ts(lst("off1"), tw, float(C), MIN, ["fmo"], ["loff1"])
+        cp(T.win[:, 0:96], T.iota[:, 0:C + 2].indirect(lst("wino", 0, 6)), ["iota", "lwino"], ["win"])
+        imo, imn = "im%d" % (rd % 2), "im%d" % ((rd + 1) % 2)
+        tt(T.di2[:], T.fm1[:, 0:2 * KW:2], T.diw[:], MUL, ["bo", "diw"], ["di2"])
+        tt(T[imn][:, 0:KW], T.di2[:], T[imo][:, 0:KW], ADD, ["di2", imo], [imn])
+        cp(lst("iv%d" % (rd + 1)), T[imn][:, 0:KW], [imn], ["liv%d" % (rd + 1)])
+        sync("g", ["liv%d" % (rd + 1)], [])
+        put(listto, T["livp%d" % rd][:], T["liv%d" % (rd + 1)][:], RI)
+        if rd == 0:
+            constants(2)
+            constants(3)
+        for b in range(4):
+            mm(1 + b, "eq", "esc", 128 * b, xq, xs, ["e%d" % b, "x%d" % rd])
+        cut = CUT if rd else KW
+        extra(2)
+        if rd == 0:
+            cp(T.uda[:], T.iota[:, 0:C].indirect(lst("udi")), ["iota", "ludi"], ["uda"], "s")
+        pick("h1", T.win[:, 0:C + 2], lambda a, b: lst("off1", a, b), ["win", "wins", "wine", "loff1"], "h1", cut)
+        hs = ["h1", "h2", "h4", "h8"]
+        for i in range(4):
+            of = T.lhoff[:, i * KW:(i + 1) * KW]
+            job = (T[hs[i]][:, 0:C], C, hs[i], of, "lhoff%d" % i)
+            if rd == 0:
+                ring(3 + i, [job])
+            else:
+                wraps([job])
+            cp(pl("th", i), bank(1 + i), ["b%d" % (1 + i)], ["th%d" % i], "s")
+            nx = hs[i + 1] if i < 3 else "hx"
+            pick(nx, T[hs[i]][:, 0:C + 2], lambda a, b: T.lhoff[:, i * KW + a:i * KW + b],
+                 [hs[i], hs[i] + "s", hs[i] + "e", "lhoff%d" % i], nx, cut)
+        job = (T.hx[:], C, "hx", lst("foff"), "lfoff", "patf")
+        if rd == 0:
+            ring(7, [job])
+            s0, s1 = places(8)
+        else:
+            wraps([job])
+        for b in range(8, -1, -1):
+            cp(T.fl[:, 32 * b:32 * b + 32], T.fl[:, 32 * b + 32:C + 2].indirect(T.lfoff[:, 2 * b:2 * b + 2]), ["fl", "fle", "lfoff"], ["fl"])
+            if rd == 0 and b == 6:
+                last = scan(T.oo[:, s0:s1], s1 - s0, "oo")
+            if rd == 0 and b == 5:
+                ts(T.lordo[:, 0:2], last[1], T.corr[:, 0:1], ADD, [last[0], "corr"], ["lordo"])
+            if rd == 0 and b == 3:
+                cp(T.r1[:, 0:C].indirect(T.lordo[:, 0:KW]), T.iom[:], ["iom", "lordo"], ["r1"])
+            if rd == 0 and b == 2:
+                last = scan(T.r1[:], C, "r1")
+            if rd == 0 and b == 1:
+                ts(lst("poso"), last[1], T.corr[:, 0:1], ADD, [last[0], "corr"], ["lposo"])
+        def partner():
+            for b in range(4):
+                k = (5, 6, 7, 0)[b]
+                mm(k, "eq", "esc", 128 * b, pq, pks, ["e%d" % b, "p%d" % rd])
+                cp(pl("tp", b), bank(k), ["b%d" % k], ["tp%d" % b], "s")
+
+        if rd in EARLY:
+            partner()
+        op("s", lambda e: e.activation(T.nf[:], T.fl[:, 0:C].indirect(lst("ordo")), IDENT, bias=1.0, scale=-1.0), ["fl", "lordo"], ["nf"])
+        tt(T.fo[:], T.fl[:, 0:C].indirect(lst("ordo")), T.oo[:], MUL, ["fl", "lordo", "oo"], ["fo"])
+        op("v", lambda e: e.tensor_tensor_scan(T.sb[:], T.nf[:], T.fo[:], 0.0, MUL, ADD), ["nf", "fo"], ["sb"])
+        pick("br", T.sb[:], lambda a, b: lst("poso", a, b), ["sb", "lposo"], "br")
+        wrap(T.br[:], C, "br", lst("bo%d" % rd), "lbo%d" % rd)
+        sync("g", ["lbo%d" % rd], [])
+        put(listto, T["lbp%d" % rd][:], T["lbo%d" % rd][:], RB)
+        if rd not in EARLY:
+            partner()
+        def past(b):
+            cp(pl("gv", b), pl("tp", b).indirect(lst("ivp%d" % rd)), ["tp%d" % b, "livp%d" % rd], ["gv%d" % b], "s")
+
+        past(0)
+        past(1)
+        c1, e1 = scan(T.pp[:], C, "pp")
+        c2, e2 = scan(T.r3[:], C, "r3")
+        tt(T.t3[:], e1, e2, ADD, [c1, c2], ["t3"])
+        ts(T.bj[:], T.t3[:], T.thr[:, 0:1], GE, ["t3", "thr"], ["bj"])
+        tt(T.dj[:], T.bj[:], T.dtw[:], MUL, ["bj", "dtw"], ["dj"])
+        tt(T.tf[:], T.dj[:], JW, ADD, ["dj"] + JK, ["tf"])
+        cp(lst("tauo"), T.tf[:], ["tf"], ["ltauo"])
+        uo, un = ud[rd % 2], ud[(rd + 1) % 2]
+        cp(T[un][:], T[uo][:].indirect(lst("tauo")), [uo, "ltauo"], [un], "s")
+        past(2)
+        past(3)
+        cp(T.r2[:], T.br[:].indirect(lst("ivp%d" % rd)), ["br", "brs", "livp%d" % rd], ["r2"])
+        wrap(T.r2[:], C, "r2", lst("eo%d" % rd), "leo%d" % rd)
+        sync("g", ["leo%d" % rd], [])
+        put(listto, T["lep%d" % rd][:], T["leo%d" % rd][:], RE)
+        wrap(T[un][:], C, un, lst("udo"), "ludo")
+        for b in range(4):
+            cp(pl("tu", b), pl("th", b).indirect(lst("udo")), ["th%d" % b, "ludo"], ["tu%d" % b], "s")
+        if rd < 2:
+            cp(T.mr[:], T.mtr[:].indirect(lst("iv%d" % (rd + 1))), ["mtr", "liv%d" % (rd + 1)], ["mr"], "s")
+        for b in range(4):
+            tt(T.zt[:, b:4 * C:4], pl("tp", b).indirect(lst("bp%d" % rd)), pl("gv", b), ADD,
+               ["tp%d" % b, "gv%d" % b, "lbp%d" % rd], ["zt%d" % b])
+        op("v", lambda e: e.quantize_mx(T.zq[:], T.zsc[:], T.zt[:]), ["zt%d" % b for b in range(4)], ["z"])
+        for b in range(4):
+            mm(1 + b, "wq", "wsc", 128 * b, "zq", "zsc", ["wq", "wsc", "z"])
+        for b in range(4):
+            op("s", lambda e: e.activation(pl("hh", b), bank(1 + b), COPY, scale=0.015625), ["b%d" % (1 + b)], ["hh%d" % b])
+        if rd < 2:
+            prepare(rd + 1)
+        else:
+            op("s", lambda e: e.activation(T.udf[:], T[un][:], COPY, bias=float(MID)), [un], ["udf"])
+            dma("y", T.uo[:], T.udf[0:128:16, :], ["udf"], [])
+            op("v", lambda e: e.quantize_mx(T.vq[:], T.vsc[:], T.vt[:]), ["vt"], ["v"])
+        for b in range(4):
+            tt(T.xt[:, b:4 * C:4], pl("hh", b).indirect(lst("ep%d" % rd)), pl("tu", b), ADD,
+               ["hh%d" % b, "tu%d" % b, "lep%d" % rd], ["xt%d" % b])
+        nq = rd + 1
+        op("v", lambda e: e.quantize_mx(T["x%dq" % nq][:], T["x%dsc" % nq][:], T.xt[:]), ["xt%d" % b for b in range(4)], ["x%d" % nq])
+
+    dma("y", T.oc[:], u8(T.x3q[:]), ["x3"], [])
+    for k in range(4):
+        dma("s" if k % 2 else "y", T.osc[4 * k:4 * k + 4, :], T.x3sc[32 * k:32 * k + 4, :], ["x3"], [])
+    mm(5, "vq", "vsc", 0, "x3q", "x3sc", ["v", "x3"], 0, HALF)
+    mm(6, "vq", "vsc", 0, "x3q", "x3sc", ["v", "x3"], HALF, C)
+    cp(T.yf[:, 0:HALF], T.ps[:, 2560:2560 + HALF], ["b5"], ["yf"])
+    cp(T.yf[:, HALF:C], T.ps[:, 3072:3072 + HALF], ["b6"], ["yfs"], "s")
+    dma("y", T.y[:, 0:HALF], T.yf[:, 0:HALF], ["yf"], [])
+    dma("s", T.y[:, HALF:C], T.yf[:, HALF:C], ["yfs"], [])
+    for s in dsems:
+        Q["y"].wait_ge(T.sem[s], 16)
+    for q in ("v", "s", "t", "g"):
+        g.wait_ge(T.sem[SEM[q]], cnt[q])
+    g.wait_ge(T.sem.snt, sent[0])

@@ -4,9 +4,14 @@ C, KW = 288, 18
 STEP = (4, 1, 2)
 MID = 145
 BIG = 512.0
-SCAN = "float16"
-EARLY = (0, 1)
-CUT = 10
+EVEN, ODD, ODD2 = C, C + 1, C + 3
+CE = C + 4
+LAST = 160
+
+CYCLE, GATHER, DONE, SLACK = 0.001, 1.5, 0.1, 0.03
+HOP, CODES, LOAD = 2.6, 5.0, 2.0
+LEADI, LEADU = 4.0, 3.0
+CUT = {"ring0": 8, "ring": 0, "mates": 8, "h0": 10, "h": 10, "br": 10}
 
 SCRATCH = {}
 for _n in ("xin", "xt", "zt", "th", "tp", "tu", "gv", "hh"):
@@ -14,45 +19,53 @@ for _n in ("xin", "xt", "zt", "th", "tp", "tu", "gv", "hh"):
 for _n in ("ut", "vt"):
     SCRATCH[_n] = ("sbuf", [128, 512], "bfloat16")
 SCRATCH["et"] = ("sbuf", [128, 520], "bfloat16")
+SCRATCH["half"] = ("sbuf", [128, 128], "bfloat16")
 for _n, _w in (("x0", C), ("x1", C), ("x2", C), ("x3", C), ("p0", C), ("p1", C), ("p2", C), ("z", C),
                ("u", 128), ("ur", 128), ("v", 128), ("e", 512), ("w", 512)):
     SCRATCH[_n + "q"] = ("sbuf", [128, _w], "float8_e4m3fn_x4")
     SCRATCH[_n + "sc"] = ("sbuf", [128, _w], "uint8")
-for _n in ("iota", "win", "h1", "h2", "h4", "h8", "fl"):
+SCRATCH["ramp"] = ("sbuf", [128, 16 + 304], "bfloat16")
+for _n in ("h1", "h2", "h4", "h8", "fl"):
     SCRATCH[_n] = ("sbuf", [128, 304], "bfloat16")
-for _n in ("iom", "pat", "patf", "pp", "r1", "r2", "r3", "hx", "nf", "fo", "sa", "sb", "br", "uda", "udb", "mtr", "mr", "oo"):
+for _n in ("pat", "patf", "pp", "r1", "r2", "r3", "hx", "nf", "fo", "sb", "br", "uda", "mtr", "mr", "um", "oo"):
     SCRATCH[_n] = ("sbuf", [128, C], "bfloat16")
-SCRATCH["hpr"] = ("sbuf", [128, 9 * C], "bfloat16")
-for _n in ("c0", "c1", "c2", "c3"):
-    SCRATCH[_n] = ("sbuf", [128, C], SCAN)
-SCRATCH["pati"] = ("sbuf", [128, C], "int32")
+SCRATCH["hpr"] = ("sbuf", [128, 8 * C], "bfloat16")
+SCRATCH["win"] = ("sbuf", [128, 2 * C + 16], "bfloat16")
+SCRATCH["d0"] = ("sbuf", [128, 2 * C], "bfloat16")
+SCRATCH["d1"] = ("sbuf", [128, 2 * C], "float16")
+SCRATCH["dd"] = ("sbuf", [128, C], "float16")
+SCANS = ("ch", "cr", "co", "cm", "cg", "ce", "cp", "c3", "cw0", "cw1", "cw2")
+SCRATCH["cc"] = ("sbuf", [128, len(SCANS) * C], "float16")
+for _n in ("i16", "pa", "pb"):
+    SCRATCH[_n] = ("sbuf", [128, 32], "bfloat16")
 for _n in ("ivl", "mtl", "udl", "hpl"):
     SCRATCH[_n] = ("sbuf", [128, KW], "int32")
 SCRATCH["qi"] = ("sbuf", [128, 8], "int32")
-for _n in ("corr", "thr", "qz"):
-    SCRATCH[_n] = ("sbuf", [128, 8], "float32")
-for _n in ("k16", "kb", "jw", "mtw", "dtw", "t1", "t3", "bj", "dj", "tf", "diw", "di2"):
-    SCRATCH[_n] = ("sbuf", [128, KW], "float32")
-for _n in ("jw2", "im0", "im1", "ta", "tb", "nim", "fm0", "fm1", "fmo"):
-    SCRATCH[_n] = ("sbuf", [128, 2 * KW], "float32")
-LOCAL = ("iv0", "mi", "mto", "udo", "wino", "off1", "poso", "tauo", "udi")
-SCRATCH["lloc"] = ("sbuf", [128, len(LOCAL) * KW], "uint16")
+SCRATCH["col"] = ("sbuf", [128, 8], "float32")
+SMALL = ("k16", "kb", "jw", "ivf", "mif", "di", "ga", "gb", "ta", "tb", "na", "nb", "e0", "sig", "bi", "ti", "fb",
+         "udf", "umf", "du", "t3", "bj", "tj")
+SCRATCH["sm"] = ("sbuf", [128, len(SMALL) * 20], "float32")
+LOCAL = ("iv0", "mi", "mto", "udo", "wo", "poso", "fa", "fb", "foff", "ordo", "go")
+SCRATCH["lloc"] = ("sbuf", [128, len(LOCAL) * 24], "uint16")
 for _n in ("iv1", "iv2", "iv3", "bo0", "bo1", "bo2", "eo0", "eo1", "eo2",
-           "ivp0", "ivp1", "ivp2", "bp0", "bp1", "bp2", "ep0", "ep1", "ep2", "hoff", "foff", "ordo"):
-    SCRATCH["l" + _n] = ("sbuf", [128, 4 * KW if _n == "hoff" else KW], "uint16")
-SCRATCH["lhp"] = ("sbuf", [128, 8 * KW], "uint16")
+           "ivp0", "ivp1", "ivp2", "bp0", "bp1", "bp2", "ep0", "ep1", "ep2"):
+    SCRATCH["l" + _n] = ("sbuf", [128, KW], "uint16")
+SCRATCH["lhoff"] = ("sbuf", [128, 4 * KW], "uint16")
+SCRATCH["lhp"] = ("sbuf", [128, 7 * KW], "uint16")
 SCRATCH["luo"] = ("sbuf", [128, 8], "uint16")
 SCRATCH["uoi"] = ("sbuf", [128, 8], "int32")
-SCRATCH["udf"] = ("sbuf", [128, C], "float32")
+SCRATCH["uof"] = ("sbuf", [128, C], "float32")
 SCRATCH["yf"] = ("sbuf", [128, C], "float32")
 SCRATCH["ps"] = ("psum", [128, 4096], "float32")
 
-SEMAPHORES = ["cv", "cs", "ct", "cg", "snt"] + ["d%d" % i for i in range(20)]
+SEMAPHORES = ["cv", "cs", "ct", "cg", "snt"] + ["d%d" % i for i in range(24)]
 SEMAPHORES += ["%s%d" % (a, i) for a in ("rx", "ri", "rb", "re") for i in range(3)]
 
 MUL, ADD, SUB, MAX, MIN = AluOpType.mult, AluOpType.add, AluOpType.subtract, AluOpType.max, AluOpType.min
-GT, GE, EQ = AluOpType.is_gt, AluOpType.is_ge, AluOpType.is_equal
-COPY, IDENT, SIGN = ActivationFunctionType.Copy, ActivationFunctionType.Identity, ActivationFunctionType.Sign
+GT, GE, EQ, NE = AluOpType.is_gt, AluOpType.is_ge, AluOpType.is_equal, AluOpType.not_equal
+AND = AluOpType.bitwise_and
+COPY = ActivationFunctionType.Copy
+IDENT = ActivationFunctionType.Identity
 
 
 def relays(topo, src, dst):
@@ -64,22 +77,54 @@ def relays(topo, src, dst):
     return (near + far)[:2]
 
 
+def arrange(calls):
+    wr, rd = {}, {}
+    for i, c in enumerate(calls):
+        c["after"] = {wr[k] for k in c["reads"] + c["writes"] if k in wr}
+        for k in c["writes"]:
+            c["after"] |= set(rd.get(k, []))
+        for k in c["reads"]:
+            rd.setdefault(k, []).append(i)
+        for k in c["writes"]:
+            wr[k], rd[k] = i, []
+        c["chain"] = 0.0
+    for c in reversed(calls):
+        c["chain"] += min(w[1] for w in c["ways"]) + c["late"] + c["lead"]
+        for a in c["after"]:
+            calls[a]["chain"] = max(calls[a]["chain"], c["chain"])
+    busy = {}
+    for c in sorted(calls, key=lambda c: -c["chain"]):
+        ready = max([calls[a]["end"] for a in c["after"]], default=0.0)
+        best = None
+        for q, cost, call in c["ways"]:
+            t = ready
+            for a, b in busy.setdefault(q, []):
+                if t + cost <= a + min(SLACK, cost / 2):
+                    break
+                t = max(t, b)
+            if best is None or t + cost < best[0] + best[2]:
+                best = (t, q, cost, call)
+        c["start"], c["queue"], cost, c["call"] = best
+        c["end"] = c["start"] + cost + c["late"]
+        busy[c["queue"]] = sorted(busy[c["queue"]] + [(c["start"], c["start"] + cost)])
+    return sorted(calls, key=lambda c: c["start"])
+
+
 def rank_program(g, core, T, topo):
     rank = T.rank_of(core)
     sent = [0]
 
+    def width(a, b):
+        return len(topo.engines(a, b)[:8])
+
     def put(dst, out, in_, sem):
-        e = topo.engines(core, dst)[:8]
+        e = topo.engines(core, dst)[:width(core, dst)]
         rid, pid = topo.addr(dst, core)
         m = 0
         for a in e:
             m |= 1 << a
         g.remote_dma(out, in_, T.sem[sem], T.sem.snt, pid, rid, m)
         sent[0] += len(e)
-        return len(e)
-
-    def width(a, b):
-        return len(topo.engines(a, b)[:8])
 
     def u8(ap):
         return ap.bitcast(dt.uint8)
@@ -107,383 +152,365 @@ def rank_program(g, core, T, topo):
             g.wait_ge(T.sem.snt, sent[0])
         return
 
+    calls = []
+
+    def add(ways, reads, writes, late=DONE, kind="op", arrive=None):
+        calls.append({"ways": ways, "reads": list(reads), "writes": list(writes), "late": late, "kind": kind, "arrive": arrive,
+                      "lead": 0.0})
+
+    def sooner(lead):
+        calls[-1]["lead"] = lead
+
+    def vcost(n, rate):
+        return max(64, n * rate) * CYCLE
+
+    def gcost(q, n):
+        return (0.05 if q == "v" else 0.065) + n * GATHER * CYCLE
+
+    def vec(call, cost, reads, writes):
+        add([("v", cost, call)], reads, writes)
+
+    def pool(call, n, reads, writes):
+        add([("g", 0.17 + 2 * n * CYCLE, call)], reads, writes, 0.25)
+
+    def dma(q, out, in_, reads, writes, late, kind="dma"):
+        add([(q, 0.05, lambda e: e.dma_start(out, in_))], reads, writes, late, kind)
+
+    def send(parts, reads, key, sem, n, late):
+        def call(e):
+            for dst, out, in_ in parts:
+                put(dst, out, in_, sem)
+        add([("g", 0.4 * len(parts), call)], reads, [key], late, "send", (sem, n))
+
+    def tt(out, a, b, o, reads, writes, cost=0.064):
+        vec(lambda e: e.tensor_tensor(out, a, b, o), cost, reads, writes)
+
+    def ts(out, a, s1, o1, reads, writes, s2=None, o2=None, cost=0.064):
+        if o2 is None:
+            vec(lambda e: e.tensor_scalar(out, a, s1, None, o1), cost, reads, writes)
+        else:
+            vec(lambda e: e.tensor_scalar(out, a, s1, s2, o1, o2), cost, reads, writes)
+
+    def cp(out, in_, reads, writes, cost=0.064):
+        vec(lambda e: e.tensor_copy(out, in_), cost, reads, writes)
+
+    def take(out, win, n, reads, writes, qs="sv"):
+        way = {"v": lambda e: e.tensor_copy(out, win), "s": lambda e: e.activation(out, win, COPY)}
+        add([(q, gcost(q, n), way[q]) for q in qs], reads, writes)
+
+    def unload(out, in_, n, reads, writes, qs="sv", scale=None):
+        if scale is None:
+            way = {"v": lambda e: e.tensor_copy(out, in_), "s": lambda e: e.activation(out, in_, COPY)}
+        else:
+            way = {"v": lambda e: e.tensor_scalar(out, in_, scale, None, MUL), "s": lambda e: e.activation(out, in_, COPY, scale=scale)}
+        add([(q, n * CYCLE + (0.065 if q == "s" else 0), way[q]) for q in qs], reads, writes)
+
+    def fill(ap, c, writes, n=64):
+        vec(lambda e: e.memset(ap, c), vcost(n, 0.5), [], writes)
+
+    def count(ap, pattern, base, n, writes, reads=()):
+        pool(lambda e: e.iota(ap, pattern, base, 0, allow_small_or_imprecise_dtypes=True), n, reads, writes)
+
+    def quant(name, tile, reads, a=0, b=C, key=None):
+        vec(lambda e: e.quantize_mx(T[name + "q"][:, a:b], T[name + "sc"][:, a:b], tile), 0.015 + 0.00105 * (b - a), reads, [key or name])
+
+    def mm(bank, l, a, r, reads, c=0, d=C):
+        add([("t", 0.07 + 0.0006 * (d - c), lambda e: e.matmul_mx(
+            T.ps[:, 512 * bank:512 * bank + d - c], T[l + "q"][:, a:a + 128], T[l + "sc"][:, a:a + 128], T[r + "q"][:, c:d],
+            T[r + "sc"][:, c:d], True, True))], reads, ["b%d" % bank])
+
+    def bank(k, n=C):
+        return T.ps[:, 512 * k:512 * k + n]
+
+    def pl(name, b, c=0, d=C):
+        return T[name][:, b * C + c:b * C + d]
+
+    def lst(name, a=0, b=KW):
+        if name in LOCAL:
+            o = 24 * LOCAL.index(name)
+            return T.lloc[:, o + a:o + b]
+        return T["l" + name][:, a:b]
+
+    def sm(name):
+        o = 20 * SMALL.index(name)
+        return T.sm[:, o:o + KW]
+
+    def small(out, a, b, o):
+        tt(sm(out), sm(a), sm(b), o, [a, b], [out])
+
+    def pick(out, win, off, reads, key, k):
+        take(out[:, 16 * k:C], win.indirect(off(k, KW)), C - 16 * k, reads, [key + "s"] + ([] if k else [key]), "s")
+        if k:
+            take(out[:, 0:16 * k], win.indirect(off(0, k)), 16 * k, reads, [key], "v")
+
+    def both(key):
+        return [key, key + "s"]
+
+    def scan(row, n, reads, b, pat="pat"):
+        o = C * SCANS.index(b)
+        vec(lambda e: e.tensor_tensor_scan(T.cc[:, o:o + n], row, T[pat][:, 0:n], -2 * BIG, MAX, ADD), vcost(n, 0.5), reads + [pat], [b])
+        return b, T.cc[:, o + 15:o + n:16]
+
+    Q0, Q15, QZ, CORR, CORR2, THR = [T.col[:, i:i + 1] for i in range(6)]
+
+    def land(job, out, key):
+        ts(out, job[1], CORR, ADD, [job[0], "corr"], [key])
+
+    IOTA = T.ramp[:, 16:16 + CE]
+
+    t = LOAD
+    for q, to, src, key, long in (("s", T.hpl[:], T.hp, "hpl", 0.3), ("y", T.mtl[:], T.mt, "mtl", 0.3), ("s", T.ivl[:], T.iv, "ivl", 0.3),
+                                  ("y", T.ut[:], T.u, "ut", 0.7), ("y", T.xin[:], T.x, "xin", 1.2), ("y", T.udl[:], T.ud, "udl", 0.3),
+                                  ("y", u8(T.wq[:]), T.wc, "wq", 1.2), ("y", T.wsc[:], T.ws, "wsc", 0.5), ("y", T.vt[:], T.v, "vt", 0.7)):
+        t += long
+        dma(q, to, src[:], [], [key], t, "load")
+
+    fill(T.half[:], 0.5, ["half"])
+    fill(T.et[:], 0.0, ["et"], 520)
+    pool(lambda e: e.iota(T.qi[:], [[15, 2], [0, 4]], 0, 1), 8, [], ["qi"])
+    count(T.i16[:], [[0, 2], [1, 16]], 0, 32, ["i16"])
+    pool(lambda e: e.affine_select(T.et[:, 3:515:4], T.half[:], [[1, 128]], EQ, 0.0, 0, -1), 128, ["et", "half"], ["et"])
+    count(T.ramp[:], [[1, 320]], -16 - MID, 320, ["iota"])
+    count(sm("k16"), [[16, KW]], 0, KW, ["k16"])
+    pool(lambda e: e.iota(T.uoi[:], [[16, 8]], 0, 0), 8, [], ["uoi"])
+    count(sm("kb"), [[-32, KW // 2], [0, 2]], -32, KW, ["kb"])
+    count(T.d0[:, 0:2 * C:2], [[0, C]], 0, C, ["d0e"])
+    for b in ("h1", "h2", "h4", "h8"):
+        count(T[b][:, C:CE], [[1, 4]], C - MID, 4, [b + "e"])
+    count(T.win[:, 2 * C:2 * CE], [[0, 8]], EVEN - MID, 8, ["wine"])
+    count(T.win[:, 2 * EVEN + 1:2 * EVEN + 2], [[0, 1]], ODD - MID, 1, ["wine"])
+    count(T.fl[:, C:CE], [[0, 4]], 0, 4, ["fle"])
+    count(T.fl[:, EVEN:EVEN + 1], [[0, 1]], 1, 1, ["fle"])
+    count(T.ramp[:, 15:16], [[0, 1]], C - 1 - MID, 1, ["iom"], ["iota"])
+    fill(lst("ordo"), C - 1, ["lordo"])
+    ts(T.qi[:], T.qi[:], 15, AND, ["qi"], ["qi"])
+    cp(T.col[:, 0:2], T.qi[:, 3:5], ["qi"], ["q0"])
+    ts(T.pa[:], T.i16[:], Q0, EQ, ["i16", "q0"], ["pa"], BIG, MUL)
+    ts(T.pb[:], T.i16[:], Q15, EQ, ["i16", "q0"], ["pb"], -2 * BIG, MUL)
+    ts(QZ, Q0, 0.0, EQ, ["q0"], ["qz"])
+    tt(T.pat[:, 0:32], T.pa[:], T.pb[:], ADD, ["pa", "pb"], ["pat"])
+    for a, n in ((32, 32), (64, 64), (128, 128), (256, 32)):
+        cp(T.pat[:, a:a + n], T.pat[:, 0:n], ["pat"], ["pat"])
+    ts(CORR, QZ, 2 * BIG, MUL, ["qz"], ["corr"], MID - BIG, ADD)
+    ts(CORR2, QZ, 2 * BIG, MUL, ["qz"], ["corr2"], MID - BIG + 0.5, ADD)
+    ts(THR, QZ, -4 * BIG, MUL, ["qz"], ["thr"], 1.5 + 2 * BIG, ADD)
+    unload(T.patf[:], T.pat[:], C, ["pat"], ["patf"], "s")
+    tt(T.patf[:, 15:C:16], T.pat[:, 15:C:16], sm("kb"), ADD, ["pat", "kb", "patf"], ["patf"])
+    ts(sm("jw"), sm("k16"), Q0, ADD, ["k16", "q0"], ["jw"])
+    for b in range(4):
+        quant("e", T.et[:, 3 - b:515 - b], ["et"], 128 * b, 128 * b + 128, "e%d" % b)
+
+    def hrow(k):
+        return T.hpr[:, k * C:(k + 1) * C]
+
+    cp(T.lhp[:, 0:KW], T.hpl[:], ["hpl"], ["lhp0"])
+    pick(hrow(0), IOTA, lambda a, b: T.lhp[:, a:b], ["iota", "lhp0"], "hpr0", CUT["ring0"])
+    for k in range(9):
+        if k < 7:
+            pick(hrow(k + 1), hrow(k), lambda a, b: T.lhp[:, k * KW + a:k * KW + b], both("hpr%d" % k) + ["lhp%d" % k],
+                 "hpr%d" % (k + 1), CUT["ring0" if k < 2 else "ring"])
+        a, b = (16, 18) if k < 6 else (14, 18) if k == 6 else (10, 18) if k == 7 else (8, 10)
+        o = 16 * a - (1 << min(k, 7))
+        if k == 0:
+            take(T.oo[:, 256:C], hrow(0).indirect(lst("ordo", a, b)), 32, both("hpr0") + ["lordo"], ["oo"])
+            take(T.oo[:, 255:C - 1], hrow(1).indirect(lst("ordo", a, b)), 32, both("hpr1") + ["lordo"], ["oo"])
+        else:
+            take(T.oo[:, o:o + 16 * (b - a)], hrow(min(k, 7)).indirect(lst("ordo", a, b)), 16 * (b - a),
+                 both("hpr%d" % min(k, 7)) + ["lordo"], ["oo"])
+        s0, s1 = (256, C) if k < 5 else (o, o + 16 * (b - a))
+        if k < 6:
+            land(scan(hrow(k + 1), C, both("hpr%d" % (k + 1)), "cr"), T.lhp[:, (k + 1) * KW:(k + 2) * KW], "lhp%d" % (k + 1))
+        land(scan(T.oo[:, s0:s1], s1 - s0, ["oo"], "co"), lst("ordo", s0 // 16, s1 // 16), "lordo")
+    cp(T.r1[:].indirect(lst("ordo")), T.ramp[:, 15:15 + C], ["iota", "iom", "lordo"], ["r1"], 0.05 + 3.5 * C * CYCLE)
+    land(scan(T.r1[:], C, ["r1"], "cg"), lst("poso"), "lposo")
+
+    cp(lst("mto"), T.mtl[:], ["mtl"], ["lmto"])
+    cp(lst("iv0"), T.ivl[:], ["ivl"], ["liv0"])
+    cp(sm("ivf"), T.ivl[:], ["ivl"], ["ivf"])
+    pick(T.mtr, IOTA, lambda a, b: lst("mto", a, b), ["iota", "lmto"], "mtr", CUT["mates"])
+    pick(T.mr, T.mtr[:], lambda a, b: lst("iv0", a, b), both("mtr") + ["liv0"], "mr", CUT["mates"])
+    job = scan(T.mr[:], C, both("mr"), "cm")
+    land(job, sm("mif"), "mif")
+    land(job, lst("mi"), "lmi")
+    for f, n, end, to in (("ivf", "a", ODD, "fa"), ("mif", "b", ODD2, "fb")):
+        small("g" + n, f, "jw", GT)
+        ts(sm("t" + n), sm(f), float(end), SUB, [f], ["t" + n])
+        small("n" + n, "g" + n, "t" + n, MUL)
+        ts(lst(to), sm("n" + n), float(end), ADD, ["n" + n], ["l" + to])
+    take(T.win[:, 1:2 * C:2], IOTA.indirect(lst("fa")), C, ["iota", "lfa"], ["win"], "s")
+    ts(sm("e0"), sm("na"), float(ODD), ADD, ["na", "corr"], ["e0"], CORR, SUB)
+    ts(sm("fb"), sm("nb"), float(ODD2), ADD, ["nb"], ["fb"])
+    small("sig", "fb", "e0", ADD)
+    small("di", "mif", "ivf", SUB)
+    cp(lst("udo"), T.udl[:], ["udl"], ["ludo"])
+    cp(sm("udf"), T.udl[:], ["udl"], ["udf"])
+    take(T.uda[:], IOTA.indirect(lst("udo")), C, ["iota", "ludo"], ["uda"])
+    take(T.um[:], T.uda[:].indirect(lst("mto")), C, ["uda", "lmto"], ["um"])
+    land(scan(T.um[:], C, ["um"], "ce"), sm("umf"), "umf")
+    small("du", "umf", "udf", SUB)
+
+    cp(T.luo[:], T.uoi[:], ["uoi"], ["luo"])
+    quant("u", T.ut[:], ["ut"], 0, 128)
+    cp(T.urq[:, 0:128].bitcast(dt.uint32), T.uq[:, 0:128].bitcast(dt.uint32).indirect(T.luo[:, 0:8]), ["u", "luo"], ["urq"], gcost("v", 128))
+    take(T.ursc[:, 0:128], T.usc[:, 0:128].indirect(T.luo[:, 0:8]), 128, ["u", "luo"], ["ursc"], "s")
+    quant("v", T.vt[:], ["vt"], 0, 128)
+    quant("x0", T.xin[:], ["xin"])
+
+    for rd, step in enumerate(STEP):
+        x, p = "x%d" % rd, "p%d" % rd
+        dst = T.cores[rank ^ step]
+        rel = relays(topo, core, dst)
+        back = relays(topo, dst, core)
+        hops = 2 if rel else 1
+        first = rd == 0
+
+        if rel:
+            parts = [(rel[0], u8(T[p + "q"][:, 0:HALF]), u8(T[x + "q"][:, 0:HALF])),
+                     (rel[1], u8(T[p + "q"][:, HALF:C]), u8(T[x + "q"][:, HALF:C])), (rel[0], T[p + "sc"][:], T[x + "sc"][:])]
+        else:
+            parts = [(dst, u8(T[p + "q"][:]), u8(T[x + "q"][:])), (dst, T[p + "sc"][:], T[x + "sc"][:])]
+        nx = 2 * width(back[0], core) + width(back[1], core) if back else 2 * width(dst, core)
+        send(parts, [x], p, "rx%d" % rd, nx, CODES + (hops - 1) * HOP)
+
+        def mail(name, to, sem):
+            send([(rel[1] if rel else dst, lst(to), lst(name))], ["l" + name], "l" + to, sem, width(back[1] if back else dst, core),
+                 hops * HOP - 0.4)
+
+        cp(T.d1[:, 1:2 * C:2], T.win[:, 1:2 * C:2], ["win"], ["d1a"], vcost(C, 0.5))
+        tt(T.dd[:], IOTA.indirect(lst("fb")), T.win[:, 1:2 * C:2], SUB, ["iota", "lfb", "win"], ["dd"], gcost("v", C))
+        mm(0, "ur", 0, x, ["urq", "ursc", x], 0, HALF)
+        mm(5, "ur", 0, x, ["urq", "ursc", x], HALF, C)
+        ts(T.pp[:, 0:HALF], bank(0, HALF), 0.0, GT, ["b0"], ["pp"], cost=vcost(HALF, 1))
+        ts(T.pp[:, HALF:C], bank(5, HALF), 0.0, GT, ["b5"], ["pps"], cost=vcost(HALF, 1))
+        take(T.d0[:, 1:2 * C:2], T.pp[:].indirect(lst("iv%d" % rd)), C, both("pp") + ["liv%d" % rd, "d0e"], ["d0"], "s")
+        tt(T.d1[:, 0:2 * C:2], T.pp[:].indirect(lst("mi")), T.dd[:], MUL, both("pp") + ["lmi", "dd"], ["d1"], gcost("v", C))
+        vec(lambda e: e.tensor_tensor_scan(T.win[:, 0:2 * C], T.d0[:], T.d1[:], 0.0, MUL, ADD), vcost(2 * C, 0.5),
+            ["d0", "d0e", "d1", "d1a"], ["win"])
+        job = scan(T.win[:, 1:2 * C:2], C, ["win"], "cw%d" % rd)
+        ts(lst("wo"), job[1], CORR2, ADD, [job[0], "corr2"], ["lwo"], 2.0, MUL)
+        old = ("e0", sm("e0")) if first else last
+        last = job
+        tt(sm("bi"), job[1], old[1], NE, [job[0], old[0]], ["bi"])
+        small("ti", "bi", "di", MUL)
+        small("ivf", "ivf", "ti", ADD)
+        cp(lst("iv%d" % (rd + 1)), sm("ivf"), ["ivf"], ["liv%d" % (rd + 1)])
+        mail("iv%d" % (rd + 1), "ivp%d" % rd, "ri%d" % rd)
+        sooner(LEADI)
+        if rd < 2:
+            small("mif", "mif", "ti", SUB)
+            cp(lst("mi"), sm("mif"), ["mif"], ["lmi"])
+            small("di", "mif", "ivf", SUB)
+            tt(sm("fb"), sm("sig"), job[1], SUB, ["sig", job[0]], ["fb"])
+            cp(lst("fb"), sm("fb"), ["fb"], ["lfb"])
+        take(T.r3[:], T.pp[:].indirect(lst("mto")), C, both("pp") + ["lmto"], ["r3"])
+        j1 = scan(T.pp[:], C, both("pp"), "cp")
+        j2 = scan(T.r3[:], C, ["r3"], "c3")
+        tt(sm("t3"), j1[1], j2[1], ADD, [j1[0], j2[0]], ["t3"])
+        ts(sm("bj"), sm("t3"), THR, GE, ["t3", "thr"], ["bj"])
+        small("tj", "bj", "du", MUL)
+        small("udf", "udf", "tj", ADD)
+        cp(lst("udo"), sm("udf"), ["udf"], ["ludo"])
+        sooner(LEADU)
+        if rd < 2:
+            small("umf", "umf", "tj", SUB)
+            small("du", "umf", "udf", SUB)
+        for b in range(4):
+            mm(1 + b, "e", 128 * b, x, ["e%d" % b, x])
+            unload(pl("th", b), bank(1 + b), C, ["b%d" % (1 + b)], ["th%d" % b])
+            take(pl("tu", b), pl("th", b).indirect(lst("udo")), C, ["th%d" % b, "ludo"], ["tu%d" % b])
+        for b in range(4):
+            k = (5, 6, 7, 0)[b]
+            mm(k, "e", 128 * b, p, ["e%d" % b, p])
+            unload(pl("tp", b), bank(k), C, ["b%d" % k], ["tp%d" % b])
+            take(pl("gv", b), pl("tp", b).indirect(lst("ivp%d" % rd)), C, ["tp%d" % b, "livp%d" % rd], ["gv%d" % b])
+        hs = ["h1", "h2", "h4", "h8", "hx"]
+        cut = CUT["h0" if first else "h"]
+        pick(T.h1, T.win[:, 0:2 * CE], lambda a, b: lst("wo", a, b), ["win", "wine", "lwo"], "h1", cut)
+        for i in range(4):
+            land(scan(T[hs[i]][:, 0:C], C, both(hs[i]), "ch"), T.lhoff[:, i * KW:(i + 1) * KW], "lhoff%d" % i)
+            pick(T[hs[i + 1]], T[hs[i]][:, 0:CE], lambda a, b: T.lhoff[:, i * KW + a:i * KW + b],
+                 both(hs[i]) + [hs[i] + "e", "lhoff%d" % i], hs[i + 1], cut)
+        land(scan(T.hx[:], C, both("hx"), "ch", "patf"), lst("foff"), "lfoff")
+        ts(T.fl[:, 256:C], T.hx[:, 256:C], float(EVEN - MID), EQ, both("hx"), ["fl"])
+        if not first:
+            take(T.r1[:], T.hx[:].indirect(lst("ordo")), C, both("hx") + ["lordo"], ["r1"], "s")
+            land(scan(T.r1[:], C, ["r1"], "cg"), lst("go"), "lgo")
+        for b in range(7, -1 if first else 0, -1):
+            take(T.fl[:, 32 * b:32 * b + 32], T.fl[:, 32 * b + 32:CE].indirect(lst("foff", 2 * b, 2 * b + 2)), 32, ["fl", "fle", "lfoff"],
+                 ["fl"], "vs")
+        key = "ordo" if first else "go"
+        add([("s", gcost("s", C), lambda e, key=key: e.activation(T.nf[:], T.fl[:, 0:CE].indirect(lst(key)), IDENT, bias=1.0, scale=-1.0))],
+            ["fl", "fle", "l" + key], ["nf"])
+        tt(T.fo[:], T.fl[:, 0:CE].indirect(lst(key)), T.oo[:], MUL, ["fl", "fle", "l" + key, "oo"], ["fo"], gcost("v", C))
+        vec(lambda e: e.tensor_tensor_scan(T.sb[:], T.nf[:], T.fo[:], 0.0, MUL, ADD), vcost(C, 0.5), ["nf", "fo"], ["sb"])
+        pick(T.br, T.sb[:], lambda a, b: lst("poso", a, b), ["sb", "lposo"], "br", CUT["br"])
+        land(scan(T.br[:], C, both("br"), "ch"), lst("bo%d" % rd), "lbo%d" % rd)
+        mail("bo%d" % rd, "bp%d" % rd, "rb%d" % rd)
+        take(T.r2[:], T.br[:].indirect(lst("ivp%d" % rd)), C, both("br") + ["livp%d" % rd], ["r2"])
+        land(scan(T.r2[:], C, ["r2"], "ce"), lst("eo%d" % rd), "leo%d" % rd)
+        mail("eo%d" % rd, "ep%d" % rd, "re%d" % rd)
+        for b in range(4):
+            tt(T.zt[:, b:4 * C:4], pl("tp", b).indirect(lst("bp%d" % rd)), pl("gv", b), ADD,
+               ["tp%d" % b, "gv%d" % b, "lbp%d" % rd], ["zt%d" % b], gcost("v", C))
+        quant("z", T.zt[:], ["zt%d" % b for b in range(4)])
+        for b in range(4):
+            mm(1 + b, "w", 128 * b, "z", ["wq", "wsc", "z"])
+            unload(pl("hh", b), bank(1 + b), C, ["b%d" % (1 + b)], ["hh%d" % b], "s" if b else "vs", 0.015625)
+            sooner(0.1 * (3 - b))
+        runs = ((0, C),) if rd < 2 else ((0, LAST), (LAST, C))
+        for c, d in runs:
+            for b in range(4):
+                tt(T.xt[:, 4 * c + b:4 * d:4], pl("hh", b).indirect(lst("ep%d" % rd, c // 16, d // 16)), pl("tu", b, c, d), ADD,
+                   ["hh%d" % b, "tu%d" % b, "lep%d" % rd], ["xt%d%d" % (b, c)], gcost("v", d - c))
+            quant("x%d" % (rd + 1), T.xt[:, 4 * c:4 * d], ["xt%d%d" % (b, c) for b in range(4)], c, d, "x%d" % (rd + 1 + c))
+
+    add([("s", gcost("s", C), lambda e: e.activation(T.uof[:], IOTA.indirect(lst("udo")), COPY, bias=float(MID)))], ["iota", "ludo"], ["uof"])
+    dma("y", T.uo[:], T.uof[0:128:16, :], ["uof"], [], LOAD)
+    for i, (c, d) in enumerate(runs):
+        x = "x%d" % (3 + c)
+        mm(5 + i, "v", 0, "x3", ["v", x], c, d)
+        unload(T.yf[:, c:d], bank(5 + i, d - c), d - c, ["b%d" % (5 + i)], ["yf%d" % i], "vs" if i else "s")
+        dma("y", T.oc[:, 4 * c:4 * d], u8(T.x3q[:, c:d]), [x], [], LOAD + 1.5 - i)
+        dma("s" if i else "y", T.y[:, c:d], T.yf[:, c:d], ["yf%d" % i], [], LOAD + 1.5 - i)
+    for k in range(4):
+        dma("y", T.osc[4 * k:4 * k + 4, :], T.x3sc[32 * k:32 * k + 4, :], ["x3", "x%d" % (3 + LAST)], [], LOAD)
+
+    order = arrange(calls)
+    order = [c for c in calls if c["kind"] == "load"] + [c for c in order if c["kind"] != "load"]
     Q = {"v": g.vector, "s": g.scalar, "t": g.tensor, "g": g, "y": g.sync}
     SEM = {"v": "cv", "s": "cs", "t": "ct", "g": "cg"}
     cnt = {"v": 0, "s": 0, "t": 0, "g": 0}
     clock = {q: {} for q in Q}
     wr, rdr = {}, {}
-    nd = [0]
     dsems = []
-
-    def sync(q, reads, writes):
-        need = []
-        for k in reads:
-            if k in wr:
-                need.append(wr[k])
-        for k in writes:
-            if k in wr:
-                need.append(wr[k])
+    for c in order:
+        q = c["queue"]
+        need = [wr[k] for k in c["reads"]] + [wr[k] for k in c["writes"] if k in wr]
+        for k in c["writes"]:
             need += rdr.get(k, [])
-        need.sort(key=lambda t: -t[1])
-        for sem, val, clk in need:
+        for sem, val, clk in sorted(need, key=lambda t: -t[1]):
             if clock[q].get(sem, 0) < val:
                 Q[q].wait_ge(T.sem[sem], val)
                 for a, b in clk.items():
-                    if clock[q].get(a, 0) < b:
-                        clock[q][a] = b
-
-    def done(q, sem, val, reads, writes):
-        clk = dict(clock[q])
-        clk[sem] = val
-        tok = (sem, val, clk)
-        for k in reads:
+                    clock[q][a] = max(clock[q].get(a, 0), b)
+        i = c["call"](Q[q])
+        if c["kind"] == "send":
+            sem, val = c["arrive"]
+            wr[c["writes"][0]] = (sem, val, {sem: val})
+            continue
+        if c["kind"] == "op":
+            cnt[q] += 1
+            sem, val = SEM[q], cnt[q]
+            i.then_inc(T.sem[sem], 1)
+        else:
+            sem, val = "d%d" % len(dsems), 16
+            dsems.append(sem)
+            i.then_inc(T.sem[sem], 16)
+        tok = (sem, val, dict(clock[q], **{sem: val}))
+        for k in c["reads"]:
             rdr.setdefault(k, []).append(tok)
-        for k in writes:
-            wr[k] = tok
-            rdr[k] = []
-
-    def op(q, call, reads, writes):
-        sync(q, reads, writes)
-        i = call(Q[q])
-        cnt[q] += 1
-        i.then_inc(T.sem[SEM[q]], 1)
-        done(q, SEM[q], cnt[q], reads, writes)
-
-    def dma(q, out, in_, reads, writes):
-        sem = "d%d" % nd[0]
-        nd[0] += 1
-        sync(q, reads, writes)
-        Q[q].dma_start(out, in_).then_inc(T.sem[sem], 16)
-        dsems.append(sem)
-        done(q, sem, 16, reads, writes)
-
-    def tt(out, a, b, o, reads, writes):
-        op("v", lambda e: e.tensor_tensor(out, a, b, o), reads, writes)
-
-    def ts(out, a, s1, o1, reads, writes, s2=None, o2=None):
-        if o2 is None:
-            op("v", lambda e: e.tensor_scalar(out, a, s1, None, o1), reads, writes)
-        else:
-            op("v", lambda e: e.tensor_scalar(out, a, s1, s2, o1, o2), reads, writes)
-
-    def cp(out, in_, reads, writes, q="v"):
-        if q == "v":
-            op("v", lambda e: e.tensor_copy(out, in_), reads, writes)
-        else:
-            op("s", lambda e: e.activation(out, in_, COPY), reads, writes)
-
-    def pick(out, win, off, reads, key, k=CUT):
-        if k < KW:
-            op("s", lambda e: e.activation(T[out][:, 16 * k:C], win.indirect(off(k, KW)), COPY), reads, [key + "s"])
-        op("v", lambda e: e.tensor_copy(T[out][:, 0:16 * k], win.indirect(off(0, k))), reads, [key])
-
-    rot = [0]
-
-    def scan(row, n, key, pat="pat"):
-        b = "c%d" % (rot[0] % 4)
-        rot[0] += 1
-        op("v", lambda e: e.tensor_tensor_scan(T[b][:, 0:n], row, T[pat][:, 0:n], -2 * BIG, MAX, ADD),
-           [key, key + "s", pat], [b])
-        return b, T[b][:, 15:n:16]
-
-    def wraps(jobs):
-        es = [scan(j[0], j[1], j[2], j[5] if len(j) > 5 else "pat") for j in jobs]
-        for (b, e), j in zip(es, jobs):
-            ts(j[3], e, T.corr[:, 0:1], ADD, [b, "corr"], [j[4]])
-
-    def wrap(*job):
-        wraps([job])
-
-    def lst(name, a=0, b=KW):
-        if name in LOCAL:
-            o = KW * LOCAL.index(name)
-            return T.lloc[:, o + a:o + b]
-        return T["l" + name][:, a:b]
-
-    dma("s", T.hpl[:], T.hp[:], [], ["hpl"])
-    dma("y", T.ut[:], T.u[:], [], ["ut"])
-    dma("s", T.ivl[:], T.iv[:], [], ["ivl"])
-    dma("s", T.mtl[:], T.mt[:], [], ["mtl"])
-    dma("y", T.xin[:], T.x[:], [], ["xin"])
-    dma("s", T.udl[:], T.ud[:], [], ["udl"])
-    dma("y", u8(T.wq[:]), T.wc[:], [], ["wq"])
-    dma("y", T.wsc[:], T.ws[:], [], ["wsc"])
-    dma("y", T.vt[:], T.v[:], [], ["vt"])
-
-    op("v", lambda e: e.memset(T.lordo[:], C - 1), [], ["lordo"])
-    op("g", lambda e: e.iota(T.qi[:], [[0, 8]], 0, 1), [], ["qi"])
-    op("g", lambda e: e.iota(T.pati[:], [[1, C]], 1024, -1), [], ["pati"])
-    op("g", lambda e: e.iota(T.iota[:], [[1, 304]], -MID, 0, allow_small_or_imprecise_dtypes=True), [], ["iota"])
-    op("v", lambda e: e.memset(T.et[:], 0.5), [], ["et"])
-    op("g", lambda e: e.iota(T.k16[:], [[16, KW]], 0, 0, allow_small_or_imprecise_dtypes=True), [], ["k16"])
-    op("g", lambda e: e.iota(T.kb[:], [[-32, KW // 2], [0, 2]], -32, 0, allow_small_or_imprecise_dtypes=True), [], ["kb"])
-    op("g", lambda e: e.iota(T.uoi[:], [[16, 8]], 0, 0), [], ["uoi"])
-    op("g", lambda e: e.iota(T.iom[:], [[1, C]], -1 - MID, 0, allow_small_or_imprecise_dtypes=True), [], ["iom"])
-    op("g", lambda e: e.affine_select(T.et[:], T.et[:], [[1, 520]], EQ, 0.0, -3, -4), ["et"], ["et"])
-    ts(T.qi[:], T.qi[:], 15, AluOpType.bitwise_and, ["qi"], ["qi"])
-    ts(T.qz[:], T.qi[:], 0.0, EQ, ["qi"], ["qz"])
-    ts(T.corr[:], T.qz[:], 2 * BIG, MUL, ["qz"], ["corr"], MID - BIG, ADD)
-    ts(T.pati[:], T.pati[:], 15, AluOpType.bitwise_and, ["pati"], ["pati"])
-    ts(T.pat[:], T.pati[:], 0.0, EQ, ["pati"], ["pat"], BIG, MUL)
-    ts(T.hx[:], T.pati[:], 15.0, EQ, ["pati"], ["hx"], -2 * BIG, MUL)
-    cp(T.lhp[:, 0:KW], T.hpl[:], ["hpl"], ["lhp0"])
-    cp(T.hpr[:, 0:C], T.iota[:, 0:C].indirect(T.lhp[:, 0:KW]), ["iota", "lhp0"], ["hpr0"], "s")
-    tt(T.pat[:], T.pat[:], T.hx[:], ADD, ["pat", "hx"], ["pat"])
-    cp(lst("iv0"), T.ivl[:], ["ivl"], ["liv0"])
-    cp(lst("mto"), T.mtl[:], ["mtl"], ["lmto"])
-    ts(T.thr[:], T.qz[:], -4 * BIG, MUL, ["qz"], ["thr"], 1.5 + 2 * BIG, ADD)
-    cp(T.jw[:, 0:1], T.qi[:, 0:1], ["qi"], ["jwq"])
-    ts(T.jw2[:, 0:KW], T.k16[:], T.jw[:, 0:1], ADD, ["k16", "jwq"], ["jwa"])
-    ts(T.jw2[:, KW:2 * KW], T.k16[:], T.jw[:, 0:1], ADD, ["k16", "jwq"], ["jwb"])
-    JW = T.jw2[:, 0:KW]
-    JK = ["jwa", "jwb"]
-
-    def square(k):
-        if k < 8:
-            cp(T.hpr[:, (k + 1) * C:(k + 2) * C], T.hpr[:, k * C:(k + 1) * C].indirect(T.lhp[:, k * KW:(k + 1) * KW]),
-               ["hpr%d" % k, "lhp%d" % k], ["hpr%d" % (k + 1)], "s")
-
-    def places(k):
-        a, b = (16, 18) if k < 6 or k == 8 else (14, 18) if k == 6 else (10, 18)
-        o = 0 if k == 8 else 16 * a - (1 << k)
-        if k == 0:
-            cp(T.oo[:, 256:C], T.hpr[:, 0:C].indirect(T.lordo[:, a:b]), ["hpr0", "lordo"], ["oo"], "s")
-            cp(T.oo[:, 255:C - 1], T.hpr[:, C:2 * C].indirect(T.lordo[:, a:b]), ["hpr1", "lordo", "oo"], ["oo"], "s")
-        else:
-            cp(T.oo[:, o:o + 16 * (b - a)], T.hpr[:, k * C:(k + 1) * C].indirect(T.lordo[:, a:b]), ["hpr%d" % k, "lordo"], ["oo"], "s")
-        return (256, 288) if k < 5 else (o, o + 16 * (b - a))
-
-    def ring(k, jobs=()):
-        jobs = list(jobs)
-        square(k)
-        s0, s1 = places(k)
-        if k < 7:
-            jobs.append((T.hpr[:, (k + 1) * C:(k + 2) * C], C, "hpr%d" % (k + 1), T.lhp[:, (k + 1) * KW:(k + 2) * KW],
-                         "lhp%d" % (k + 1)))
-        jobs.append((T.oo[:, s0:s1], s1 - s0, "oo", T.lordo[:, s0 // 16:s1 // 16], "lordo"))
-        wraps(jobs)
-
-    op("v", lambda e: e.tensor_copy(T.luo[:], T.uoi[:]), ["uoi"], ["luo"])
-    op("v", lambda e: e.memset(T.fm0[:], 0.0), [], ["fm0"])
-    op("v", lambda e: e.memset(T.fl[:, C + 1:C + 2], 0.0), [], ["fle"])
-    op("v", lambda e: e.memset(T.fl[:, C:C + 1], 1.0), [], ["fl"])
-    cp(T.patf[:], T.pat[:], ["pat"], ["patf"])
-    tt(T.patf[:, 15:C:16], T.pat[:, 15:C:16], T.kb[:], ADD, ["pat", "kb", "patf"], ["patf"])
-    cp(T.im0[:, 0:KW], T.ivl[:], ["ivl"], ["im0"])
-    cp(T.mtw[:], T.mtl[:], ["mtl"], ["mtw"])
-    ring(0)
-    cp(T.mtr[:], T.iota[:, 0:C].indirect(lst("mto")), ["iota", "lmto"], ["mtr"], "s")
-    cp(T.mr[:], T.mtr[:].indirect(lst("iv0")), ["mtr", "liv0"], ["mr"], "s")
-    tt(T.dtw[:], T.mtw[:], JW, SUB, ["mtw"] + JK, ["dtw"])
-    cp(lst("udi"), T.udl[:], ["udl"], ["ludi"])
-
-    def prepare(rd):
-        im = "im%d" % (rd % 2)
-        b, e = scan(T.mr[:], C, "mr")
-        ts(T[im][:, KW:2 * KW], e, T.corr[:, 0:1], ADD, [b, "corr"], [im + "m"])
-        cp(lst("mi"), T[im][:, KW:2 * KW], [im + "m"], ["lmi"])
-        tt(T.ta[:], T[im][:], T.jw2[:], GT, [im, im + "m"] + JK, ["ta"])
-        ts(T.tb[:], T[im][:], float(C + 1), SUB, [im, im + "m"], ["tb"])
-        tt(T.diw[:], T[im][:, KW:2 * KW], T[im][:, 0:KW], SUB, [im, im + "m"], ["diw"])
-        tt(T.nim[:], T.ta[:], T.tb[:], MUL, ["ta", "tb"], ["nim"])
-        tt(T.fm0[:, 1:2 * KW:2], T.nim[:, KW:2 * KW], T.nim[:, 0:KW], SUB, ["nim"], ["fm0"])
-        ts(T.fm1[:, 1:2 * KW:2], T.nim[:, 0:KW], float(C + 1), ADD, ["nim"], ["fm1"])
-
-    for b in ("win", "h1", "h2", "h4", "h8"):
-        cp(T[b][:, C:C + 2], T.iota[:, C:C + 2], ["iota"], [b + "e"])
-    op("v", lambda e: e.memset(T.iom[:, 0:1], float(C - 1 - MID)), ["iom"], ["iom"])
-    op("v", lambda e: e.quantize_mx(T.uq[:], T.usc[:], T.ut[:]), ["ut"], ["u"])
-    op("v", lambda e: e.tensor_copy(T.urq[:, 0:128].bitcast(dt.uint32), T.uq[:, 0:128].bitcast(dt.uint32).indirect(T.luo[:, 0:8])),
-       ["u", "luo"], ["urq"])
-    op("s", lambda e: e.activation(T.ursc[:, 0:128], T.usc[:, 0:128].indirect(T.luo[:, 0:8]), COPY), ["u", "luo"], ["ursc"])
-    prepare(0)
-    op("v", lambda e: e.quantize_mx(T.x0q[:], T.x0sc[:], T.xin[:]), ["xin"], ["x0"])
-    ring(1)
-
-    def mm(bank, l, ls, a, r, rs, reads, c=0, d=C):
-        op("t", lambda e: e.matmul_mx(T.ps[:, 512 * bank:512 * bank + d - c], T[l][:, a:a + 128], T[ls][:, a:a + 128], T[r][:, c:d],
-                                      T[rs][:, c:d], True, True), reads, ["b%d" % bank])
-
-    def bank(k):
-        return T.ps[:, 512 * k:512 * k + C]
-
-    def pl(name, b):
-        return T[name][:, b * C:(b + 1) * C]
-
-    def constants(b):
-        op("v", lambda e: e.quantize_mx(T.eq[:, 128 * b:128 * b + 128], T.esc[:, 128 * b:128 * b + 128], T.et[:, 3 - b:515 - b]),
-           ["et"], ["e%d" % b])
-
-    ud = ["uda", "udb"]
-    for rd, step in enumerate(STEP):
-        xq, xs = "x%dq" % rd, "x%dsc" % rd
-        dst = T.cores[rank ^ step]
-        rel = relays(topo, core, dst)
-        backrel = relays(topo, dst, core)
-        RX, RI, RB, RE = ["%s%d" % (a, rd) for a in ("rx", "ri", "rb", "re")]
-        pq, pks = "p%dq" % rd, "p%dsc" % rd
-
-        def extra(k):
-            if rd == 0:
-                ring(k)
-
-        sync("g", ["x%d" % rd], [])
-        if rel:
-            put(rel[0], u8(T[pq][:, 0:HALF]), u8(T[xq][:, 0:HALF]), RX)
-            put(rel[1], u8(T[pq][:, HALF:C]), u8(T[xq][:, HALF:C]), RX)
-            put(rel[0], T[pks][:], T[xs][:], RX)
-        else:
-            put(dst, u8(T[pq][:]), u8(T[xq][:]), RX)
-            put(dst, T[pks][:], T[xs][:], RX)
-        listto = rel[1] if rel else dst
-        if backrel:
-            wr["p%d" % rd] = (RX, 2 * width(backrel[0], core) + width(backrel[1], core), {})
-            nl = width(backrel[1], core)
-        else:
-            wr["p%d" % rd] = (RX, 2 * width(dst, core), {})
-            nl = width(dst, core)
-        wr["livp%d" % rd] = (RI, nl, {RI: nl})
-        wr["lbp%d" % rd] = (RB, nl, {RB: nl})
-        wr["lep%d" % rd] = (RE, nl, {RE: nl})
-        wr["p%d" % rd][2][RX] = wr["p%d" % rd][1]
-
-        mm(0, "urq", "ursc", 0, xq, xs, ["urq", "ursc", "x%d" % rd], 0, HALF)
-        mm(5, "urq", "ursc", 0, xq, xs, ["urq", "ursc", "x%d" % rd], HALF, C)
-        ts(T.pp[:, 0:HALF], T.ps[:, 0:HALF], 0.0, GT, ["b0"], ["pp"])
-        if rd == 0:
-            constants(0)
-            constants(1)
-        op("s", lambda e: e.activation(T.pp[:, HALF:C], T.ps[:, 2560:2560 + HALF], SIGN), ["b5"], ["pps"])
-        cp(T.r1[:], T.pp[:].indirect(lst("iv%d" % rd)), ["pp", "pps", "liv%d" % rd], ["r1"], "s")
-        cp(T.r3[:], T.pp[:].indirect(lst("mto")), ["pp", "pps", "lmto"], ["r3"], "s")
-        cp(T.r2[:], T.pp[:].indirect(lst("mi")), ["pp", "pps", "lmi"], ["r2"])
-        c2, e2 = scan(T.r2[:], C, "r2")
-        c1, e1 = scan(T.r1[:], C, "r1")
-        tt(T.t1[:], e1, e2, ADD, [c1, c2], ["t1"])
-        ts(T.fm1[:, 0:2 * KW:2], T.t1[:], T.thr[:, 0:1], GE, ["t1", "thr"], ["bo"])
-        op("v", lambda e: e.tensor_tensor_scan(T.fmo[:], T.fm0[:], T.fm1[:], 0.0, MUL, ADD), ["bo", "fm0", "fm1"], ["fmo"])
-        tw = T.fmo[:, 1:2 * KW:2]
-        cp(lst("wino"), tw, ["fmo"], ["lwino"])
-        op("s", lambda e: e.activation(T.win[:, 96:C], T.iota[:, 0:C + 2].indirect(lst("wino", 6, KW)), COPY), ["iota", "lwino"], ["wins"])
-        ts(lst("off1"), tw, float(C), MIN, ["fmo"], ["loff1"])
-        cp(T.win[:, 0:96], T.iota[:, 0:C + 2].indirect(lst("wino", 0, 6)), ["iota", "lwino"], ["win"])
-        imo, imn = "im%d" % (rd % 2), "im%d" % ((rd + 1) % 2)
-        tt(T.di2[:], T.fm1[:, 0:2 * KW:2], T.diw[:], MUL, ["bo", "diw"], ["di2"])
-        tt(T[imn][:, 0:KW], T.di2[:], T[imo][:, 0:KW], ADD, ["di2", imo], [imn])
-        cp(lst("iv%d" % (rd + 1)), T[imn][:, 0:KW], [imn], ["liv%d" % (rd + 1)])
-        sync("g", ["liv%d" % (rd + 1)], [])
-        put(listto, T["livp%d" % rd][:], T["liv%d" % (rd + 1)][:], RI)
-        if rd == 0:
-            constants(2)
-            constants(3)
-        for b in range(4):
-            mm(1 + b, "eq", "esc", 128 * b, xq, xs, ["e%d" % b, "x%d" % rd])
-        cut = CUT if rd else KW
-        extra(2)
-        if rd == 0:
-            cp(T.uda[:], T.iota[:, 0:C].indirect(lst("udi")), ["iota", "ludi"], ["uda"], "s")
-        pick("h1", T.win[:, 0:C + 2], lambda a, b: lst("off1", a, b), ["win", "wins", "wine", "loff1"], "h1", cut)
-        hs = ["h1", "h2", "h4", "h8"]
-        for i in range(4):
-            of = T.lhoff[:, i * KW:(i + 1) * KW]
-            job = (T[hs[i]][:, 0:C], C, hs[i], of, "lhoff%d" % i)
-            if rd == 0:
-                ring(3 + i, [job])
-            else:
-                wraps([job])
-            cp(pl("th", i), bank(1 + i), ["b%d" % (1 + i)], ["th%d" % i], "s")
-            nx = hs[i + 1] if i < 3 else "hx"
-            pick(nx, T[hs[i]][:, 0:C + 2], lambda a, b: T.lhoff[:, i * KW + a:i * KW + b],
-                 [hs[i], hs[i] + "s", hs[i] + "e", "lhoff%d" % i], nx, cut)
-        job = (T.hx[:], C, "hx", lst("foff"), "lfoff", "patf")
-        if rd == 0:
-            ring(7, [job])
-            s0, s1 = places(8)
-        else:
-            wraps([job])
-        for b in range(8, -1, -1):
-            cp(T.fl[:, 32 * b:32 * b + 32], T.fl[:, 32 * b + 32:C + 2].indirect(T.lfoff[:, 2 * b:2 * b + 2]), ["fl", "fle", "lfoff"], ["fl"])
-            if rd == 0 and b == 6:
-                last = scan(T.oo[:, s0:s1], s1 - s0, "oo")
-            if rd == 0 and b == 5:
-                ts(T.lordo[:, 0:2], last[1], T.corr[:, 0:1], ADD, [last[0], "corr"], ["lordo"])
-            if rd == 0 and b == 3:
-                cp(T.r1[:, 0:C].indirect(T.lordo[:, 0:KW]), T.iom[:], ["iom", "lordo"], ["r1"])
-            if rd == 0 and b == 2:
-                last = scan(T.r1[:], C, "r1")
-            if rd == 0 and b == 1:
-                ts(lst("poso"), last[1], T.corr[:, 0:1], ADD, [last[0], "corr"], ["lposo"])
-        def partner():
-            for b in range(4):
-                k = (5, 6, 7, 0)[b]
-                mm(k, "eq", "esc", 128 * b, pq, pks, ["e%d" % b, "p%d" % rd])
-                cp(pl("tp", b), bank(k), ["b%d" % k], ["tp%d" % b], "s")
-
-        if rd in EARLY:
-            partner()
-        op("s", lambda e: e.activation(T.nf[:], T.fl[:, 0:C].indirect(lst("ordo")), IDENT, bias=1.0, scale=-1.0), ["fl", "lordo"], ["nf"])
-        tt(T.fo[:], T.fl[:, 0:C].indirect(lst("ordo")), T.oo[:], MUL, ["fl", "lordo", "oo"], ["fo"])
-        op("v", lambda e: e.tensor_tensor_scan(T.sb[:], T.nf[:], T.fo[:], 0.0, MUL, ADD), ["nf", "fo"], ["sb"])
-        pick("br", T.sb[:], lambda a, b: lst("poso", a, b), ["sb", "lposo"], "br")
-        wrap(T.br[:], C, "br", lst("bo%d" % rd), "lbo%d" % rd)
-        sync("g", ["lbo%d" % rd], [])
-        put(listto, T["lbp%d" % rd][:], T["lbo%d" % rd][:], RB)
-        if rd not in EARLY:
-            partner()
-        def past(b):
-            cp(pl("gv", b), pl("tp", b).indirect(lst("ivp%d" % rd)), ["tp%d" % b, "livp%d" % rd], ["gv%d" % b], "s")
-
-        past(0)
-        past(1)
-        c1, e1 = scan(T.pp[:], C, "pp")
-        c2, e2 = scan(T.r3[:], C, "r3")
-        tt(T.t3[:], e1, e2, ADD, [c1, c2], ["t3"])
-        ts(T.bj[:], T.t3[:], T.thr[:, 0:1], GE, ["t3", "thr"], ["bj"])
-        tt(T.dj[:], T.bj[:], T.dtw[:], MUL, ["bj", "dtw"], ["dj"])
-        tt(T.tf[:], T.dj[:], JW, ADD, ["dj"] + JK, ["tf"])
-        cp(lst("tauo"), T.tf[:], ["tf"], ["ltauo"])
-        uo, un = ud[rd % 2], ud[(rd + 1) % 2]
-        cp(T[un][:], T[uo][:].indirect(lst("tauo")), [uo, "ltauo"], [un], "s")
-        past(2)
-        past(3)
-        cp(T.r2[:], T.br[:].indirect(lst("ivp%d" % rd)), ["br", "brs", "livp%d" % rd], ["r2"])
-        wrap(T.r2[:], C, "r2", lst("eo%d" % rd), "leo%d" % rd)
-        sync("g", ["leo%d" % rd], [])
-        put(listto, T["lep%d" % rd][:], T["leo%d" % rd][:], RE)
-        wrap(T[un][:], C, un, lst("udo"), "ludo")
-        for b in range(4):
-            cp(pl("tu", b), pl("th", b).indirect(lst("udo")), ["th%d" % b, "ludo"], ["tu%d" % b], "s")
-        if rd < 2:
-            cp(T.mr[:], T.mtr[:].indirect(lst("iv%d" % (rd + 1))), ["mtr", "liv%d" % (rd + 1)], ["mr"], "s")
-        for b in range(4):
-            tt(T.zt[:, b:4 * C:4], pl("tp", b).indirect(lst("bp%d" % rd)), pl("gv", b), ADD,
-               ["tp%d" % b, "gv%d" % b, "lbp%d" % rd], ["zt%d" % b])
-        op("v", lambda e: e.quantize_mx(T.zq[:], T.zsc[:], T.zt[:]), ["zt%d" % b for b in range(4)], ["z"])
-        for b in range(4):
-            mm(1 + b, "wq", "wsc", 128 * b, "zq", "zsc", ["wq", "wsc", "z"])
-        for b in range(4):
-            op("s", lambda e: e.activation(pl("hh", b), bank(1 + b), COPY, scale=0.015625), ["b%d" % (1 + b)], ["hh%d" % b])
-        if rd < 2:
-            prepare(rd + 1)
-        else:
-            op("s", lambda e: e.activation(T.udf[:], T[un][:], COPY, bias=float(MID)), [un], ["udf"])
-            dma("y", T.uo[:], T.udf[0:128:16, :], ["udf"], [])
-            op("v", lambda e: e.quantize_mx(T.vq[:], T.vsc[:], T.vt[:]), ["vt"], ["v"])
-        for b in range(4):
-            tt(T.xt[:, b:4 * C:4], pl("hh", b).indirect(lst("ep%d" % rd)), pl("tu", b), ADD,
-               ["hh%d" % b, "tu%d" % b, "lep%d" % rd], ["xt%d" % b])
-        nq = rd + 1
-        op("v", lambda e: e.quantize_mx(T["x%dq" % nq][:], T["x%dsc" % nq][:], T.xt[:]), ["xt%d" % b for b in range(4)], ["x%d" % nq])
-
-    dma("y", T.oc[:], u8(T.x3q[:]), ["x3"], [])
-    for k in range(4):
-        dma("s" if k % 2 else "y", T.osc[4 * k:4 * k + 4, :], T.x3sc[32 * k:32 * k + 4, :], ["x3"], [])
-    mm(5, "vq", "vsc", 0, "x3q", "x3sc", ["v", "x3"], 0, HALF)
-    mm(6, "vq", "vsc", 0, "x3q", "x3sc", ["v", "x3"], HALF, C)
-    cp(T.yf[:, 0:HALF], T.ps[:, 2560:2560 + HALF], ["b5"], ["yf"])
-    cp(T.yf[:, HALF:C], T.ps[:, 3072:3072 + HALF], ["b6"], ["yfs"], "s")
-    dma("y", T.y[:, 0:HALF], T.yf[:, 0:HALF], ["yf"], [])
-    dma("s", T.y[:, HALF:C], T.yf[:, HALF:C], ["yfs"], [])
+        for k in c["writes"]:
+            wr[k], rdr[k] = tok, []
     for s in dsems:
         Q["y"].wait_ge(T.sem[s], 16)
     for q in ("v", "s", "t", "g"):

@@ -6,12 +6,17 @@ MID = 145
 BIG = 512.0
 EVEN, ODD, ODD2 = C, C + 1, C + 3
 CE = C + 4
-LAST = 160
+RUNS = ((0, 160), (160, C))
+ZRUNS = ((0, C),)
 
-CYCLE, GATHER, DONE, SLACK = 0.001, 1.5, 0.1, 0.03
-HOP, CODES, LOAD = 2.6, 5.0, 2.0
-LEADI, LEADU = 4.0, 3.0
-CUT = {"ring0": 8, "ring": 0, "mates": 8, "h0": 10, "h": 10, "br": 10}
+CYCLE, GATHER, DONE, SLACK = 0.001, 1.5, 0.12, 0.03
+HOP, SPARE, CODES, LOAD = 2.5, 1.0, 5.5, 2.0
+LEADI, LEADU, LEADR, LEADP = 3.0, 1.0, 1.0, 8.0
+PLACE = "sv"
+TWO0, TWO, PASSES = False, True, 4
+MOVES, MARGIN = 40000, 0.1
+ARRANGED = {}
+CUT = {"ring0": 0, "ring": 0, "mates": 8, "h0": 6, "h": 10, "br": 10}
 
 SCRATCH = {}
 for _n in ("xin", "xt", "zt", "th", "tp", "tu", "gv", "hh"):
@@ -19,7 +24,6 @@ for _n in ("xin", "xt", "zt", "th", "tp", "tu", "gv", "hh"):
 for _n in ("ut", "vt"):
     SCRATCH[_n] = ("sbuf", [128, 512], "bfloat16")
 SCRATCH["et"] = ("sbuf", [128, 520], "bfloat16")
-SCRATCH["half"] = ("sbuf", [128, 128], "bfloat16")
 for _n, _w in (("x0", C), ("x1", C), ("x2", C), ("x3", C), ("p0", C), ("p1", C), ("p2", C), ("z", C),
                ("u", 128), ("ur", 128), ("v", 128), ("e", 512), ("w", 512)):
     SCRATCH[_n + "q"] = ("sbuf", [128, _w], "float8_e4m3fn_x4")
@@ -27,22 +31,25 @@ for _n, _w in (("x0", C), ("x1", C), ("x2", C), ("x3", C), ("p0", C), ("p1", C),
 SCRATCH["ramp"] = ("sbuf", [128, 16 + 304], "bfloat16")
 for _n in ("h1", "h2", "h4", "h8", "fl"):
     SCRATCH[_n] = ("sbuf", [128, 304], "bfloat16")
-for _n in ("pat", "patf", "pp", "r1", "r2", "r3", "hx", "nf", "fo", "sb", "br", "uda", "mtr", "mr", "um", "oo"):
+for _n in ("patf", "pp", "r1", "r2", "r3", "hx", "nf", "fo", "sb", "br", "uda", "mtr", "mr", "um", "oo"):
     SCRATCH[_n] = ("sbuf", [128, C], "bfloat16")
-SCRATCH["hpr"] = ("sbuf", [128, 8 * C], "bfloat16")
+SCRATCH["pat"] = ("sbuf", [128, C + 64], "bfloat16")
+SCRATCH["hpr"] = ("sbuf", [128, 2 * C + 64], "bfloat16")
 SCRATCH["win"] = ("sbuf", [128, 2 * C + 16], "bfloat16")
 SCRATCH["d0"] = ("sbuf", [128, 2 * C], "bfloat16")
 SCRATCH["d1"] = ("sbuf", [128, 2 * C], "float16")
-SCRATCH["dd"] = ("sbuf", [128, C], "float16")
-SCANS = ("ch", "cr", "co", "cm", "cg", "ce", "cp", "c3", "cw0", "cw1", "cw2")
-SCRATCH["cc"] = ("sbuf", [128, len(SCANS) * C], "float16")
-for _n in ("i16", "pa", "pb"):
+SCRATCH["dd"] = ("sbuf", [128, C], "float32")
+SCRATCH["wide"] = ("sbuf", [128, 2 * CE], "float32")
+SCANS = ("ch", "co", "cm", "cg", "ce", "cp", "c3", "cw0", "cw1", "cw2", "cr")
+SCRATCH["cc"] = ("sbuf", [128, len(SCANS) * C + 64], "float16")
+for _n in ("pa", "pb"):
     SCRATCH[_n] = ("sbuf", [128, 32], "bfloat16")
 for _n in ("ivl", "mtl", "udl", "hpl"):
     SCRATCH[_n] = ("sbuf", [128, KW], "int32")
-SCRATCH["qi"] = ("sbuf", [128, 8], "int32")
+SCRATCH["i32"] = ("sbuf", [128, 32], "int32")
+SCRATCH["qi"] = ("sbuf", [128, 2], "int32")
 SCRATCH["col"] = ("sbuf", [128, 8], "float32")
-SMALL = ("k16", "kb", "jw", "ivf", "mif", "di", "ga", "gb", "ta", "tb", "na", "nb", "e0", "sig", "bi", "ti", "fb",
+SMALL = ("k16", "kb", "jw", "ivf", "mif", "di", "ga", "gb", "ta", "tb", "na", "nb", "e0", "df", "sg", "bi", "ti", "fb",
          "udf", "umf", "du", "t3", "bj", "tj")
 SCRATCH["sm"] = ("sbuf", [128, len(SMALL) * 20], "float32")
 LOCAL = ("iv0", "mi", "mto", "udo", "wo", "poso", "fa", "fb", "foff", "ordo", "go")
@@ -51,7 +58,7 @@ for _n in ("iv1", "iv2", "iv3", "bo0", "bo1", "bo2", "eo0", "eo1", "eo2",
            "ivp0", "ivp1", "ivp2", "bp0", "bp1", "bp2", "ep0", "ep1", "ep2"):
     SCRATCH["l" + _n] = ("sbuf", [128, KW], "uint16")
 SCRATCH["lhoff"] = ("sbuf", [128, 4 * KW], "uint16")
-SCRATCH["lhp"] = ("sbuf", [128, 7 * KW], "uint16")
+SCRATCH["lhp"] = ("sbuf", [128, 2 * KW + 4], "uint16")
 SCRATCH["luo"] = ("sbuf", [128, 8], "uint16")
 SCRATCH["uoi"] = ("sbuf", [128, 8], "int32")
 SCRATCH["uof"] = ("sbuf", [128, C], "float32")
@@ -80,34 +87,104 @@ def relays(topo, src, dst):
 def arrange(calls):
     wr, rd = {}, {}
     for i, c in enumerate(calls):
-        c["after"] = {wr[k] for k in c["reads"] + c["writes"] if k in wr}
+        after = {wr[k] for k in c["reads"] + c["writes"] if k in wr}
         for k in c["writes"]:
-            c["after"] |= set(rd.get(k, []))
+            after |= set(rd.get(k, []))
         for k in c["reads"]:
             rd.setdefault(k, []).append(i)
         for k in c["writes"]:
             wr[k], rd[k] = i, []
-        c["chain"] = 0.0
+        c["after"] = dict({a: 0.0 for a in c["behind"]}, **{})
+        c["after"].update({a: calls[a]["late"] for a in after})
+        c["before"], c["chain"] = {}, c["late"]
+        for a, gap in c["after"].items():
+            calls[a]["before"][i] = gap
     for c in reversed(calls):
-        c["chain"] += min(w[1] for w in c["ways"]) + c["late"] + c["lead"]
-        for a in c["after"]:
-            calls[a]["chain"] = max(calls[a]["chain"], c["chain"])
-    busy = {}
-    for c in sorted(calls, key=lambda c: -c["chain"]):
-        ready = max([calls[a]["end"] for a in c["after"]], default=0.0)
-        best = None
-        for q, cost, call in c["ways"]:
-            t = ready
-            for a, b in busy.setdefault(q, []):
-                if t + cost <= a + min(SLACK, cost / 2):
-                    break
-                t = max(t, b)
-            if best is None or t + cost < best[0] + best[2]:
-                best = (t, q, cost, call)
-        c["start"], c["queue"], cost, c["call"] = best
-        c["end"] = c["start"] + cost + c["late"]
-        busy[c["queue"]] = sorted(busy[c["queue"]] + [(c["start"], c["start"] + cost)])
-    return sorted(calls, key=lambda c: c["start"])
+        c["chain"] += min(w[1] for w in c["ways"]) + c["lead"]
+        for a, gap in c["after"].items():
+            calls[a]["chain"] = max(calls[a]["chain"], c["chain"] + gap)
+
+    every = range(len(calls))
+    shape = tuple(c["late"] for c in calls)
+    if shape not in ARRANGED:
+        busy, end, way = {}, {}, {}
+        for i in sorted(every, key=lambda i: -calls[i]["chain"]):
+            ready = max([end[a] + gap for a, gap in calls[i]["after"].items()], default=0.0)
+            best = None
+            for q, cost, call in calls[i]["ways"]:
+                t = ready
+                for a, b in busy.setdefault(q, []):
+                    if t + cost <= a + SLACK:
+                        break
+                    t = max(t, b)
+                if best is None or t + cost < best[0] + best[2]:
+                    best = (t, q, cost)
+            way[i], end[i] = best, best[0] + best[2]
+            busy[best[1]] = sorted(busy[best[1]] + [(best[0], end[i])])
+        ARRANGED[shape] = shorten(calls, sorted(every, key=lambda i: way[i][0]), [way[i][1] for i in every])
+    order, queue = ARRANGED[shape]
+    for i, c in enumerate(calls):
+        c["queue"] = queue[i]
+        c["call"] = [w[2] for w in c["ways"] if w[0] == queue[i]][0]
+    return [calls[i] for i in order]
+
+
+def shorten(calls, order, queue):
+    n = len(calls)
+    after = [list(c["after"].items()) for c in calls]
+    cost = [{w[0]: w[1] for w in c["ways"]} for c in calls]
+
+    ends = [i for i in range(n) if not calls[i]["before"]]
+
+    def run(order, queue, bound):
+        end, cause, free, last = [0.0] * n, [-1] * n, {}, {}
+        for i in order:
+            q = queue[i]
+            t, c = free.get(q, 0.0), last.get(q, -1)
+            for a, gap in after[i]:
+                if end[a] + gap > t:
+                    t, c = end[a] + gap, a
+            cause[i], last[q] = c, i
+            end[i] = free[q] = t + cost[i][q]
+        long, i = max((end[i] + calls[i]["late"], i) for i in ends)
+        if long > bound:
+            return None
+        held = []
+        while cause[i] >= 0:
+            if cause[i] not in calls[i]["after"]:
+                held.append((cause[i], i))
+            i = cause[i]
+        return long, held, sorted(order, key=lambda i: end[i] - cost[i][queue[i]]), queue
+
+    seed = [1]
+
+    def some(k):
+        seed[0] = (seed[0] * 1103515245 + 12345) % 2 ** 31
+        return (seed[0] >> 8) % k
+
+    now = best = run(order, queue, 1e9)
+    for step in range(MOVES):
+        c, i = now[1][some(len(now[1]))]
+        order, queue, kind = list(now[2]), now[3], some(7)
+        if kind == 0:
+            x = (c, i)[some(2)]
+            queue = list(queue)
+            queue[x] = [q for q in cost[x] if q != queue[x] or len(cost[x]) == 1][0]
+        elif kind < 4:
+            a, b = order.index(i), min([order.index(k) for k in calls[c]["before"]], default=n)
+            if b <= a:
+                continue
+            order.remove(c)
+            order.insert(a + some(b - a) * some(2), c)
+        else:
+            a, b = max([order.index(k) for k in calls[i]["after"]], default=-1), order.index(c)
+            if b <= a:
+                continue
+            order.remove(i)
+            order.insert(b - some(b - a) * some(2), i)
+        now = run(order, queue, now[0] + MARGIN * (1 - step / MOVES) * some(100) / 100) or now
+        best = min(best, now, key=lambda r: r[0])
+    return best[2:]
 
 
 def rank_program(g, core, T, topo):
@@ -115,7 +192,7 @@ def rank_program(g, core, T, topo):
     sent = [0]
 
     def width(a, b):
-        return len(topo.engines(a, b)[:8])
+        return len(topo.engines(a, b))
 
     def put(dst, out, in_, sem):
         e = topo.engines(core, dst)[:width(core, dst)]
@@ -156,7 +233,10 @@ def rank_program(g, core, T, topo):
 
     def add(ways, reads, writes, late=DONE, kind="op", arrive=None):
         calls.append({"ways": ways, "reads": list(reads), "writes": list(writes), "late": late, "kind": kind, "arrive": arrive,
-                      "lead": 0.0})
+                      "lead": 0.0, "behind": []})
+
+    def behind():
+        calls[-1]["behind"].append(len(calls) - 2)
 
     def sooner(lead):
         calls[-1]["lead"] = lead
@@ -238,23 +318,35 @@ def rank_program(g, core, T, topo):
     def small(out, a, b, o):
         tt(sm(out), sm(a), sm(b), o, [a, b], [out])
 
-    def pick(out, win, off, reads, key, k):
-        take(out[:, 16 * k:C], win.indirect(off(k, KW)), C - 16 * k, reads, [key + "s"] + ([] if k else [key]), "s")
+    def pick(out, win, off, reads, key, k, okey=None):
+        take(out[:, 16 * k:C], win.indirect(off(k, KW)), C - 16 * k, reads + (both(okey)[k > 0:] if okey else []),
+             both(key)[k > 0:], "s")
         if k:
-            take(out[:, 0:16 * k], win.indirect(off(0, k)), 16 * k, reads, [key], "v")
+            take(out[:, 0:16 * k], win.indirect(off(0, k)), 16 * k, reads + ([okey] if okey else []), [key], "v")
 
     def both(key):
         return [key, key + "s"]
 
-    def scan(row, n, reads, b, pat="pat"):
-        o = C * SCANS.index(b)
-        vec(lambda e: e.tensor_tensor_scan(T.cc[:, o:o + n], row, T[pat][:, 0:n], -2 * BIG, MAX, ADD), vcost(n, 0.5), reads + [pat], [b])
-        return b, T.cc[:, o + 15:o + n:16]
+    def scan(row, n, reads, b, pat="pat", c=0, key=None):
+        o = C * SCANS.index(b) + c
+        vec(lambda e: e.tensor_tensor_scan(T.cc[:, o:o + n], row, T[pat][:, c:c + n], -2 * BIG, MAX, ADD), vcost(n, 0.5), reads + [pat],
+            [key or b])
+        return key or b, T.cc[:, o + 15:o + n:16]
 
-    Q0, Q15, QZ, CORR, CORR2, THR = [T.col[:, i:i + 1] for i in range(6)]
+    Q0, QZ, CORR, CORR2, THR, QP = [T.col[:, i:i + 1] for i in range(6)]
 
     def land(job, out, key):
         ts(out, job[1], CORR, ADD, [job[0], "corr"], [key])
+
+    def wrap(row, key, off, okey, k, pat="pat"):
+        if not k:
+            job = scan(row[:, 0:C], C, both(key), "ch", pat)
+            calls[-1]["writes"].append("chs")
+            land(job, off(0, KW), okey)
+            calls[-1]["writes"].append(okey + "s")
+            return
+        land(scan(row[:, 16 * k:C], C - 16 * k, [key + "s"], "ch", pat, 16 * k, "chs"), off(k, KW), okey + "s")
+        land(scan(row[:, 0:16 * k], 16 * k, [key], "ch", pat), off(0, k), okey)
 
     IOTA = T.ramp[:, 16:16 + CE]
 
@@ -265,64 +357,89 @@ def rank_program(g, core, T, topo):
         t += long
         dma(q, to, src[:], [], [key], t, "load")
 
-    fill(T.half[:], 0.5, ["half"])
     fill(T.et[:], 0.0, ["et"], 520)
-    pool(lambda e: e.iota(T.qi[:], [[15, 2], [0, 4]], 0, 1), 8, [], ["qi"])
-    count(T.i16[:], [[0, 2], [1, 16]], 0, 32, ["i16"])
-    pool(lambda e: e.affine_select(T.et[:, 3:515:4], T.half[:], [[1, 128]], EQ, 0.0, 0, -1), 128, ["et", "half"], ["et"])
-    count(T.ramp[:], [[1, 320]], -16 - MID, 320, ["iota"])
+    fill(T.d0[:, 0:2 * C:2], 0.0, ["d0e"], C)
+    fill(T.win[:, 2 * C:2 * CE], float(EVEN - MID), ["wine"])
+    fill(T.win[:, 2 * EVEN + 1:2 * EVEN + 2], float(ODD - MID), ["wine"])
+    fill(T.fl[:, C:CE], 0.0, ["fle"])
+    fill(T.fl[:, EVEN:EVEN + 1], 1.0, ["fle"])
+    fill(T.ramp[:, 15:16], float(C - 1 - MID), ["iom"])
+    pool(lambda e: e.iota(T.i32[:], [[1, 32]], 1024, -1), 32, [], ["i32"])
+    sooner(1.0)
+    pool(lambda e: e.iota(T.qi[:], [[0, 2]], 0, 1), 2, [], ["qi"])
+    count(T.ramp[:, 16:320], [[1, 304]], -MID, 304, ["iota"])
+    count(T.wide[:], [[1, 2 * CE]], -CE, 2 * CE, ["wide"])
     count(sm("k16"), [[16, KW]], 0, KW, ["k16"])
     pool(lambda e: e.iota(T.uoi[:], [[16, 8]], 0, 0), 8, [], ["uoi"])
     count(sm("kb"), [[-32, KW // 2], [0, 2]], -32, KW, ["kb"])
-    count(T.d0[:, 0:2 * C:2], [[0, C]], 0, C, ["d0e"])
     for b in ("h1", "h2", "h4", "h8"):
         count(T[b][:, C:CE], [[1, 4]], C - MID, 4, [b + "e"])
-    count(T.win[:, 2 * C:2 * CE], [[0, 8]], EVEN - MID, 8, ["wine"])
-    count(T.win[:, 2 * EVEN + 1:2 * EVEN + 2], [[0, 1]], ODD - MID, 1, ["wine"])
-    count(T.fl[:, C:CE], [[0, 4]], 0, 4, ["fle"])
-    count(T.fl[:, EVEN:EVEN + 1], [[0, 1]], 1, 1, ["fle"])
-    count(T.ramp[:, 15:16], [[0, 1]], C - 1 - MID, 1, ["iom"], ["iota"])
-    fill(lst("ordo"), C - 1, ["lordo"])
+    ts(QP, T.qi[:, 0:1], float(MID), SUB, ["qi"], ["qp"])
+    ts(T.et[:, 3:515:4], IOTA[:, 0:128], QP, EQ, ["iota", "qp", "et"], ["et"], 0.5, MUL)
     ts(T.qi[:], T.qi[:], 15, AND, ["qi"], ["qi"])
-    cp(T.col[:, 0:2], T.qi[:, 3:5], ["qi"], ["q0"])
-    ts(T.pa[:], T.i16[:], Q0, EQ, ["i16", "q0"], ["pa"], BIG, MUL)
-    ts(T.pb[:], T.i16[:], Q15, EQ, ["i16", "q0"], ["pb"], -2 * BIG, MUL)
-    ts(QZ, Q0, 0.0, EQ, ["q0"], ["qz"])
-    tt(T.pat[:, 0:32], T.pa[:], T.pb[:], ADD, ["pa", "pb"], ["pat"])
-    for a, n in ((32, 32), (64, 64), (128, 128), (256, 32)):
-        cp(T.pat[:, a:a + n], T.pat[:, 0:n], ["pat"], ["pat"])
+    cp(Q0, T.qi[:, 0:1], ["qi"], ["q0"])
+    ts(QZ, T.qi[:, 0:1], 0.0, EQ, ["qi"], ["qz"])
+    ts(T.i32[:], T.i32[:], 15, AND, ["i32"], ["i32"])
+    ts(T.pa[:], T.i32[:], 0.0, EQ, ["i32"], ["pa"], BIG, MUL)
+    ts(T.pb[:], T.i32[:], 15.0, EQ, ["i32"], ["pb"], -2 * BIG, MUL)
+    tt(T.pat[:, 0:32], T.pa[:], T.pb[:], ADD, ["pa", "pb"], ["pat0"])
+    for a in (32, 64, 96):
+        cp(T.pat[:, a:a + 32], T.pat[:, 0:32], ["pat0"], ["pat%d" % a])
+    cp(T.pat[:, 128:256], T.pat[:, 0:128], ["pat0", "pat32", "pat64", "pat96"], ["pat128"])
+    cp(T.pat[:, 256:352], T.pat[:, 0:96], ["pat0", "pat32", "pat64", "pat128"], ["pat"])
     ts(CORR, QZ, 2 * BIG, MUL, ["qz"], ["corr"], MID - BIG, ADD)
     ts(CORR2, QZ, 2 * BIG, MUL, ["qz"], ["corr2"], MID - BIG + 0.5, ADD)
     ts(THR, QZ, -4 * BIG, MUL, ["qz"], ["thr"], 1.5 + 2 * BIG, ADD)
-    unload(T.patf[:], T.pat[:], C, ["pat"], ["patf"], "s")
+    unload(T.patf[:], T.pat[:, 0:C], C, ["pat"], ["patf"], "s")
+    sooner(LEADP)
     tt(T.patf[:, 15:C:16], T.pat[:, 15:C:16], sm("kb"), ADD, ["pat", "kb", "patf"], ["patf"])
     ts(sm("jw"), sm("k16"), Q0, ADD, ["k16", "q0"], ["jw"])
     for b in range(4):
         quant("e", T.et[:, 3 - b:515 - b], ["et"], 128 * b, 128 * b + 128, "e%d" % b)
 
-    def hrow(k):
-        return T.hpr[:, k * C:(k + 1) * C]
+    TOP = C + 32
 
-    cp(T.lhp[:, 0:KW], T.hpl[:], ["hpl"], ["lhp0"])
-    pick(hrow(0), IOTA, lambda a, b: T.lhp[:, a:b], ["iota", "lhp0"], "hpr0", CUT["ring0"])
+    def hrow(k):
+        return T.hpr[:, TOP + 32:TOP + 32 + C] if k % 2 else T.hpr[:, 0:C]
+
+    def hoff(k):
+        return lambda a, b: T.lhp[:, (k % 2) * (TOP + 32) // 16 + a:(k % 2) * (TOP + 32) // 16 + b]
+
+    top = T.lhp[:, TOP // 16:TOP // 16 + 2]
+    fill(top, C - 1, ["ltop"])
+    fill(T.hpr[:, C:TOP], 0.0, ["top"])
+    cp(hoff(0)(0, KW), T.hpl[:], ["hpl"], ["lhp0"])
+    pick(hrow(0), IOTA, hoff(0), ["iota", "lhp0"], "hpr0", CUT["ring0"])
     for k in range(9):
+        here, there = both("hpr%d" % (min(k, 7) % 2)), "hpr%d" % ((k + 1) % 2)
         if k < 7:
-            pick(hrow(k + 1), hrow(k), lambda a, b: T.lhp[:, k * KW + a:k * KW + b], both("hpr%d" % k) + ["lhp%d" % k],
-                 "hpr%d" % (k + 1), CUT["ring0" if k < 2 else "ring"])
-        a, b = (16, 18) if k < 6 else (14, 18) if k == 6 else (10, 18) if k == 7 else (8, 10)
-        o = 16 * a - (1 << min(k, 7))
+            pick(hrow(k + 1), hrow(k), hoff(k), here + ["lhp%d" % (k % 2)], there, CUT["ring0" if k < 2 else "ring"])
         if k == 0:
-            take(T.oo[:, 256:C], hrow(0).indirect(lst("ordo", a, b)), 32, both("hpr0") + ["lordo"], ["oo"])
-            take(T.oo[:, 255:C - 1], hrow(1).indirect(lst("ordo", a, b)), 32, both("hpr1") + ["lordo"], ["oo"])
-        else:
-            take(T.oo[:, o:o + 16 * (b - a)], hrow(min(k, 7)).indirect(lst("ordo", a, b)), 16 * (b - a),
-                 both("hpr%d" % min(k, 7)) + ["lordo"], ["oo"])
-        s0, s1 = (256, C) if k < 5 else (o, o + 16 * (b - a))
-        if k < 6:
-            land(scan(hrow(k + 1), C, both("hpr%d" % (k + 1)), "cr"), T.lhp[:, (k + 1) * KW:(k + 2) * KW], "lhp%d" % (k + 1))
+            take(T.hpr[:, TOP:TOP + 32], hrow(0).indirect(top), 32, here + ["ltop"], ["top"], PLACE)
+            take(T.hpr[:, TOP - 1:TOP + 31], hrow(1).indirect(top), 32, both(there) + ["ltop"], ["top"], PLACE)
+        elif k < 5:
+            take(T.hpr[:, TOP - (1 << k):TOP + 32 - (1 << k)], hrow(k).indirect(top), 32, here + ["ltop"], ["top"], PLACE)
+        if k < 5:
+            s0, s1 = (0, TOP + 32) if k % 2 else (TOP, TOP + 32 + C)
+            land(scan(T.hpr[:, s0:s1], s1 - s0, both(there) + ["top"], "cr"), T.lhp[:, s0 // 16:s1 // 16], "ltop")
+            calls[-1]["writes"].append("lhp%d" % ((k + 1) % 2))
+            continue
+        if k == 5:
+            cp(lst("ordo", 16, 18), top, ["ltop"], ["lordo"])
+            cp(T.oo[:, 256:C], T.hpr[:, TOP:TOP + 32], ["top"], ["ootop"])
+            land(scan(hrow(6), C, both(there), "cr"), hoff(6)(0, KW), "lhp0")
+        a, b = {5: (16, 18), 6: (14, 18), 7: (10, 18), 8: (8, 10)}[k]
+        s0 = 16 * a - (1 << min(k, 7))
+        s1 = s0 + 16 * (b - a)
+        take(T.oo[:, s0:s1], hrow(min(k, 7)).indirect(top if k == 5 else lst("ordo", a, b)), s1 - s0,
+             here + ["ltop" if k == 5 else "lordo"], ["oo"], PLACE)
         land(scan(T.oo[:, s0:s1], s1 - s0, ["oo"], "co"), lst("ordo", s0 // 16, s1 // 16), "lordo")
-    cp(T.r1[:].indirect(lst("ordo")), T.ramp[:, 15:15 + C], ["iota", "iom", "lordo"], ["r1"], 0.05 + 3.5 * C * CYCLE)
+        if k >= 6:
+            s1 = C if k == 6 else s1
+            cp(T.r1[:].indirect(lst("ordo", s0 // 16, s1 // 16)), T.ramp[:, 15 + s0:15 + s1], ["iota", "iom", "lordo"], ["r1"],
+               0.05 + 3.5 * (s1 - s0) * CYCLE)
     land(scan(T.r1[:], C, ["r1"], "cg"), lst("poso"), "lposo")
+    sooner(LEADR)
 
     cp(lst("mto"), T.mtl[:], ["mtl"], ["lmto"])
     cp(lst("iv0"), T.ivl[:], ["ivl"], ["liv0"])
@@ -332,15 +449,16 @@ def rank_program(g, core, T, topo):
     job = scan(T.mr[:], C, both("mr"), "cm")
     land(job, sm("mif"), "mif")
     land(job, lst("mi"), "lmi")
-    for f, n, end, to in (("ivf", "a", ODD, "fa"), ("mif", "b", ODD2, "fb")):
+    for f, n, end in (("ivf", "a", ODD), ("mif", "b", ODD2)):
         small("g" + n, f, "jw", GT)
         ts(sm("t" + n), sm(f), float(end), SUB, [f], ["t" + n])
         small("n" + n, "g" + n, "t" + n, MUL)
-        ts(lst(to), sm("n" + n), float(end), ADD, ["n" + n], ["l" + to])
+    ts(lst("fa"), sm("na"), float(ODD), ADD, ["na"], ["lfa"])
     take(T.win[:, 1:2 * C:2], IOTA.indirect(lst("fa")), C, ["iota", "lfa"], ["win"], "s")
+    small("fb", "nb", "na", SUB)
+    ts(lst("fb"), sm("fb"), float(ODD2 - ODD + CE), ADD, ["fb"], ["lfb"])
+    ts(sm("df"), sm("fb"), float(ODD2 - ODD), ADD, ["fb"], ["df"])
     ts(sm("e0"), sm("na"), float(ODD), ADD, ["na", "corr"], ["e0"], CORR, SUB)
-    ts(sm("fb"), sm("nb"), float(ODD2), ADD, ["nb"], ["fb"])
-    small("sig", "fb", "e0", ADD)
     small("di", "mif", "ivf", SUB)
     cp(lst("udo"), T.udl[:], ["udl"], ["ludo"])
     cp(sm("udf"), T.udl[:], ["udl"], ["udf"])
@@ -372,12 +490,12 @@ def rank_program(g, core, T, topo):
         nx = 2 * width(back[0], core) + width(back[1], core) if back else 2 * width(dst, core)
         send(parts, [x], p, "rx%d" % rd, nx, CODES + (hops - 1) * HOP)
 
-        def mail(name, to, sem):
+        def mail(name, to, sem, spare=SPARE):
             send([(rel[1] if rel else dst, lst(to), lst(name))], ["l" + name], "l" + to, sem, width(back[1] if back else dst, core),
-                 hops * HOP - 0.4)
+                 hops * HOP - 0.4 + spare)
 
         cp(T.d1[:, 1:2 * C:2], T.win[:, 1:2 * C:2], ["win"], ["d1a"], vcost(C, 0.5))
-        tt(T.dd[:], IOTA.indirect(lst("fb")), T.win[:, 1:2 * C:2], SUB, ["iota", "lfb", "win"], ["dd"], gcost("v", C))
+        take(T.dd[:], T.wide[:].indirect(lst("fb")), C, ["wide", "lfb"], ["dd"], "s" if first else "sv")
         mm(0, "ur", 0, x, ["urq", "ursc", x], 0, HALF)
         mm(5, "ur", 0, x, ["urq", "ursc", x], HALF, C)
         ts(T.pp[:, 0:HALF], bank(0, HALF), 0.0, GT, ["b0"], ["pp"], cost=vcost(HALF, 1))
@@ -386,11 +504,16 @@ def rank_program(g, core, T, topo):
         tt(T.d1[:, 0:2 * C:2], T.pp[:].indirect(lst("mi")), T.dd[:], MUL, both("pp") + ["lmi", "dd"], ["d1"], gcost("v", C))
         vec(lambda e: e.tensor_tensor_scan(T.win[:, 0:2 * C], T.d0[:], T.d1[:], 0.0, MUL, ADD), vcost(2 * C, 0.5),
             ["d0", "d0e", "d1", "d1a"], ["win"])
-        job = scan(T.win[:, 1:2 * C:2], C, ["win"], "cw%d" % rd)
-        ts(lst("wo"), job[1], CORR2, ADD, [job[0], "corr2"], ["lwo"], 2.0, MUL)
-        old = ("e0", sm("e0")) if first else last
-        last = job
-        tt(sm("bi"), job[1], old[1], NE, [job[0], old[0]], ["bi"])
+        cut = CUT["h0" if first else "h"]
+        two = cut if (TWO0 if first else TWO) else 0
+        cw = "cw%d" % rd
+        for a, b, keys in ((two, KW, both(cw)[two > 0:]), (0, two, [cw]))[:2 if two else 1]:
+            job = scan(T.win[:, 32 * a + 1:32 * b:2], 16 * (b - a), ["win"], cw, "pat", 16 * a, keys[-1])
+            calls[-1]["writes"] = keys
+            ts(lst("wo", a, b), job[1], CORR2, ADD, keys + ["corr2"], ["lwo" + k[3:] for k in keys], 2.0, MUL)
+        old = (["e0"], sm("e0")) if first else last
+        last = (both(cw), T.cc[:, C * SCANS.index(cw) + 15:C * (SCANS.index(cw) + 1):16])
+        tt(sm("bi"), last[1], old[1], NE, last[0] + old[0], ["bi"])
         small("ti", "bi", "di", MUL)
         small("ivf", "ivf", "ti", ADD)
         cp(lst("iv%d" % (rd + 1)), sm("ivf"), ["ivf"], ["liv%d" % (rd + 1)])
@@ -400,8 +523,9 @@ def rank_program(g, core, T, topo):
             small("mif", "mif", "ti", SUB)
             cp(lst("mi"), sm("mif"), ["mif"], ["lmi"])
             small("di", "mif", "ivf", SUB)
-            tt(sm("fb"), sm("sig"), job[1], SUB, ["sig", job[0]], ["fb"])
-            cp(lst("fb"), sm("fb"), ["fb"], ["lfb"])
+            ts(sm("sg"), sm("bi"), -2.0, MUL, ["bi"], ["sg"], 1.0, ADD)
+            small("df", "df", "sg", MUL)
+            ts(lst("fb"), sm("df"), float(CE), ADD, ["df"], ["lfb"])
         take(T.r3[:], T.pp[:].indirect(lst("mto")), C, both("pp") + ["lmto"], ["r3"])
         j1 = scan(T.pp[:], C, both("pp"), "cp")
         j2 = scan(T.r3[:], C, ["r3"], "c3")
@@ -424,56 +548,66 @@ def rank_program(g, core, T, topo):
             unload(pl("tp", b), bank(k), C, ["b%d" % k], ["tp%d" % b])
             take(pl("gv", b), pl("tp", b).indirect(lst("ivp%d" % rd)), C, ["tp%d" % b, "livp%d" % rd], ["gv%d" % b])
         hs = ["h1", "h2", "h4", "h8", "hx"]
-        cut = CUT["h0" if first else "h"]
-        pick(T.h1, T.win[:, 0:2 * CE], lambda a, b: lst("wo", a, b), ["win", "wine", "lwo"], "h1", cut)
+        pick(T.h1, T.win[:, 0:2 * CE], lambda a, b: lst("wo", a, b), ["win", "wine"], "h1", cut, "lwo")
         for i in range(4):
-            land(scan(T[hs[i]][:, 0:C], C, both(hs[i]), "ch"), T.lhoff[:, i * KW:(i + 1) * KW], "lhoff%d" % i)
-            pick(T[hs[i + 1]], T[hs[i]][:, 0:CE], lambda a, b: T.lhoff[:, i * KW + a:i * KW + b],
-                 both(hs[i]) + [hs[i] + "e", "lhoff%d" % i], hs[i + 1], cut)
-        land(scan(T.hx[:], C, both("hx"), "ch", "patf"), lst("foff"), "lfoff")
+            def off(a, b):
+                return T.lhoff[:, i * KW + a:i * KW + b]
+            wrap(T[hs[i]], hs[i], off, "lhoff%d" % i, two)
+            pick(T[hs[i + 1]], T[hs[i]][:, 0:CE], off, both(hs[i]) + [hs[i] + "e"], hs[i + 1], cut, "lhoff%d" % i)
+        wrap(T.hx, "hx", lambda a, b: lst("foff", a, b), "lfoff", two, "patf")
         ts(T.fl[:, 256:C], T.hx[:, 256:C], float(EVEN - MID), EQ, both("hx"), ["fl"])
         if not first:
             take(T.r1[:], T.hx[:].indirect(lst("ordo")), C, both("hx") + ["lordo"], ["r1"], "s")
             land(scan(T.r1[:], C, ["r1"], "cg"), lst("go"), "lgo")
         for b in range(7, -1 if first else 0, -1):
-            take(T.fl[:, 32 * b:32 * b + 32], T.fl[:, 32 * b + 32:CE].indirect(lst("foff", 2 * b, 2 * b + 2)), 32, ["fl", "fle", "lfoff"],
-                 ["fl"], "vs")
+            take(T.fl[:, 32 * b:32 * b + 32], T.fl[:, 32 * b + 32:CE].indirect(lst("foff", 2 * b, 2 * b + 2)), 32,
+                 ["fl", "fle", both("lfoff")[2 * b >= two]], ["fl"], "vs")
         key = "ordo" if first else "go"
         add([("s", gcost("s", C), lambda e, key=key: e.activation(T.nf[:], T.fl[:, 0:CE].indirect(lst(key)), IDENT, bias=1.0, scale=-1.0))],
             ["fl", "fle", "l" + key], ["nf"])
-        tt(T.fo[:], T.fl[:, 0:CE].indirect(lst(key)), T.oo[:], MUL, ["fl", "fle", "l" + key, "oo"], ["fo"], gcost("v", C))
+        tt(T.fo[:], T.fl[:, 0:CE].indirect(lst(key)), T.oo[:], MUL, ["fl", "fle", "l" + key, "oo", "ootop"], ["fo"], gcost("v", C))
         vec(lambda e: e.tensor_tensor_scan(T.sb[:], T.nf[:], T.fo[:], 0.0, MUL, ADD), vcost(C, 0.5), ["nf", "fo"], ["sb"])
         pick(T.br, T.sb[:], lambda a, b: lst("poso", a, b), ["sb", "lposo"], "br", CUT["br"])
-        land(scan(T.br[:], C, both("br"), "ch"), lst("bo%d" % rd), "lbo%d" % rd)
-        mail("bo%d" % rd, "bp%d" % rd, "rb%d" % rd)
+        wrap(T.br, "br", lambda a, b: lst("bo%d" % rd, a, b), "lbo%d" % rd, CUT["br"] if TWO else 0)
+        mail("bo%d" % rd, "bp%d" % rd, "rb%d" % rd, 0.0)
+        calls[-1]["reads"].append("lbo%ds" % rd)
         take(T.r2[:], T.br[:].indirect(lst("ivp%d" % rd)), C, both("br") + ["livp%d" % rd], ["r2"])
         land(scan(T.r2[:], C, ["r2"], "ce"), lst("eo%d" % rd), "leo%d" % rd)
         mail("eo%d" % rd, "ep%d" % rd, "re%d" % rd)
-        for b in range(4):
-            tt(T.zt[:, b:4 * C:4], pl("tp", b).indirect(lst("bp%d" % rd)), pl("gv", b), ADD,
-               ["tp%d" % b, "gv%d" % b, "lbp%d" % rd], ["zt%d" % b], gcost("v", C))
-        quant("z", T.zt[:], ["zt%d" % b for b in range(4)])
-        for b in range(4):
-            mm(1 + b, "w", 128 * b, "z", ["wq", "wsc", "z"])
-            unload(pl("hh", b), bank(1 + b), C, ["b%d" % (1 + b)], ["hh%d" % b], "s" if b else "vs", 0.015625)
-            sooner(0.1 * (3 - b))
-        runs = ((0, C),) if rd < 2 else ((0, LAST), (LAST, C))
-        for c, d in runs:
+        def mean(to, runs, win, off, other, reads, q):
+            for i, (c, d) in enumerate(runs):
+                for b in range(4):
+                    tt(T[to][:, 4 * c + b:4 * d:4], pl(win, b).indirect(lst(off, c // 16, d // 16)), pl(other, b, c, d), ADD,
+                       reads(b) + ["%s%d" % (other, b), "l" + off], ["%s%d%d" % (to, b, i)], gcost("v", d - c))
+                    if i or b:
+                        behind()
+                    if i and not b:
+                        a, z = runs[i - 1]
+                        quant(q, T[to][:, 4 * a:4 * z], ["%s%d%d" % (to, k, i - 1) for k in range(4)], a, z, "%s.%d" % (q, i - 1))
+                        behind()
+            quant(q, T[to][:, 4 * c:4 * d], ["%s%d%d" % (to, k, i) for k in range(4)], c, d, q)
+
+        mean("zt", ZRUNS, "tp", "bp%d" % rd, "gv", lambda b: ["tp%d" % b], "z")
+        for i, (c, d) in enumerate(ZRUNS):
+            end = i + 1 == len(ZRUNS)
             for b in range(4):
-                tt(T.xt[:, 4 * c + b:4 * d:4], pl("hh", b).indirect(lst("ep%d" % rd, c // 16, d // 16)), pl("tu", b, c, d), ADD,
-                   ["hh%d" % b, "tu%d" % b, "lep%d" % rd], ["xt%d%d" % (b, c)], gcost("v", d - c))
-            quant("x%d" % (rd + 1), T.xt[:, 4 * c:4 * d], ["xt%d%d" % (b, c) for b in range(4)], c, d, "x%d" % (rd + 1 + c))
+                k = (1 + b + 4 * i) % 8
+                mm(k, "w", 128 * b, "z", ["wq", "wsc", "z" if end else "z.%d" % i], c, d)
+                unload(pl("hh", b, c, d), bank(k, d - c), d - c, ["b%d" % k], ["hh%d%d" % (b, i)], "vs" if end and not b else "s", 0.015625)
+                sooner(0.1 * (3 - b))
+        runs = ((0, C),) if rd < 2 else RUNS
+        mean("xt", runs, "hh", "ep%d" % rd, "tu", lambda b: ["hh%d%d" % (b, i) for i in range(len(ZRUNS))], "x%d" % (rd + 1))
 
     add([("s", gcost("s", C), lambda e: e.activation(T.uof[:], IOTA.indirect(lst("udo")), COPY, bias=float(MID)))], ["iota", "ludo"], ["uof"])
     dma("y", T.uo[:], T.uof[0:128:16, :], ["uof"], [], LOAD)
     for i, (c, d) in enumerate(runs):
-        x = "x%d" % (3 + c)
+        x = "x3" if i else "x3.0"
         mm(5 + i, "v", 0, "x3", ["v", x], c, d)
         unload(T.yf[:, c:d], bank(5 + i, d - c), d - c, ["b%d" % (5 + i)], ["yf%d" % i], "vs" if i else "s")
         dma("y", T.oc[:, 4 * c:4 * d], u8(T.x3q[:, c:d]), [x], [], LOAD + 1.5 - i)
         dma("s" if i else "y", T.y[:, c:d], T.yf[:, c:d], ["yf%d" % i], [], LOAD + 1.5 - i)
     for k in range(4):
-        dma("y", T.osc[4 * k:4 * k + 4, :], T.x3sc[32 * k:32 * k + 4, :], ["x3", "x%d" % (3 + LAST)], [], LOAD)
+        dma("y", T.osc[4 * k:4 * k + 4, :], T.x3sc[32 * k:32 * k + 4, :], ["x3", "x3.0"], [], LOAD)
 
     order = arrange(calls)
     order = [c for c in calls if c["kind"] == "load"] + [c for c in order if c["kind"] != "load"]

@@ -7,14 +7,18 @@ BIG = 512.0
 EVEN, ODD, ODD2 = C, C + 1, C + 3
 CE = C + 4
 RUNS = ((0, 160), (160, C))
-ZRUNS = ((0, C),)
+LASTWHOLE, SPLIT = 0, True
+LOW, UP = 128, 224
+ZONES, HALVES = ((UP, C), (LOW, UP), (0, LOW)), ((LOW, C), (0, LOW))
+FILL = (("h8", 256, 272, 272), ("h8", 240, 256, 256), ("h8", UP, 240, 240), ("hx", 192, UP, UP), ("hx", 160, 192, 192),
+        ("hx", LOW, 160, 160), ("hy", 64, LOW, LOW), ("hy", 0, 64, 64))
 
 CYCLE, GATHER, DONE, SLACK = 0.001, 1.5, 0.12, 0.03
-HOP, SPARE, CODES, LOAD = 2.5, 1.0, 5.5, 2.0
+HOP, SPARE, CODES, LOAD = 2.3, 1.0, 5.5, 2.0
 LEADI, LEADU, LEADR, LEADP = 3.0, 1.0, 1.0, 8.0
 PLACE = "sv"
 TWO0, TWO, PASSES = False, True, 4
-MOVES, MARGIN = 40000, 0.1
+MOVES, MARGIN = 250000, 0.25
 ARRANGED = {}
 CUT = {"ring0": 0, "ring": 0, "mates": 8, "h0": 6, "h": 10, "br": 10}
 
@@ -29,9 +33,11 @@ for _n, _w in (("x0", C), ("x1", C), ("x2", C), ("x3", C), ("p0", C), ("p1", C),
     SCRATCH[_n + "q"] = ("sbuf", [128, _w], "float8_e4m3fn_x4")
     SCRATCH[_n + "sc"] = ("sbuf", [128, _w], "uint8")
 SCRATCH["ramp"] = ("sbuf", [128, 16 + 304], "bfloat16")
-for _n in ("h1", "h2", "h4", "h8", "fl"):
+for _n in ("h1", "h2", "h4", "h8", "hx"):
     SCRATCH[_n] = ("sbuf", [128, 304], "bfloat16")
-for _n in ("patf", "pp", "r1", "r2", "r3", "hx", "nf", "fo", "sb", "br", "uda", "mtr", "mr", "um", "oo"):
+SCRATCH["fl"] = ("sbuf", [128, C + 48], "bfloat16")
+SCRATCH["hy"] = ("sbuf", [128, LOW], "bfloat16")
+for _n in ("patf", "pp", "r1", "r2", "r3", "nf", "fo", "sb", "br", "uda", "mtr", "mr", "um", "oo"):
     SCRATCH[_n] = ("sbuf", [128, C], "bfloat16")
 SCRATCH["pat"] = ("sbuf", [128, C + 64], "bfloat16")
 SCRATCH["hpr"] = ("sbuf", [128, 2 * C + 64], "bfloat16")
@@ -40,7 +46,7 @@ SCRATCH["d0"] = ("sbuf", [128, 2 * C], "bfloat16")
 SCRATCH["d1"] = ("sbuf", [128, 2 * C], "float16")
 SCRATCH["dd"] = ("sbuf", [128, C], "float32")
 SCRATCH["wide"] = ("sbuf", [128, 2 * CE], "float32")
-SCANS = ("ch", "co", "cm", "cg", "ce", "cp", "c3", "cw0", "cw1", "cw2", "cr")
+SCANS = ("ch", "co", "cm", "cg", "ce", "cp", "c3", "cw0", "cw1", "cw2", "cx", "cy", "cr")
 SCRATCH["cc"] = ("sbuf", [128, len(SCANS) * C + 64], "float16")
 for _n in ("pa", "pb"):
     SCRATCH[_n] = ("sbuf", [128, 32], "bfloat16")
@@ -48,16 +54,16 @@ for _n in ("ivl", "mtl", "udl", "hpl"):
     SCRATCH[_n] = ("sbuf", [128, KW], "int32")
 SCRATCH["i32"] = ("sbuf", [128, 32], "int32")
 SCRATCH["qi"] = ("sbuf", [128, 2], "int32")
-SCRATCH["col"] = ("sbuf", [128, 8], "float32")
+SCRATCH["col"] = ("sbuf", [128, 16], "float32")
 SMALL = ("k16", "kb", "jw", "ivf", "mif", "di", "ga", "gb", "ta", "tb", "na", "nb", "e0", "df", "sg", "bi", "ti", "fb",
          "udf", "umf", "du", "t3", "bj", "tj")
 SCRATCH["sm"] = ("sbuf", [128, len(SMALL) * 20], "float32")
-LOCAL = ("iv0", "mi", "mto", "udo", "wo", "poso", "fa", "fb", "foff", "ordo", "go")
+LOCAL = ("iv0", "mi", "mto", "udo", "wo", "poso", "fa", "fb", "foff", "hx", "hy", "ordo")
 SCRATCH["lloc"] = ("sbuf", [128, len(LOCAL) * 24], "uint16")
 for _n in ("iv1", "iv2", "iv3", "bo0", "bo1", "bo2", "eo0", "eo1", "eo2",
            "ivp0", "ivp1", "ivp2", "bp0", "bp1", "bp2", "ep0", "ep1", "ep2"):
     SCRATCH["l" + _n] = ("sbuf", [128, KW], "uint16")
-SCRATCH["lhoff"] = ("sbuf", [128, 4 * KW], "uint16")
+SCRATCH["lhoff"] = ("sbuf", [128, 5 * KW], "uint16")
 SCRATCH["lhp"] = ("sbuf", [128, 2 * KW + 4], "uint16")
 SCRATCH["luo"] = ("sbuf", [128, 8], "uint16")
 SCRATCH["uoi"] = ("sbuf", [128, 8], "int32")
@@ -136,25 +142,26 @@ def shorten(calls, order, queue):
 
     ends = [i for i in range(n) if not calls[i]["before"]]
 
-    def run(order, queue, bound):
-        end, cause, free, last = [0.0] * n, [-1] * n, {}, {}
-        for i in order:
+    def run(order, queue, bound, same, end, cause):
+        end, cause, last = end + [], cause + [], {queue[i]: i for i in order[:same]}
+        for i in order[same:]:
             q = queue[i]
-            t, c = free.get(q, 0.0), last.get(q, -1)
+            c = last.get(q, n)
+            t = end[c]
             for a, gap in after[i]:
                 if end[a] + gap > t:
                     t, c = end[a] + gap, a
-            cause[i], last[q] = c, i
-            end[i] = free[q] = t + cost[i][q]
+            cause[i], last[q], end[i] = c, i, t + cost[i][q]
         long, i = max((end[i] + calls[i]["late"], i) for i in ends)
         if long > bound:
             return None
         held = []
-        while cause[i] >= 0:
+        while cause[i] < n:
             if cause[i] not in calls[i]["after"]:
                 held.append((cause[i], i))
             i = cause[i]
-        return long, held, sorted(order, key=lambda i: end[i] - cost[i][queue[i]]), queue
+        order = sorted(order, key=lambda i: end[i] - cost[i][queue[i]])
+        return long, held, order, queue, {i: k for k, i in enumerate(order)}, end, cause
 
     seed = [1]
 
@@ -162,29 +169,32 @@ def shorten(calls, order, queue):
         seed[0] = (seed[0] * 1103515245 + 12345) % 2 ** 31
         return (seed[0] >> 8) % k
 
-    now = best = run(order, queue, 1e9)
+    now = best = run(order, queue, 1e9, 0, [0.0] * (n + 1), [n] * n)
     for step in range(MOVES):
-        c, i = now[1][some(len(now[1]))]
-        order, queue, kind = list(now[2]), now[3], some(7)
+        long, held, order, queue, at = now[:5]
+        c, i = held[some(len(held))]
+        kind = some(7)
         if kind == 0:
             x = (c, i)[some(2)]
-            queue = list(queue)
-            queue[x] = [q for q in cost[x] if q != queue[x] or len(cost[x]) == 1][0]
+            if len(cost[x]) == 1:
+                continue
+            same, queue = at[x], list(queue)
+            queue[x] = [q for q in cost[x] if q != queue[x]][0]
         elif kind < 4:
-            a, b = order.index(i), min([order.index(k) for k in calls[c]["before"]], default=n)
+            a, b = at[i], min([at[k] for k in calls[c]["before"]], default=n)
             if b <= a:
                 continue
-            order.remove(c)
-            order.insert(a + some(b - a) * some(2), c)
+            same, to = at[c], a + some(b - a) * some(2)
+            order = order[:same] + order[same + 1:to + 1] + [c] + order[to + 1:]
         else:
-            a, b = max([order.index(k) for k in calls[i]["after"]], default=-1), order.index(c)
+            a, b = max([at[k] for k in calls[i]["after"]], default=-1), at[c]
             if b <= a:
                 continue
-            order.remove(i)
-            order.insert(b - some(b - a) * some(2), i)
-        now = run(order, queue, now[0] + MARGIN * (1 - step / MOVES) * some(100) / 100) or now
+            same = b - some(b - a) * some(2)
+            order = order[:same] + [i] + order[same:at[i]] + order[at[i] + 1:]
+        now = run(order, queue, long + MARGIN * (1 - step / MOVES) * some(100) / 100, same, now[5], now[6]) or now
         best = min(best, now, key=lambda r: r[0])
-    return best[2:]
+    return best[2:4]
 
 
 def rank_program(g, core, T, topo):
@@ -283,7 +293,7 @@ def rank_program(g, core, T, topo):
             way = {"v": lambda e: e.tensor_copy(out, in_), "s": lambda e: e.activation(out, in_, COPY)}
         else:
             way = {"v": lambda e: e.tensor_scalar(out, in_, scale, None, MUL), "s": lambda e: e.activation(out, in_, COPY, scale=scale)}
-        add([(q, n * CYCLE + (0.065 if q == "s" else 0), way[q]) for q in qs], reads, writes)
+        add([(q, n * CYCLE + 0.065 if q == "s" else vcost(n, 1), way[q]) for q in qs], reads, writes)
 
     def fill(ap, c, writes, n=64):
         vec(lambda e: e.memset(ap, c), vcost(n, 0.5), [], writes)
@@ -311,9 +321,9 @@ def rank_program(g, core, T, topo):
             return T.lloc[:, o + a:o + b]
         return T["l" + name][:, a:b]
 
-    def sm(name):
+    def sm(name, a=0, b=KW):
         o = 20 * SMALL.index(name)
-        return T.sm[:, o:o + KW]
+        return T.sm[:, o + a:o + b]
 
     def small(out, a, b, o):
         tt(sm(out), sm(a), sm(b), o, [a, b], [out])
@@ -333,7 +343,14 @@ def rank_program(g, core, T, topo):
             [key or b])
         return key or b, T.cc[:, o + 15:o + n:16]
 
-    Q0, QZ, CORR, CORR2, THR, QP = [T.col[:, i:i + 1] for i in range(6)]
+    Q0, QZ, CORR, THR, QP = [T.col[:, i:i + 1] for i in range(5)]
+
+    def zoned(key, c, d):
+        return ["%s.%d" % (key, a) for a, b in ZONES if a < d and c < b]
+
+    def base(c, half):
+        k = 8 + 2 * [a for a, b in ZONES].index(c) + half
+        return T.col[:, k:k + 1]
 
     def land(job, out, key):
         ts(out, job[1], CORR, ADD, [job[0], "corr"], [key])
@@ -361,7 +378,7 @@ def rank_program(g, core, T, topo):
     fill(T.d0[:, 0:2 * C:2], 0.0, ["d0e"], C)
     fill(T.win[:, 2 * C:2 * CE], float(EVEN - MID), ["wine"])
     fill(T.win[:, 2 * EVEN + 1:2 * EVEN + 2], float(ODD - MID), ["wine"])
-    fill(T.fl[:, C:CE], 0.0, ["fle"])
+    fill(T.fl[:, C:C + 48], 0.0, ["fle"])
     fill(T.fl[:, EVEN:EVEN + 1], 1.0, ["fle"])
     fill(T.ramp[:, 15:16], float(C - 1 - MID), ["iom"])
     pool(lambda e: e.iota(T.i32[:], [[1, 32]], 1024, -1), 32, [], ["i32"])
@@ -371,9 +388,12 @@ def rank_program(g, core, T, topo):
     count(T.wide[:], [[1, 2 * CE]], -CE, 2 * CE, ["wide"])
     count(sm("k16"), [[16, KW]], 0, KW, ["k16"])
     pool(lambda e: e.iota(T.uoi[:], [[16, 8]], 0, 0), 8, [], ["uoi"])
-    count(sm("kb"), [[-32, KW // 2], [0, 2]], -32, KW, ["kb"])
+    count(sm("kb", 0, 8), [[-64, 2], [0, 4]], -64, 8, ["kb0"])
+    count(sm("kb", 8, 14), [[-32, 3], [0, 2]], -160, 6, ["kb1"])
+    count(sm("kb", 14, KW), [[-16, 4]], -240, 4, ["kb2"])
     for b in ("h1", "h2", "h4", "h8"):
         count(T[b][:, C:CE], [[1, 4]], C - MID, 4, [b + "e"])
+    count(T.hx[:, UP:CE], [[1, CE - UP]], UP - MID, CE - UP, ["hxe"])
     ts(QP, T.qi[:, 0:1], float(MID), SUB, ["qi"], ["qp"])
     ts(T.et[:, 3:515:4], IOTA[:, 0:128], QP, EQ, ["iota", "qp", "et"], ["et"], 0.5, MUL)
     ts(T.qi[:], T.qi[:], 15, AND, ["qi"], ["qi"])
@@ -388,56 +408,59 @@ def rank_program(g, core, T, topo):
     cp(T.pat[:, 128:256], T.pat[:, 0:128], ["pat0", "pat32", "pat64", "pat96"], ["pat128"])
     cp(T.pat[:, 256:352], T.pat[:, 0:96], ["pat0", "pat32", "pat64", "pat128"], ["pat"])
     ts(CORR, QZ, 2 * BIG, MUL, ["qz"], ["corr"], MID - BIG, ADD)
-    ts(CORR2, QZ, 2 * BIG, MUL, ["qz"], ["corr2"], MID - BIG + 0.5, ADD)
+    for c, d in ZONES:
+        for half in range(2):
+            ts(base(c, half), QZ, 2 * BIG, MUL, ["qz"], ["base%d%d" % (c, half)], MID - BIG - c + half / 2, ADD)
     ts(THR, QZ, -4 * BIG, MUL, ["qz"], ["thr"], 1.5 + 2 * BIG, ADD)
     unload(T.patf[:], T.pat[:, 0:C], C, ["pat"], ["patf"], "s")
     sooner(LEADP)
-    tt(T.patf[:, 15:C:16], T.pat[:, 15:C:16], sm("kb"), ADD, ["pat", "kb", "patf"], ["patf"])
+    tt(T.patf[:, 15:C:16], T.pat[:, 15:C:16], sm("kb"), ADD, ["pat", "kb0", "kb1", "kb2", "patf"], ["patf"])
     ts(sm("jw"), sm("k16"), Q0, ADD, ["k16", "q0"], ["jw"])
     for b in range(4):
         quant("e", T.et[:, 3 - b:515 - b], ["et"], 128 * b, 128 * b + 128, "e%d" % b)
 
-    TOP = C + 32
+    TOP, END = C + 32, C + 64
 
     def hrow(k):
-        return T.hpr[:, TOP + 32:TOP + 32 + C] if k % 2 else T.hpr[:, 0:C]
+        return T.hpr[:, END:END + C] if k else T.hpr[:, 0:C]
 
     def hoff(k):
-        return lambda a, b: T.lhp[:, (k % 2) * (TOP + 32) // 16 + a:(k % 2) * (TOP + 32) // 16 + b]
+        return lambda a, b: T.lhp[:, k * END // 16 + a:k * END // 16 + b]
 
-    top = T.lhp[:, TOP // 16:TOP // 16 + 2]
-    fill(top, C - 1, ["ltop"])
+    def power(k, off, cut):
+        pick(hrow(k), hrow(1 - k), hoff(off), both("hpr%d" % (1 - k)) + ["lhp%d" % off], "hpr%d" % k, cut)
+
+    def known(k):
+        s0, s1 = (TOP, END + C) if k else (0, END)
+        land(scan(T.hpr[:, s0:s1], s1 - s0, both("hpr%d" % k) + ["top", "top1", "top2"], "cr"), T.lhp[:, s0 // 16:s1 // 16], "ltop")
+        calls[-1]["writes"].append("lhp%d" % k)
+
+    def places(row, off, keys, s0, s1, k0):
+        take(T.oo[:, s0:s1], hrow(row).indirect(off), s1 - s0, both("hpr%d" % row) + keys, ["oo"], PLACE)
+        land(scan(T.oo[:, k0:s1], s1 - k0, ["oo"], "co"), lst("ordo", k0 // 16, s1 // 16), "lordo")
+        cp(T.r1[:].indirect(lst("ordo", k0 // 16, k0 // 16 + 6)), T.ramp[:, 15 + k0:15 + k0 + 96], ["iota", "iom", "lordo", "lordt"], ["r1"],
+           0.05 + 3.5 * 96 * CYCLE)
+
     fill(T.hpr[:, C:TOP], 0.0, ["top"])
     cp(hoff(0)(0, KW), T.hpl[:], ["hpl"], ["lhp0"])
     pick(hrow(0), IOTA, hoff(0), ["iota", "lhp0"], "hpr0", CUT["ring0"])
-    for k in range(9):
-        here, there = both("hpr%d" % (min(k, 7) % 2)), "hpr%d" % ((k + 1) % 2)
-        if k < 7:
-            pick(hrow(k + 1), hrow(k), hoff(k), here + ["lhp%d" % (k % 2)], there, CUT["ring0" if k < 2 else "ring"])
-        if k == 0:
-            take(T.hpr[:, TOP:TOP + 32], hrow(0).indirect(top), 32, here + ["ltop"], ["top"], PLACE)
-            take(T.hpr[:, TOP - 1:TOP + 31], hrow(1).indirect(top), 32, both(there) + ["ltop"], ["top"], PLACE)
-        elif k < 5:
-            take(T.hpr[:, TOP - (1 << k):TOP + 32 - (1 << k)], hrow(k).indirect(top), 32, here + ["ltop"], ["top"], PLACE)
-        if k < 5:
-            s0, s1 = (0, TOP + 32) if k % 2 else (TOP, TOP + 32 + C)
-            land(scan(T.hpr[:, s0:s1], s1 - s0, both(there) + ["top"], "cr"), T.lhp[:, s0 // 16:s1 // 16], "ltop")
-            calls[-1]["writes"].append("lhp%d" % ((k + 1) % 2))
-            continue
-        if k == 5:
-            cp(lst("ordo", 16, 18), top, ["ltop"], ["lordo"])
-            cp(T.oo[:, 256:C], T.hpr[:, TOP:TOP + 32], ["top"], ["ootop"])
-            land(scan(hrow(6), C, both(there), "cr"), hoff(6)(0, KW), "lhp0")
-        a, b = {5: (16, 18), 6: (14, 18), 7: (10, 18), 8: (8, 10)}[k]
-        s0 = 16 * a - (1 << min(k, 7))
-        s1 = s0 + 16 * (b - a)
-        take(T.oo[:, s0:s1], hrow(min(k, 7)).indirect(top if k == 5 else lst("ordo", a, b)), s1 - s0,
-             here + ["ltop" if k == 5 else "lordo"], ["oo"], PLACE)
-        land(scan(T.oo[:, s0:s1], s1 - s0, ["oo"], "co"), lst("ordo", s0 // 16, s1 // 16), "lordo")
-        if k >= 6:
-            s1 = C if k == 6 else s1
-            cp(T.r1[:].indirect(lst("ordo", s0 // 16, s1 // 16)), T.ramp[:, 15 + s0:15 + s1], ["iota", "iom", "lordo"], ["r1"],
-               0.05 + 3.5 * (s1 - s0) * CYCLE)
+    unload(T.hpr[:, END - 1:END], T.hpr[:, C - 1:C], 1, both("hpr0"), ["top1"])
+    power(1, 0, CUT["ring0"])
+    unload(T.hpr[:, END - 2:END - 1], T.hpr[:, END + C - 1:END + C], 1, both("hpr1"), ["top2"])
+    take(T.hpr[:, TOP - 2:END - 2], hrow(1).indirect(hoff(0)(KW - 2, KW)), 32, both("hpr1") + ["lhp0"], ["top"], PLACE)
+    power(0, 0, CUT["ring0"])
+    known(0)
+    for k, n in enumerate((3, 6, 12, 24)):
+        power(1 - k % 2, k % 2, CUT["ring"])
+        take(T.hpr[:, TOP - n:END - n], hrow(k % 2).indirect(T.lhp[:, TOP // 16:END // 16]), 32, both("hpr%d" % (k % 2)) + ["ltop"],
+             ["top"], PLACE)
+        known(1 - k % 2)
+    power(1, 0, CUT["ring"])
+    cp(lst("ordo", 15, KW), T.lhp[:, TOP // 16 - 1:END // 16], ["ltop"], ["lordt"])
+    cp(T.oo[:, 240:C], T.hpr[:, TOP - 16:END], ["top"], ["ootop"])
+    places(0, T.lhp[:, C // 16:END // 16], ["ltop"], 176, 240, 192)
+    places(1, lst("ordo", 12, KW), ["lordo", "lordt"], 96, 192, 96)
+    places(1, lst("ordo", 6, 12), ["lordo"], 0, 96, 0)
     land(scan(T.r1[:], C, ["r1"], "cg"), lst("poso"), "lposo")
     sooner(LEADR)
 
@@ -454,7 +477,7 @@ def rank_program(g, core, T, topo):
         ts(sm("t" + n), sm(f), float(end), SUB, [f], ["t" + n])
         small("n" + n, "g" + n, "t" + n, MUL)
     ts(lst("fa"), sm("na"), float(ODD), ADD, ["na"], ["lfa"])
-    take(T.win[:, 1:2 * C:2], IOTA.indirect(lst("fa")), C, ["iota", "lfa"], ["win"], "s")
+    take(T.win[:, 1:2 * C:2], IOTA.indirect(lst("fa")), C, ["iota", "lfa"], zoned("win", 0, C), "s")
     small("fb", "nb", "na", SUB)
     ts(lst("fb"), sm("fb"), float(ODD2 - ODD + CE), ADD, ["fb"], ["lfb"])
     ts(sm("df"), sm("fb"), float(ODD2 - ODD), ADD, ["fb"], ["df"])
@@ -472,7 +495,8 @@ def rank_program(g, core, T, topo):
     cp(T.urq[:, 0:128].bitcast(dt.uint32), T.uq[:, 0:128].bitcast(dt.uint32).indirect(T.luo[:, 0:8]), ["u", "luo"], ["urq"], gcost("v", 128))
     take(T.ursc[:, 0:128], T.usc[:, 0:128].indirect(T.luo[:, 0:8]), 128, ["u", "luo"], ["ursc"], "s")
     quant("v", T.vt[:], ["vt"], 0, 128)
-    quant("x0", T.xin[:], ["xin"])
+    for i, (c, d) in enumerate(RUNS):
+        quant("x0", T.xin[:, 4 * c:4 * d], ["xin"], c, d, both("x0")[i])
 
     for rd, step in enumerate(STEP):
         x, p = "x%d" % rd, "p%d" % rd
@@ -488,31 +512,33 @@ def rank_program(g, core, T, topo):
         else:
             parts = [(dst, u8(T[p + "q"][:]), u8(T[x + "q"][:])), (dst, T[p + "sc"][:], T[x + "sc"][:])]
         nx = 2 * width(back[0], core) + width(back[1], core) if back else 2 * width(dst, core)
-        send(parts, [x], p, "rx%d" % rd, nx, CODES + (hops - 1) * HOP)
+        send(parts, both(x), p, "rx%d" % rd, nx, CODES + (hops - 1) * HOP)
 
         def mail(name, to, sem, spare=SPARE):
             send([(rel[1] if rel else dst, lst(to), lst(name))], ["l" + name], "l" + to, sem, width(back[1] if back else dst, core),
                  hops * HOP - 0.4 + spare)
 
-        cp(T.d1[:, 1:2 * C:2], T.win[:, 1:2 * C:2], ["win"], ["d1a"], vcost(C, 0.5))
+        cp(T.d1[:, 1:2 * C:2], T.win[:, 1:2 * C:2], zoned("win", 0, C), ["d1a"], vcost(C, 0.5))
         take(T.dd[:], T.wide[:].indirect(lst("fb")), C, ["wide", "lfb"], ["dd"], "s" if first else "sv")
-        mm(0, "ur", 0, x, ["urq", "ursc", x], 0, HALF)
-        mm(5, "ur", 0, x, ["urq", "ursc", x], HALF, C)
-        ts(T.pp[:, 0:HALF], bank(0, HALF), 0.0, GT, ["b0"], ["pp"], cost=vcost(HALF, 1))
-        ts(T.pp[:, HALF:C], bank(5, HALF), 0.0, GT, ["b5"], ["pps"], cost=vcost(HALF, 1))
-        take(T.d0[:, 1:2 * C:2], T.pp[:].indirect(lst("iv%d" % rd)), C, both("pp") + ["liv%d" % rd, "d0e"], ["d0"], "s")
-        tt(T.d1[:, 0:2 * C:2], T.pp[:].indirect(lst("mi")), T.dd[:], MUL, both("pp") + ["lmi", "dd"], ["d1"], gcost("v", C))
-        vec(lambda e: e.tensor_tensor_scan(T.win[:, 0:2 * C], T.d0[:], T.d1[:], 0.0, MUL, ADD), vcost(2 * C, 0.5),
-            ["d0", "d0e", "d1", "d1a"], ["win"])
-        cut = CUT["h0" if first else "h"]
-        two = cut if (TWO0 if first else TWO) else 0
+        for i, (c, d) in enumerate(RUNS):
+            mm(5 * i, "ur", 0, x, ["urq", "ursc", both(x)[i]], c, d)
+            ts(T.pp[:, c:d], bank(5 * i, d - c), 0.0, GT, ["b%d" % (5 * i)], [both("pp")[i]], cost=vcost(d - c, 1))
+        apart = TWO0 if first else TWO
+        takes, scans = (ZONES, ZONES) if apart else (HALVES, ((0, C),))
         cw = "cw%d" % rd
-        for a, b, keys in ((two, KW, both(cw)[two > 0:]), (0, two, [cw]))[:2 if two else 1]:
-            job = scan(T.win[:, 32 * a + 1:32 * b:2], 16 * (b - a), ["win"], cw, "pat", 16 * a, keys[-1])
-            calls[-1]["writes"] = keys
-            ts(lst("wo", a, b), job[1], CORR2, ADD, keys + ["corr2"], ["lwo" + k[3:] for k in keys], 2.0, MUL)
+        for c, d in HALVES if apart else ((0, C),):
+            take(T.d0[:, 2 * c + 1:2 * d:2], T.pp[:].indirect(lst("iv%d" % rd, c // 16, d // 16)), d - c,
+                 both("pp") + ["liv%d" % rd, "d0e"], zoned("d0", c, d), "s")
+            tt(T.d1[:, 2 * c:2 * d:2], T.pp[:].indirect(lst("mi", c // 16, d // 16)), T.dd[:, c:d], MUL, both("pp") + ["lmi", "dd"],
+               zoned("d1", c, d), gcost("v", d - c))
+            vec(lambda e, c=c, d=d: e.tensor_tensor_scan(T.win[:, 2 * c:2 * d], T.d0[:, 2 * c:2 * d], T.d1[:, 2 * c:2 * d], 0.0, MUL, ADD),
+                vcost(2 * (d - c), 0.5), zoned("d0", c, d) + zoned("d1", c, d) + ["d0e", "d1a"], zoned("win", c, d))
+        for c, d in scans:
+            job = scan(T.win[:, 2 * c + 1:2 * d:2], d - c, zoned("win", c, d), cw, "pat", c)
+            calls[-1]["writes"] = zoned(cw, c, d)
+            ts(lst("wo", c // 16, d // 16), job[1], base(c, 1), ADD, zoned(cw, c, d) + ["base%d1" % c], zoned("lwo", c, d), 2.0, MUL)
         old = (["e0"], sm("e0")) if first else last
-        last = (both(cw), T.cc[:, C * SCANS.index(cw) + 15:C * (SCANS.index(cw) + 1):16])
+        last = (zoned(cw, 0, C), T.cc[:, C * SCANS.index(cw) + 15:C * (SCANS.index(cw) + 1):16])
         tt(sm("bi"), last[1], old[1], NE, last[0] + old[0], ["bi"])
         small("ti", "bi", "di", MUL)
         small("ivf", "ivf", "ti", ADD)
@@ -539,33 +565,42 @@ def rank_program(g, core, T, topo):
             small("umf", "umf", "tj", SUB)
             small("du", "umf", "udf", SUB)
         for b in range(4):
-            mm(1 + b, "e", 128 * b, x, ["e%d" % b, x])
+            mm(1 + b, "e", 128 * b, x, ["e%d" % b] + both(x))
             unload(pl("th", b), bank(1 + b), C, ["b%d" % (1 + b)], ["th%d" % b])
             take(pl("tu", b), pl("th", b).indirect(lst("udo")), C, ["th%d" % b, "ludo"], ["tu%d" % b])
         for b in range(4):
             k = (5, 6, 7, 0)[b]
             mm(k, "e", 128 * b, p, ["e%d" % b, p])
-            unload(pl("tp", b), bank(k), C, ["b%d" % k], ["tp%d" % b])
+            unload(pl("tp", b), bank(k), C, ["b%d" % k], both("tp%d" % b))
             take(pl("gv", b), pl("tp", b).indirect(lst("ivp%d" % rd)), C, ["tp%d" % b, "livp%d" % rd], ["gv%d" % b])
-        hs = ["h1", "h2", "h4", "h8", "hx"]
-        pick(T.h1, T.win[:, 0:2 * CE], lambda a, b: lst("wo", a, b), ["win", "wine"], "h1", cut, "lwo")
-        for i in range(4):
-            def off(a, b):
-                return T.lhoff[:, i * KW + a:i * KW + b]
-            wrap(T[hs[i]], hs[i], off, "lhoff%d" % i, two)
-            pick(T[hs[i + 1]], T[hs[i]][:, 0:CE], off, both(hs[i]) + [hs[i] + "e"], hs[i + 1], cut, "lhoff%d" % i)
-        wrap(T.hx, "hx", lambda a, b: lst("foff", a, b), "lfoff", two, "patf")
-        ts(T.fl[:, 256:C], T.hx[:, 256:C], float(EVEN - MID), EQ, both("hx"), ["fl"])
-        if not first:
-            take(T.r1[:], T.hx[:].indirect(lst("ordo")), C, both("hx") + ["lordo"], ["r1"], "s")
-            land(scan(T.r1[:], C, ["r1"], "cg"), lst("go"), "lgo")
-        for b in range(7, -1 if first else 0, -1):
-            take(T.fl[:, 32 * b:32 * b + 32], T.fl[:, 32 * b + 32:CE].indirect(lst("foff", 2 * b, 2 * b + 2)), 32,
-                 ["fl", "fle", both("lfoff")[2 * b >= two]], ["fl"], "vs")
-        key = "ordo" if first else "go"
-        add([("s", gcost("s", C), lambda e, key=key: e.activation(T.nf[:], T.fl[:, 0:CE].indirect(lst(key)), IDENT, bias=1.0, scale=-1.0))],
-            ["fl", "fle", "l" + key], ["nf"])
-        tt(T.fo[:], T.fl[:, 0:CE].indirect(lst(key)), T.oo[:], MUL, ["fl", "fle", "l" + key, "oo", "ootop"], ["fo"], gcost("v", C))
+        for c, d in takes:
+            a = c if apart else 0
+            take(T.h1[:, c:d], T.win[:, 2 * a:2 * CE].indirect(lst("wo", c // 16, d // 16)), d - c,
+                 zoned("win", a, C) + ["wine"] + zoned("lwo", c, d), zoned("h1", c, d), "sv" if first else "s" if c else "v")
+        for i, (row, to, end) in enumerate((("h1", "h2", C), ("h2", "h4", C), ("h4", "h8", C), ("h8", "hx", UP), ("hx", "hy", LOW))):
+            for c, d in scans:
+                d = min(d, end)
+                if c < d:
+                    job = scan(T[row][:, c:d], d - c, zoned(row, c, d), "ch", "pat", c)
+                    calls[-1]["writes"] = zoned("ch", c, d)
+                    ts(T.lhoff[:, i * KW + c // 16:i * KW + d // 16], job[1], base(c, 0), ADD, zoned("ch", c, d) + ["base%d0" % c],
+                       zoned("l" + to, c, d))
+            for c, d in takes:
+                a, d = c if apart else 0, min(d, end)
+                if c < d:
+                    take(T[to][:, c:d], T[row][:, a:CE].indirect(T.lhoff[:, i * KW + c // 16:i * KW + d // 16]), d - c,
+                         zoned(row, a, UP if row == "hx" else C) + [row + "e"] + zoned("l" + to, c, d), zoned(to, c, d),
+                         "sv" if first or to == "hy" else "s" if c else "v")
+        ts(T.fl[:, C - 16:C], T.h8[:, C - 16:C], float(EVEN - MID), EQ, zoned("h8", UP, C), ["fl"])
+        for row, c, d in (("h8", UP, C - 16), ("hx", LOW, UP), ("hy", 0, LOW)):
+            land(scan(T[row][:, c:d], d - c, zoned(row, c, d), "cy", "patf", c, "cy" + row), lst("foff", c // 16, d // 16), "lfoff" + row)
+        for row, c, d, e in FILL:
+            c = c // 32 * 32
+            take(T.fl[:, c:d], T.fl[:, e:e + 64 if e > UP else CE].indirect(lst("foff", c // 16, d // 16)), d - c,
+                 ["fl", "fle", "lfoff" + row], ["fl"], "vs")
+        add([("s", gcost("s", C), lambda e: e.activation(T.nf[:], T.fl[:, 0:C].indirect(lst("ordo")), IDENT, bias=1.0, scale=-1.0))],
+            ["fl", "lordo"], ["nf"])
+        tt(T.fo[:], T.fl[:, 0:C].indirect(lst("ordo")), T.oo[:], MUL, ["fl", "lordo", "oo", "ootop"], ["fo"], gcost("v", C))
         vec(lambda e: e.tensor_tensor_scan(T.sb[:], T.nf[:], T.fo[:], 0.0, MUL, ADD), vcost(C, 0.5), ["nf", "fo"], ["sb"])
         pick(T.br, T.sb[:], lambda a, b: lst("poso", a, b), ["sb", "lposo"], "br", CUT["br"])
         wrap(T.br, "br", lambda a, b: lst("bo%d" % rd, a, b), "lbo%d" % rd, CUT["br"] if TWO else 0)
@@ -574,40 +609,44 @@ def rank_program(g, core, T, topo):
         take(T.r2[:], T.br[:].indirect(lst("ivp%d" % rd)), C, both("br") + ["livp%d" % rd], ["r2"])
         land(scan(T.r2[:], C, ["r2"], "ce"), lst("eo%d" % rd), "leo%d" % rd)
         mail("eo%d" % rd, "ep%d" % rd, "re%d" % rd)
-        def mean(to, runs, win, off, other, reads, q):
-            for i, (c, d) in enumerate(runs):
-                for b in range(4):
-                    tt(T[to][:, 4 * c + b:4 * d:4], pl(win, b).indirect(lst(off, c // 16, d // 16)), pl(other, b, c, d), ADD,
-                       reads(b) + ["%s%d" % (other, b), "l" + off], ["%s%d%d" % (to, b, i)], gcost("v", d - c))
-                    if i or b:
-                        behind()
-                    if i and not b:
-                        a, z = runs[i - 1]
-                        quant(q, T[to][:, 4 * a:4 * z], ["%s%d%d" % (to, k, i - 1) for k in range(4)], a, z, "%s.%d" % (q, i - 1))
-                        behind()
-            quant(q, T[to][:, 4 * c:4 * d], ["%s%d%d" % (to, k, i) for k in range(4)], c, d, q)
+        def mean(to, whole, win, off, other, q):
+            def plane(b, c, d, keys):
+                tt(T[to][:, 4 * c + b:4 * d:4], pl(win, b).indirect(lst(off, c // 16, d // 16)), pl(other, b, c, d), ADD,
+                   both("%s%d" % (win, b)) + ["%s%d" % (other, b), "l" + off], keys, gcost("v", d - c))
 
-        mean("zt", ZRUNS, "tp", "bp%d" % rd, "gv", lambda b: ["tp%d" % b], "z")
-        for i, (c, d) in enumerate(ZRUNS):
-            end = i + 1 == len(ZRUNS)
-            for b in range(4):
-                k = (1 + b + 4 * i) % 8
-                mm(k, "w", 128 * b, "z", ["wq", "wsc", "z" if end else "z.%d" % i], c, d)
-                unload(pl("hh", b, c, d), bank(k, d - c), d - c, ["b%d" % k], ["hh%d%d" % (b, i)], "vs" if end and not b else "s", 0.015625)
-                sooner(0.1 * (3 - b))
-        runs = ((0, C),) if rd < 2 else RUNS
-        mean("xt", runs, "hh", "ep%d" % rd, "tu", lambda b: ["hh%d%d" % (b, i) for i in range(len(ZRUNS))], "x%d" % (rd + 1))
+            steps = [(b, None) for b in range(whole)] + [(b, i) for i in range(2) for b in list(range(whole, 4)) + [None]]
+            k = steps.index((None, 0))
+            steps[k:k + 2] = steps[k + 1], steps[k]
+            for n, (b, i) in enumerate(steps):
+                c, d = (0, C) if i is None else RUNS[i]
+                if b is None:
+                    quant(q, T[to][:, 4 * c:4 * d], [both("%s%d" % (to, a))[i] for a in range(4)], c, d, both(q)[i])
+                else:
+                    plane(b, c, d, both("%s%d" % (to, b)) if i is None else [both("%s%d" % (to, b))[i]])
+                if n:
+                    behind()
+
+        mean("zt", 3, "tp", "bp%d" % rd, "gv", "z")
+        for i, (c, d) in enumerate(RUNS):
+            mm(1 + 4 * i, "w", 0, "z", ["wq", "wsc", both("z")[i]], c, d)
+            unload(pl("hh", 0, c, d), bank(1 + 4 * i, d - c), d - c, ["b%d" % (1 + 4 * i)], [both("hh0")[i]], "vs", 0.015625)
+            sooner(0.3)
+        for b in range(1, 4):
+            mm(1 + b, "w", 128 * b, "z", ["wq", "wsc"] + both("z"))
+            unload(pl("hh", b), bank(1 + b), C, ["b%d" % (1 + b)], both("hh%d" % b), "s", 0.015625)
+            sooner(0.1 * (3 - b))
+        mean("xt", 3 if rd < 2 else LASTWHOLE, "hh", "ep%d" % rd, "tu", "x%d" % (rd + 1))
 
     add([("s", gcost("s", C), lambda e: e.activation(T.uof[:], IOTA.indirect(lst("udo")), COPY, bias=float(MID)))], ["iota", "ludo"], ["uof"])
     dma("y", T.uo[:], T.uof[0:128:16, :], ["uof"], [], LOAD)
-    for i, (c, d) in enumerate(runs):
-        x = "x3" if i else "x3.0"
+    for i, (c, d) in enumerate(RUNS):
+        x = both("x3")[i]
         mm(5 + i, "v", 0, "x3", ["v", x], c, d)
         unload(T.yf[:, c:d], bank(5 + i, d - c), d - c, ["b%d" % (5 + i)], ["yf%d" % i], "vs" if i else "s")
         dma("y", T.oc[:, 4 * c:4 * d], u8(T.x3q[:, c:d]), [x], [], LOAD + 1.5 - i)
         dma("s" if i else "y", T.y[:, c:d], T.yf[:, c:d], ["yf%d" % i], [], LOAD + 1.5 - i)
     for k in range(4):
-        dma("y", T.osc[4 * k:4 * k + 4, :], T.x3sc[32 * k:32 * k + 4, :], ["x3", "x3.0"], [], LOAD)
+        dma("ys"[k % 2], T.osc[4 * k:4 * k + 4, :], T.x3sc[32 * k:32 * k + 4, :], both("x3"), [], LOAD)
 
     order = arrange(calls)
     order = [c for c in calls if c["kind"] == "load"] + [c for c in order if c["kind"] != "load"]

@@ -10,15 +10,21 @@ RUNS = ((0, 160), (160, C))
 LASTWHOLE, SPLIT = 0, True
 LOW, UP = 128, 224
 ZONES, HALVES = ((UP, C), (LOW, UP), (0, LOW)), ((LOW, C), (0, LOW))
-FILL = (("h8", 256, 272, 272), ("h8", 240, 256, 256), ("h8", UP, 240, 240), ("hx", 192, UP, UP), ("hx", 160, 192, 192),
-        ("hx", LOW, 160, 160), ("hy", 64, LOW, LOW), ("hy", 0, 64, 64))
+FILL = ((UP, 256, 272, 272), (UP, 240, 256, 256), (UP, UP, 240, 240), (LOW, 192, UP, UP), (LOW, 160, 192, 192),
+        (LOW, LOW, 160, 160), (0, 64, LOW, LOW), (0, 0, 64, 64))
+PLAN = ((1, (2, 3, 4)), (4, (8, 12, 16)), (16, (32, 48, 64)))
+NEAR = (16, 32, 64)
+SKIP0, SKIP = False, True
+TAKES = ((UP, C, UP, "s"), (LOW, UP, LOW, "v"), (64, LOW, 0, "s"), (0, 64, 0, "v"))
+FIRST = HALVES
+WZ, WX = 3, 3
 
-CYCLE, GATHER, DONE, SLACK = 0.001, 1.5, 0.12, 0.03
+CYCLE, GATHER, DONE, SLACK = 0.001, 1.6, 0.2, 0.03
 HOP, SPARE, CODES, LOAD = 2.3, 1.0, 5.5, 2.0
 LEADI, LEADU, LEADR, LEADP = 3.0, 1.0, 1.0, 8.0
 PLACE = "sv"
-TWO0, TWO, PASSES = False, True, 4
-MOVES, MARGIN = 250000, 0.25
+TWO0, TWO = True, True
+MOVES, MARGIN = 200000, 0.3
 ARRANGED = {}
 CUT = {"ring0": 0, "ring": 0, "mates": 8, "h0": 6, "h": 10, "br": 10}
 
@@ -33,10 +39,9 @@ for _n, _w in (("x0", C), ("x1", C), ("x2", C), ("x3", C), ("p0", C), ("p1", C),
     SCRATCH[_n + "q"] = ("sbuf", [128, _w], "float8_e4m3fn_x4")
     SCRATCH[_n + "sc"] = ("sbuf", [128, _w], "uint8")
 SCRATCH["ramp"] = ("sbuf", [128, 16 + 304], "bfloat16")
-for _n in ("h1", "h2", "h4", "h8", "hx"):
-    SCRATCH[_n] = ("sbuf", [128, 304], "bfloat16")
+POWERS = [n for m, rows in PLAN for n in rows]
+SCRATCH["pw"] = ("sbuf", [128, 304 * len(POWERS)], "bfloat16")
 SCRATCH["fl"] = ("sbuf", [128, C + 48], "bfloat16")
-SCRATCH["hy"] = ("sbuf", [128, LOW], "bfloat16")
 for _n in ("patf", "pp", "r1", "r2", "r3", "nf", "fo", "sb", "br", "uda", "mtr", "mr", "um", "oo"):
     SCRATCH[_n] = ("sbuf", [128, C], "bfloat16")
 SCRATCH["pat"] = ("sbuf", [128, C + 64], "bfloat16")
@@ -58,12 +63,12 @@ SCRATCH["col"] = ("sbuf", [128, 16], "float32")
 SMALL = ("k16", "kb", "jw", "ivf", "mif", "di", "ga", "gb", "ta", "tb", "na", "nb", "e0", "df", "sg", "bi", "ti", "fb",
          "udf", "umf", "du", "t3", "bj", "tj")
 SCRATCH["sm"] = ("sbuf", [128, len(SMALL) * 20], "float32")
-LOCAL = ("iv0", "mi", "mto", "udo", "wo", "poso", "fa", "fb", "foff", "hx", "hy", "ordo")
+LOCAL = ("iv0", "mi", "mto", "udo", "wo", "poso", "fa", "fb", "foff", "ordo", "go")
 SCRATCH["lloc"] = ("sbuf", [128, len(LOCAL) * 24], "uint16")
 for _n in ("iv1", "iv2", "iv3", "bo0", "bo1", "bo2", "eo0", "eo1", "eo2",
            "ivp0", "ivp1", "ivp2", "bp0", "bp1", "bp2", "ep0", "ep1", "ep2"):
     SCRATCH["l" + _n] = ("sbuf", [128, KW], "uint16")
-SCRATCH["lhoff"] = ("sbuf", [128, 5 * KW], "uint16")
+SCRATCH["lhoff"] = ("sbuf", [128, len(PLAN) * KW], "uint16")
 SCRATCH["lhp"] = ("sbuf", [128, 2 * KW + 4], "uint16")
 SCRATCH["luo"] = ("sbuf", [128, 8], "uint16")
 SCRATCH["uoi"] = ("sbuf", [128, 8], "int32")
@@ -272,16 +277,16 @@ def rank_program(g, core, T, topo):
                 put(dst, out, in_, sem)
         add([("g", 0.4 * len(parts), call)], reads, [key], late, "send", (sem, n))
 
-    def tt(out, a, b, o, reads, writes, cost=0.064):
+    def tt(out, a, b, o, reads, writes, cost=64 * CYCLE):
         vec(lambda e: e.tensor_tensor(out, a, b, o), cost, reads, writes)
 
-    def ts(out, a, s1, o1, reads, writes, s2=None, o2=None, cost=0.064):
+    def ts(out, a, s1, o1, reads, writes, s2=None, o2=None, cost=64 * CYCLE):
         if o2 is None:
             vec(lambda e: e.tensor_scalar(out, a, s1, None, o1), cost, reads, writes)
         else:
             vec(lambda e: e.tensor_scalar(out, a, s1, s2, o1, o2), cost, reads, writes)
 
-    def cp(out, in_, reads, writes, cost=0.064):
+    def cp(out, in_, reads, writes, cost=64 * CYCLE):
         vec(lambda e: e.tensor_copy(out, in_), cost, reads, writes)
 
     def take(out, win, n, reads, writes, qs="sv"):
@@ -302,7 +307,7 @@ def rank_program(g, core, T, topo):
         pool(lambda e: e.iota(ap, pattern, base, 0, allow_small_or_imprecise_dtypes=True), n, reads, writes)
 
     def quant(name, tile, reads, a=0, b=C, key=None):
-        vec(lambda e: e.quantize_mx(T[name + "q"][:, a:b], T[name + "sc"][:, a:b], tile), 0.015 + 0.00105 * (b - a), reads, [key or name])
+        vec(lambda e: e.quantize_mx(T[name + "q"][:, a:b], T[name + "sc"][:, a:b], tile), (15 + 1.05 * (b - a)) * CYCLE, reads, [key or name])
 
     def mm(bank, l, a, r, reads, c=0, d=C):
         add([("t", 0.07 + 0.0006 * (d - c), lambda e: e.matmul_mx(
@@ -345,8 +350,15 @@ def rank_program(g, core, T, topo):
 
     Q0, QZ, CORR, THR, QP = [T.col[:, i:i + 1] for i in range(5)]
 
+    def row(n, c, d):
+        o = 304 * POWERS.index(n)
+        return T.pw[:, o + c:o + d]
+
+    def reach(n):
+        return C if n <= NEAR[0] else UP if n <= NEAR[1] else LOW
+
     def zoned(key, c, d):
-        return ["%s.%d" % (key, a) for a, b in ZONES if a < d and c < b]
+        return ["%s.%d" % (key, a) for a, b, z, q in TAKES if a < d and c < b]
 
     def base(c, half):
         k = 8 + 2 * [a for a, b in ZONES].index(c) + half
@@ -355,15 +367,9 @@ def rank_program(g, core, T, topo):
     def land(job, out, key):
         ts(out, job[1], CORR, ADD, [job[0], "corr"], [key])
 
-    def wrap(row, key, off, okey, k, pat="pat"):
-        if not k:
-            job = scan(row[:, 0:C], C, both(key), "ch", pat)
-            calls[-1]["writes"].append("chs")
-            land(job, off(0, KW), okey)
-            calls[-1]["writes"].append(okey + "s")
-            return
-        land(scan(row[:, 16 * k:C], C - 16 * k, [key + "s"], "ch", pat, 16 * k, "chs"), off(k, KW), okey + "s")
-        land(scan(row[:, 0:16 * k], 16 * k, [key], "ch", pat), off(0, k), okey)
+    def wrap(row, key, off, okey, k, b):
+        land(scan(row[:, 16 * k:C], C - 16 * k, [key + "s"], b, "pat", 16 * k, b + "s"), off(k, KW), okey + "s")
+        land(scan(row[:, 0:16 * k], 16 * k, [key], b), off(0, k), okey)
 
     IOTA = T.ramp[:, 16:16 + CE]
 
@@ -391,9 +397,11 @@ def rank_program(g, core, T, topo):
     count(sm("kb", 0, 8), [[-64, 2], [0, 4]], -64, 8, ["kb0"])
     count(sm("kb", 8, 14), [[-32, 3], [0, 2]], -160, 6, ["kb1"])
     count(sm("kb", 14, KW), [[-16, 4]], -240, 4, ["kb2"])
-    for b in ("h1", "h2", "h4", "h8"):
-        count(T[b][:, C:CE], [[1, 4]], C - MID, 4, [b + "e"])
-    count(T.hx[:, UP:CE], [[1, CE - UP]], UP - MID, CE - UP, ["hxe"])
+    for n in POWERS:
+        if n % 2:
+            count(row(n, C, CE), [[0, 2], [-1, 2]], ODD - MID, 4, ["h%de" % n])
+        else:
+            count(row(n, reach(n), CE), [[1, CE - reach(n)]], reach(n) - MID, CE - reach(n), ["h%de" % n])
     ts(QP, T.qi[:, 0:1], float(MID), SUB, ["qi"], ["qp"])
     ts(T.et[:, 3:515:4], IOTA[:, 0:128], QP, EQ, ["iota", "qp", "et"], ["et"], 0.5, MUL)
     ts(T.qi[:], T.qi[:], 15, AND, ["qi"], ["qi"])
@@ -524,9 +532,9 @@ def rank_program(g, core, T, topo):
             mm(5 * i, "ur", 0, x, ["urq", "ursc", both(x)[i]], c, d)
             ts(T.pp[:, c:d], bank(5 * i, d - c), 0.0, GT, ["b%d" % (5 * i)], [both("pp")[i]], cost=vcost(d - c, 1))
         apart = TWO0 if first else TWO
-        takes, scans = (ZONES, ZONES) if apart else (HALVES, ((0, C),))
+        takes, scans = (TAKES, ZONES) if apart else ([h + (0, "sv") for h in HALVES], ((0, C),))
         cw = "cw%d" % rd
-        for c, d in HALVES if apart else ((0, C),):
+        for c, d in FIRST if apart else ((0, C),):
             take(T.d0[:, 2 * c + 1:2 * d:2], T.pp[:].indirect(lst("iv%d" % rd, c // 16, d // 16)), d - c,
                  both("pp") + ["liv%d" % rd, "d0e"], zoned("d0", c, d), "s")
             tt(T.d1[:, 2 * c:2 * d:2], T.pp[:].indirect(lst("mi", c // 16, d // 16)), T.dd[:, c:d], MUL, both("pp") + ["lmi", "dd"],
@@ -538,7 +546,10 @@ def rank_program(g, core, T, topo):
             calls[-1]["writes"] = zoned(cw, c, d)
             ts(lst("wo", c // 16, d // 16), job[1], base(c, 1), ADD, zoned(cw, c, d) + ["base%d1" % c], zoned("lwo", c, d), 2.0, MUL)
         old = (["e0"], sm("e0")) if first else last
-        last = (zoned(cw, 0, C), T.cc[:, C * SCANS.index(cw) + 15:C * (SCANS.index(cw) + 1):16])
+        def led(c, d, cw=cw):
+            return T.cc[:, C * SCANS.index(cw) + c + 15:C * SCANS.index(cw) + d:16]
+
+        last = (zoned(cw, 0, C), led(0, C))
         tt(sm("bi"), last[1], old[1], NE, last[0] + old[0], ["bi"])
         small("ti", "bi", "di", MUL)
         small("ivf", "ivf", "ti", ADD)
@@ -573,37 +584,48 @@ def rank_program(g, core, T, topo):
             mm(k, "e", 128 * b, p, ["e%d" % b, p])
             unload(pl("tp", b), bank(k), C, ["b%d" % k], both("tp%d" % b))
             take(pl("gv", b), pl("tp", b).indirect(lst("ivp%d" % rd)), C, ["tp%d" % b, "livp%d" % rd], ["gv%d" % b])
-        for c, d in takes:
-            a = c if apart else 0
-            take(T.h1[:, c:d], T.win[:, 2 * a:2 * CE].indirect(lst("wo", c // 16, d // 16)), d - c,
-                 zoned("win", a, C) + ["wine"] + zoned("lwo", c, d), zoned("h1", c, d), "sv" if first else "s" if c else "v")
-        for i, (row, to, end) in enumerate((("h1", "h2", C), ("h2", "h4", C), ("h4", "h8", C), ("h8", "hx", UP), ("hx", "hy", LOW))):
+        for i, (m, rows) in enumerate(PLAN):
+            def off(c, d):
+                return T.lhoff[:, i * KW + c // 16:i * KW + d // 16]
+
             for c, d in scans:
-                d = min(d, end)
-                if c < d:
-                    job = scan(T[row][:, c:d], d - c, zoned(row, c, d), "ch", "pat", c)
+                d = min(d, reach(rows[0]))
+                if c < d and m > 1:
+                    job = scan(row(m, c, d), d - c, zoned("h%d" % m, c, d), "ch", "pat", c)
                     calls[-1]["writes"] = zoned("ch", c, d)
-                    ts(T.lhoff[:, i * KW + c // 16:i * KW + d // 16], job[1], base(c, 0), ADD, zoned("ch", c, d) + ["base%d0" % c],
-                       zoned("l" + to, c, d))
-            for c, d in takes:
-                a, d = c if apart else 0, min(d, end)
-                if c < d:
-                    take(T[to][:, c:d], T[row][:, a:CE].indirect(T.lhoff[:, i * KW + c // 16:i * KW + d // 16]), d - c,
-                         zoned(row, a, UP if row == "hx" else C) + [row + "e"] + zoned("l" + to, c, d), zoned(to, c, d),
-                         "sv" if first or to == "hy" else "s" if c else "v")
-        ts(T.fl[:, C - 16:C], T.h8[:, C - 16:C], float(EVEN - MID), EQ, zoned("h8", UP, C), ["fl"])
-        for row, c, d in (("h8", UP, C - 16), ("hx", LOW, UP), ("hy", 0, LOW)):
-            land(scan(T[row][:, c:d], d - c, zoned(row, c, d), "cy", "patf", c, "cy" + row), lst("foff", c // 16, d // 16), "lfoff" + row)
-        for row, c, d, e in FILL:
+                    ts(off(c, d), job[1], base(c, 0), ADD, zoned("ch", c, d) + ["base%d0" % c], zoned("lh%d" % m, c, d))
+                elif c < d and len(rows) > 1:
+                    ts(off(c, d), led(c, d), base(c, 0), ADD, zoned(cw, c, d) + ["base%d0" % c], zoned("lh1", c, d))
+            for n in rows:
+                for c, d, a, qs in takes:
+                    d = min(d, reach(n))
+                    qs = "sv" if n > NEAR[0] else qs
+                    if c < d and n == 2:
+                        take(row(n, c, d), T.win[:, 2 * a:2 * CE].indirect(lst("wo", c // 16, d // 16)), d - c,
+                             zoned("win", a, C) + ["wine"] + zoned("lwo", c, d), zoned("h2", c, d), qs)
+                    elif c < d:
+                        take(row(n, c, d), row(n - m, a, CE).indirect(off(c, d)), d - c,
+                             zoned("h%d" % (n - m), a, reach(n - m)) + ["h%de" % (n - m)] + zoned("lh%d" % m, c, d), zoned("h%d" % n, c, d), qs)
+        ts(T.fl[:, C - 16:C], row(NEAR[0], C - 16, C), float(EVEN - MID), EQ, zoned("h%d" % NEAR[0], UP, C), ["fl"])
+        for n, (c, d) in zip(NEAR, ZONES):
+            d = min(d, C - 16)
+            land(scan(row(n, c, d), d - c, zoned("h%d" % n, c, d), "cy", "patf", c, "cy%d" % n), lst("foff", c // 16, d // 16), "lfoff%d" % c)
+        skip = SKIP0 if first else SKIP
+        if skip:
+            pick(T.r1, row(NEAR[2], 0, CE), lambda a, b: lst("ordo", a, b), zoned("h%d" % NEAR[2], 0, LOW) + ["h%de" % NEAR[2], "lordo"],
+                 "r1", CUT["br"])
+            wrap(T.r1, "r1", lambda a, b: lst("go", a, b), "lgo", CUT["br"], "cg")
+        for z, c, d, e in FILL[:-1 if skip else None]:
             c = c // 32 * 32
             take(T.fl[:, c:d], T.fl[:, e:e + 64 if e > UP else CE].indirect(lst("foff", c // 16, d // 16)), d - c,
-                 ["fl", "fle", "lfoff" + row], ["fl"], "vs")
-        add([("s", gcost("s", C), lambda e: e.activation(T.nf[:], T.fl[:, 0:C].indirect(lst("ordo")), IDENT, bias=1.0, scale=-1.0))],
-            ["fl", "lordo"], ["nf"])
-        tt(T.fo[:], T.fl[:, 0:C].indirect(lst("ordo")), T.oo[:], MUL, ["fl", "lordo", "oo", "ootop"], ["fo"], gcost("v", C))
+                 ["fl", "fle", "lfoff%d" % z], ["fl"], "vs")
+        by, keys = ("go", both("lgo")) if skip else ("ordo", ["lordo"])
+        add([("s", gcost("s", C), lambda e, by=by: e.activation(T.nf[:], T.fl[:, 0:CE].indirect(lst(by)), IDENT, bias=1.0, scale=-1.0))],
+            ["fl", "fle"] + keys, ["nf"])
+        tt(T.fo[:], T.fl[:, 0:CE].indirect(lst(by)), T.oo[:], MUL, ["fl", "fle", "oo", "ootop"] + keys, ["fo"], gcost("v", C))
         vec(lambda e: e.tensor_tensor_scan(T.sb[:], T.nf[:], T.fo[:], 0.0, MUL, ADD), vcost(C, 0.5), ["nf", "fo"], ["sb"])
         pick(T.br, T.sb[:], lambda a, b: lst("poso", a, b), ["sb", "lposo"], "br", CUT["br"])
-        wrap(T.br, "br", lambda a, b: lst("bo%d" % rd, a, b), "lbo%d" % rd, CUT["br"] if TWO else 0)
+        wrap(T.br, "br", lambda a, b: lst("bo%d" % rd, a, b), "lbo%d" % rd, CUT["br"], "cx")
         mail("bo%d" % rd, "bp%d" % rd, "rb%d" % rd, 0.0)
         calls[-1]["reads"].append("lbo%ds" % rd)
         take(T.r2[:], T.br[:].indirect(lst("ivp%d" % rd)), C, both("br") + ["livp%d" % rd], ["r2"])
@@ -626,7 +648,7 @@ def rank_program(g, core, T, topo):
                 if n:
                     behind()
 
-        mean("zt", 3, "tp", "bp%d" % rd, "gv", "z")
+        mean("zt", WZ, "tp", "bp%d" % rd, "gv", "z")
         for i, (c, d) in enumerate(RUNS):
             mm(1 + 4 * i, "w", 0, "z", ["wq", "wsc", both("z")[i]], c, d)
             unload(pl("hh", 0, c, d), bank(1 + 4 * i, d - c), d - c, ["b%d" % (1 + 4 * i)], [both("hh0")[i]], "vs", 0.015625)
@@ -635,7 +657,7 @@ def rank_program(g, core, T, topo):
             mm(1 + b, "w", 128 * b, "z", ["wq", "wsc"] + both("z"))
             unload(pl("hh", b), bank(1 + b), C, ["b%d" % (1 + b)], both("hh%d" % b), "s", 0.015625)
             sooner(0.1 * (3 - b))
-        mean("xt", 3 if rd < 2 else LASTWHOLE, "hh", "ep%d" % rd, "tu", "x%d" % (rd + 1))
+        mean("xt", WX if rd < 2 else LASTWHOLE, "hh", "ep%d" % rd, "tu", "x%d" % (rd + 1))
 
     add([("s", gcost("s", C), lambda e: e.activation(T.uof[:], IOTA.indirect(lst("udo")), COPY, bias=float(MID)))], ["iota", "ludo"], ["uof"])
     dma("y", T.uo[:], T.uof[0:128:16, :], ["uof"], [], LOAD)

@@ -13,18 +13,20 @@ ZONES, HALVES = ((UP, C), (LOW, UP), (0, LOW)), ((LOW, C), (0, LOW))
 FILL = ((UP, 256, 272, 272), (UP, 240, 256, 256), (UP, UP, 240, 240), (LOW, 192, UP, UP), (LOW, 160, 192, 192),
         (LOW, LOW, 160, 160), (0, 64, LOW, LOW), (0, 0, 64, 64))
 PLAN = ((1, (2, 3, 4)), (4, (8, 12, 16)), (16, (32, 48, 64)))
+PLAN0 = ((1, (2,)), (2, (4,)), (4, (8, 12, 16)), (16, (32, 48, 64)))
 NEAR = (16, 32, 64)
 SKIP0, SKIP = False, True
 TAKES = ((UP, C, UP, "s"), (LOW, UP, LOW, "v"), (64, LOW, 0, "s"), (0, 64, 0, "v"))
 FIRST = HALVES
 WZ, WX = 3, 3
 
-CYCLE, GATHER, DONE, SLACK = 0.001, 1.6, 0.2, 0.03
-HOP, SPARE, CODES, LOAD = 2.3, 1.0, 5.5, 2.0
+CYCLE, GATHER, DONE, SLACK = 0.00105, 1.65, 0.27, 0.03
+HOP, SPARE, CODES, LOAD, LONG = 1.6, 1.0, 4.8, 1.3, 0.7
 LEADI, LEADU, LEADR, LEADP = 3.0, 1.0, 1.0, 8.0
 PLACE = "sv"
 TWO0, TWO = True, True
-MOVES, MARGIN = 200000, 0.3
+MOVES = ((170000, 0.3), (70000, 0.2), (70000, 0.2), (30000, 0.05))
+SEED = 7
 ARRANGED = {}
 CUT = {"ring0": 0, "ring": 0, "mates": 8, "h0": 6, "h": 10, "br": 10}
 
@@ -39,7 +41,7 @@ for _n, _w in (("x0", C), ("x1", C), ("x2", C), ("x3", C), ("p0", C), ("p1", C),
     SCRATCH[_n + "q"] = ("sbuf", [128, _w], "float8_e4m3fn_x4")
     SCRATCH[_n + "sc"] = ("sbuf", [128, _w], "uint8")
 SCRATCH["ramp"] = ("sbuf", [128, 16 + 304], "bfloat16")
-POWERS = [n for m, rows in PLAN for n in rows]
+POWERS = sorted({n for m, rows in PLAN + PLAN0 for n in rows})
 SCRATCH["pw"] = ("sbuf", [128, 304 * len(POWERS)], "bfloat16")
 SCRATCH["fl"] = ("sbuf", [128, C + 48], "bfloat16")
 for _n in ("patf", "pp", "r1", "r2", "r3", "nf", "fo", "sb", "br", "uda", "mtr", "mr", "um", "oo"):
@@ -47,9 +49,11 @@ for _n in ("patf", "pp", "r1", "r2", "r3", "nf", "fo", "sb", "br", "uda", "mtr",
 SCRATCH["pat"] = ("sbuf", [128, C + 64], "bfloat16")
 SCRATCH["hpr"] = ("sbuf", [128, 2 * C + 64], "bfloat16")
 SCRATCH["win"] = ("sbuf", [128, 2 * C + 16], "bfloat16")
-SCRATCH["d0"] = ("sbuf", [128, 2 * C], "bfloat16")
+for _n in ("d0", "alt", "gv3"):
+    SCRATCH[_n] = ("sbuf", [128, 2 * C], "bfloat16")
 SCRATCH["d1"] = ("sbuf", [128, 2 * C], "float16")
 SCRATCH["dd"] = ("sbuf", [128, C], "float32")
+SCRATCH["pair"] = ("sbuf", [128, 6 * KW], "float32")
 SCRATCH["wide"] = ("sbuf", [128, 2 * CE], "float32")
 SCANS = ("ch", "co", "cm", "cg", "ce", "cp", "c3", "cw0", "cw1", "cw2", "cx", "cy", "cr")
 SCRATCH["cc"] = ("sbuf", [128, len(SCANS) * C + 64], "float16")
@@ -60,7 +64,7 @@ for _n in ("ivl", "mtl", "udl", "hpl"):
 SCRATCH["i32"] = ("sbuf", [128, 32], "int32")
 SCRATCH["qi"] = ("sbuf", [128, 2], "int32")
 SCRATCH["col"] = ("sbuf", [128, 16], "float32")
-SMALL = ("k16", "kb", "jw", "ivf", "mif", "di", "ga", "gb", "ta", "tb", "na", "nb", "e0", "df", "sg", "bi", "ti", "fb",
+SMALL = ("k16", "kb", "jw", "ivf", "mif", "di", "ga", "ta", "na", "jc", "e0", "df", "sg", "bi", "ti",
          "udf", "umf", "du", "t3", "bj", "tj")
 SCRATCH["sm"] = ("sbuf", [128, len(SMALL) * 20], "float32")
 LOCAL = ("iv0", "mi", "mto", "udo", "wo", "poso", "fa", "fb", "foff", "ordo", "go")
@@ -68,7 +72,7 @@ SCRATCH["lloc"] = ("sbuf", [128, len(LOCAL) * 24], "uint16")
 for _n in ("iv1", "iv2", "iv3", "bo0", "bo1", "bo2", "eo0", "eo1", "eo2",
            "ivp0", "ivp1", "ivp2", "bp0", "bp1", "bp2", "ep0", "ep1", "ep2"):
     SCRATCH["l" + _n] = ("sbuf", [128, KW], "uint16")
-SCRATCH["lhoff"] = ("sbuf", [128, len(PLAN) * KW], "uint16")
+SCRATCH["lhoff"] = ("sbuf", [128, 6 * KW], "uint16")
 SCRATCH["lhp"] = ("sbuf", [128, 2 * KW + 4], "uint16")
 SCRATCH["luo"] = ("sbuf", [128, 8], "uint16")
 SCRATCH["uoi"] = ("sbuf", [128, 8], "int32")
@@ -147,9 +151,10 @@ def shorten(calls, order, queue):
 
     ends = [i for i in range(n) if not calls[i]["before"]]
 
-    def run(order, queue, bound, same, end, cause):
+    def run(order, queue, bound, same, end, cause, goal, since):
         end, cause, last = end + [], cause + [], {queue[i]: i for i in order[:same]}
-        for i in order[same:]:
+        stop = order.index(goal) + 1 if goal < n else n
+        for i in order[same:stop]:
             q = queue[i]
             c = last.get(q, n)
             t = end[c]
@@ -157,49 +162,53 @@ def shorten(calls, order, queue):
                 if end[a] + gap > t:
                     t, c = end[a] + gap, a
             cause[i], last[q], end[i] = c, i, t + cost[i][q]
-        long, i = max((end[i] + calls[i]["late"], i) for i in ends)
+        long, i = (end[goal], goal) if goal < n else max((end[i] + calls[i]["late"], i) for i in ends)
         if long > bound:
             return None
         held = []
-        while cause[i] < n:
+        while cause[i] < n and end[i] > since:
             if cause[i] not in calls[i]["after"]:
                 held.append((cause[i], i))
             i = cause[i]
-        order = sorted(order, key=lambda i: end[i] - cost[i][queue[i]])
+        order = sorted(order[:stop], key=lambda i: end[i] - cost[i][queue[i]]) + order[stop:]
         return long, held, order, queue, {i: k for k, i in enumerate(order)}, end, cause
 
-    seed = [1]
+    seed = [SEED]
 
     def some(k):
         seed[0] = (seed[0] * 1103515245 + 12345) % 2 ** 31
         return (seed[0] >> 8) % k
 
-    now = best = run(order, queue, 1e9, 0, [0.0] * (n + 1), [n] * n)
-    for step in range(MOVES):
-        long, held, order, queue, at = now[:5]
-        c, i = held[some(len(held))]
-        kind = some(7)
-        if kind == 0:
-            x = (c, i)[some(2)]
-            if len(cost[x]) == 1:
-                continue
-            same, queue = at[x], list(queue)
-            queue[x] = [q for q in cost[x] if q != queue[x]][0]
-        elif kind < 4:
-            a, b = at[i], min([at[k] for k in calls[c]["before"]], default=n)
-            if b <= a:
-                continue
-            same, to = at[c], a + some(b - a) * some(2)
-            order = order[:same] + order[same + 1:to + 1] + [c] + order[to + 1:]
-        else:
-            a, b = max([at[k] for k in calls[i]["after"]], default=-1), at[c]
-            if b <= a:
-                continue
-            same = b - some(b - a) * some(2)
-            order = order[:same] + [i] + order[same:at[i]] + order[at[i] + 1:]
-        now = run(order, queue, long + MARGIN * (1 - step / MOVES) * some(100) / 100, same, now[5], now[6]) or now
-        best = min(best, now, key=lambda r: r[0])
-    return best[2:4]
+    since = 0.0
+    for goal, (moves, margin) in zip([i for i in range(n) if calls[i]["ends"]] + [n, n], MOVES):
+        now = best = run(order, queue, 1e9, 0, [0.0] * (n + 1), [n] * n, goal, since)
+        for step in range(moves):
+            long, held, order, queue, at = now[:5]
+            c, i = held[some(len(held))]
+            kind = some(7)
+            if kind == 0:
+                x = (c, i)[some(2)]
+                if len(cost[x]) == 1:
+                    continue
+                same, queue = at[x], list(queue)
+                queue[x] = [q for q in cost[x] if q != queue[x]][0]
+            elif kind < 4:
+                a, b = at[i], min([at[k] for k in calls[c]["before"]], default=n)
+                if b <= a:
+                    continue
+                same, to = at[c], a + some(b - a) * some(2)
+                order = order[:same] + order[same + 1:to + 1] + [c] + order[to + 1:]
+            else:
+                a, b = max([at[k] for k in calls[i]["after"]], default=-1), at[c]
+                if b <= a:
+                    continue
+                same = b - some(b - a) * some(2)
+                order = order[:same] + [i] + order[same:at[i]] + order[at[i] + 1:]
+            now = run(order, queue, long + margin * (1 - step / moves) * some(100) / 100, same, now[5], now[6], goal, since) or now
+            best = min(best, now, key=lambda r: r[0])
+        order, queue = best[2:4]
+        since = best[0] - 3.0 if goal < n else 0.0
+    return order, queue
 
 
 def rank_program(g, core, T, topo):
@@ -248,7 +257,7 @@ def rank_program(g, core, T, topo):
 
     def add(ways, reads, writes, late=DONE, kind="op", arrive=None):
         calls.append({"ways": ways, "reads": list(reads), "writes": list(writes), "late": late, "kind": kind, "arrive": arrive,
-                      "lead": 0.0, "behind": []})
+                      "lead": 0.0, "behind": [], "ends": False})
 
     def behind():
         calls[-1]["behind"].append(len(calls) - 2)
@@ -318,6 +327,8 @@ def rank_program(g, core, T, topo):
         return T.ps[:, 512 * k:512 * k + n]
 
     def pl(name, b, c=0, d=C):
+        if b == 3 and name == "gv":
+            return T[name + "3"][:, 2 * c:2 * d:2]
         return T[name][:, b * C + c:b * C + d]
 
     def lst(name, a=0, b=KW):
@@ -360,8 +371,8 @@ def rank_program(g, core, T, topo):
     def zoned(key, c, d):
         return ["%s.%d" % (key, a) for a, b, z, q in TAKES if a < d and c < b]
 
-    def base(c, half):
-        k = 8 + 2 * [a for a, b in ZONES].index(c) + half
+    def base(c):
+        k = 8 + [a for a, b in ZONES].index(c)
         return T.col[:, k:k + 1]
 
     def land(job, out, key):
@@ -377,11 +388,13 @@ def rank_program(g, core, T, topo):
     for q, to, src, key, long in (("s", T.hpl[:], T.hp, "hpl", 0.3), ("y", T.mtl[:], T.mt, "mtl", 0.3), ("s", T.ivl[:], T.iv, "ivl", 0.3),
                                   ("y", T.ut[:], T.u, "ut", 0.7), ("y", T.xin[:], T.x, "xin", 1.2), ("y", T.udl[:], T.ud, "udl", 0.3),
                                   ("y", u8(T.wq[:]), T.wc, "wq", 1.2), ("y", T.wsc[:], T.ws, "wsc", 0.5), ("y", T.vt[:], T.v, "vt", 0.7)):
-        t += long
+        t += long * LONG
         dma(q, to, src[:], [], [key], t, "load")
 
     fill(T.et[:], 0.0, ["et"], 520)
-    fill(T.d0[:, 0:2 * C:2], 0.0, ["d0e"], C)
+    fill(T.alt[:, 0:2 * C:2], 0.0, ["alt"], C)
+    unload(T.d0[:, 0:2 * C:2], T.alt[:, 0:2 * C:2], C, ["alt"], ["d0e"], "s")
+    add([("s", C * CYCLE + 0.065, lambda e: e.activation(T.alt[:, 1:2 * C:2], T.alt[:, 0:2 * C:2], IDENT, bias=1.0))], ["alt"], ["alts"])
     fill(T.win[:, 2 * C:2 * CE], float(EVEN - MID), ["wine"])
     fill(T.win[:, 2 * EVEN + 1:2 * EVEN + 2], float(ODD - MID), ["wine"])
     fill(T.fl[:, C:C + 48], 0.0, ["fle"])
@@ -412,13 +425,12 @@ def rank_program(g, core, T, topo):
     ts(T.pb[:], T.i32[:], 15.0, EQ, ["i32"], ["pb"], -2 * BIG, MUL)
     tt(T.pat[:, 0:32], T.pa[:], T.pb[:], ADD, ["pa", "pb"], ["pat0"])
     for a in (32, 64, 96):
-        cp(T.pat[:, a:a + 32], T.pat[:, 0:32], ["pat0"], ["pat%d" % a])
-    cp(T.pat[:, 128:256], T.pat[:, 0:128], ["pat0", "pat32", "pat64", "pat96"], ["pat128"])
-    cp(T.pat[:, 256:352], T.pat[:, 0:96], ["pat0", "pat32", "pat64", "pat128"], ["pat"])
+        unload(T.pat[:, a:a + 32], T.pat[:, 0:32], 32, ["pat0"], ["pat%d" % a])
+    unload(T.pat[:, 128:256], T.pat[:, 0:128], 64, ["pat0", "pat32", "pat64", "pat96"], ["pat128"])
+    unload(T.pat[:, 256:352], T.pat[:, 0:96], 64, ["pat0", "pat32", "pat64", "pat128"], ["pat"])
     ts(CORR, QZ, 2 * BIG, MUL, ["qz"], ["corr"], MID - BIG, ADD)
     for c, d in ZONES:
-        for half in range(2):
-            ts(base(c, half), QZ, 2 * BIG, MUL, ["qz"], ["base%d%d" % (c, half)], MID - BIG - c + half / 2, ADD)
+        ts(base(c), QZ, 2 * BIG, MUL, ["qz"], ["base%d" % c], MID - BIG - c + 0.5, ADD)
     ts(THR, QZ, -4 * BIG, MUL, ["qz"], ["thr"], 1.5 + 2 * BIG, ADD)
     unload(T.patf[:], T.pat[:, 0:C], C, ["pat"], ["patf"], "s")
     sooner(LEADP)
@@ -478,17 +490,22 @@ def rank_program(g, core, T, topo):
     pick(T.mtr, IOTA, lambda a, b: lst("mto", a, b), ["iota", "lmto"], "mtr", CUT["mates"])
     pick(T.mr, T.mtr[:], lambda a, b: lst("iv0", a, b), both("mtr") + ["liv0"], "mr", CUT["mates"])
     job = scan(T.mr[:], C, both("mr"), "cm")
-    land(job, sm("mif"), "mif")
     land(job, lst("mi"), "lmi")
-    for f, n, end in (("ivf", "a", ODD), ("mif", "b", ODD2)):
-        small("g" + n, f, "jw", GT)
-        ts(sm("t" + n), sm(f), float(end), SUB, [f], ["t" + n])
-        small("n" + n, "g" + n, "t" + n, MUL)
+    land(job, sm("mif"), "mif")
+    tt(sm("ga"), T.ivl[:], sm("jw"), GT, ["ivl", "jw"], ["ga"])
+    ts(sm("ta"), T.ivl[:], float(ODD), SUB, ["ivl"], ["ta"])
+    small("na", "ga", "ta", MUL)
     ts(lst("fa"), sm("na"), float(ODD), ADD, ["na"], ["lfa"])
     take(T.win[:, 1:2 * C:2], IOTA.indirect(lst("fa")), C, ["iota", "lfa"], zoned("win", 0, C), "s")
-    small("fb", "nb", "na", SUB)
-    ts(lst("fb"), sm("fb"), float(ODD2 - ODD + CE), ADD, ["fb"], ["lfb"])
-    ts(sm("df"), sm("fb"), float(ODD2 - ODD), ADD, ["fb"], ["df"])
+    ts(sm("jc"), sm("jw"), CORR, SUB, ["jw", "corr"], ["jc"])
+    fill(T.pair[:, 0:2 * KW:2], 0.0, ["pair0"])
+    tt(T.pair[:, 1:2 * KW:2], job[1], sm("jc"), GT, ["cm", "jc"], ["pair1"])
+    ts(T.pair[:, 2 * KW:4 * KW:2], job[1], CORR, ADD, ["cm", "corr"], ["pair2"], float(ODD2), SUB)
+    ts(T.pair[:, 2 * KW + 1:4 * KW:2], sm("na"), -1.0, MUL, ["na"], ["pair3"], float(ODD2 - ODD), ADD)
+    vec(lambda e: e.tensor_tensor_scan(T.pair[:, 4 * KW:6 * KW], T.pair[:, 0:2 * KW], T.pair[:, 2 * KW:4 * KW], 0.0, MUL, ADD), vcost(0, 1),
+        ["pair%d" % i for i in range(4)], ["pair"])
+    ts(lst("fb"), T.pair[:, 4 * KW + 1:6 * KW:2], float(CE), ADD, ["pair"], ["lfb"])
+    cp(sm("df"), T.pair[:, 4 * KW + 1:6 * KW:2], ["pair"], ["df"])
     ts(sm("e0"), sm("na"), float(ODD), ADD, ["na", "corr"], ["e0"], CORR, SUB)
     small("di", "mif", "ivf", SUB)
     cp(lst("udo"), T.udl[:], ["udl"], ["ludo"])
@@ -520,14 +537,16 @@ def rank_program(g, core, T, topo):
         else:
             parts = [(dst, u8(T[p + "q"][:]), u8(T[x + "q"][:])), (dst, T[p + "sc"][:], T[x + "sc"][:])]
         nx = 2 * width(back[0], core) + width(back[1], core) if back else 2 * width(dst, core)
-        send(parts, both(x), p, "rx%d" % rd, nx, CODES + (hops - 1) * HOP)
+        send(parts, both(x), p, "rx%d" % rd, nx, CODES + (hops - 1) * (HOP + SPARE))
+        if first:
+            calls[-1]["behind"] = [i for i, c in enumerate(calls[:-1]) if c["ways"][0][0] == "g"]
 
         def mail(name, to, sem, spare=SPARE):
             send([(rel[1] if rel else dst, lst(to), lst(name))], ["l" + name], "l" + to, sem, width(back[1] if back else dst, core),
-                 hops * HOP - 0.4 + spare)
+                 hops * (HOP + spare) - 0.4)
 
         cp(T.d1[:, 1:2 * C:2], T.win[:, 1:2 * C:2], zoned("win", 0, C), ["d1a"], vcost(C, 0.5))
-        take(T.dd[:], T.wide[:].indirect(lst("fb")), C, ["wide", "lfb"], ["dd"], "s" if first else "sv")
+        take(T.dd[:], T.wide[:].indirect(lst("fb")), C, ["wide", "lfb"], ["dd"])
         for i, (c, d) in enumerate(RUNS):
             mm(5 * i, "ur", 0, x, ["urq", "ursc", both(x)[i]], c, d)
             ts(T.pp[:, c:d], bank(5 * i, d - c), 0.0, GT, ["b%d" % (5 * i)], [both("pp")[i]], cost=vcost(d - c, 1))
@@ -544,7 +563,7 @@ def rank_program(g, core, T, topo):
         for c, d in scans:
             job = scan(T.win[:, 2 * c + 1:2 * d:2], d - c, zoned("win", c, d), cw, "pat", c)
             calls[-1]["writes"] = zoned(cw, c, d)
-            ts(lst("wo", c // 16, d // 16), job[1], base(c, 1), ADD, zoned(cw, c, d) + ["base%d1" % c], zoned("lwo", c, d), 2.0, MUL)
+            ts(lst("wo", c // 16, d // 16), job[1], base(c), ADD, zoned(cw, c, d) + ["base%d" % c], zoned("lwo", c, d), 2.0, MUL)
         old = (["e0"], sm("e0")) if first else last
         def led(c, d, cw=cw):
             return T.cc[:, C * SCANS.index(cw) + c + 15:C * SCANS.index(cw) + d:16]
@@ -554,7 +573,7 @@ def rank_program(g, core, T, topo):
         small("ti", "bi", "di", MUL)
         small("ivf", "ivf", "ti", ADD)
         cp(lst("iv%d" % (rd + 1)), sm("ivf"), ["ivf"], ["liv%d" % (rd + 1)])
-        mail("iv%d" % (rd + 1), "ivp%d" % rd, "ri%d" % rd)
+        mail("iv%d" % (rd + 1), "ivp%d" % rd, "ri%d" % rd, 2 * SPARE)
         sooner(LEADI)
         if rd < 2:
             small("mif", "mif", "ti", SUB)
@@ -584,7 +603,7 @@ def rank_program(g, core, T, topo):
             mm(k, "e", 128 * b, p, ["e%d" % b, p])
             unload(pl("tp", b), bank(k), C, ["b%d" % k], both("tp%d" % b))
             take(pl("gv", b), pl("tp", b).indirect(lst("ivp%d" % rd)), C, ["tp%d" % b, "livp%d" % rd], ["gv%d" % b])
-        for i, (m, rows) in enumerate(PLAN):
+        for i, (m, rows) in enumerate(PLAN0 if first else PLAN):
             def off(c, d):
                 return T.lhoff[:, i * KW + c // 16:i * KW + d // 16]
 
@@ -593,9 +612,9 @@ def rank_program(g, core, T, topo):
                 if c < d and m > 1:
                     job = scan(row(m, c, d), d - c, zoned("h%d" % m, c, d), "ch", "pat", c)
                     calls[-1]["writes"] = zoned("ch", c, d)
-                    ts(off(c, d), job[1], base(c, 0), ADD, zoned("ch", c, d) + ["base%d0" % c], zoned("lh%d" % m, c, d))
+                    ts(off(c, d), job[1], CORR, ADD, zoned("ch", c, d) + ["corr"], zoned("lh%d" % m, c, d), float(c), SUB)
                 elif c < d and len(rows) > 1:
-                    ts(off(c, d), led(c, d), base(c, 0), ADD, zoned(cw, c, d) + ["base%d0" % c], zoned("lh1", c, d))
+                    ts(off(c, d), led(c, d), CORR, ADD, zoned(cw, c, d) + ["corr"], zoned("lh1", c, d), float(c), SUB)
             for n in rows:
                 for c, d, a, qs in takes:
                     d = min(d, reach(n))
@@ -636,19 +655,24 @@ def rank_program(g, core, T, topo):
                 tt(T[to][:, 4 * c + b:4 * d:4], pl(win, b).indirect(lst(off, c // 16, d // 16)), pl(other, b, c, d), ADD,
                    both("%s%d" % (win, b)) + ["%s%d" % (other, b), "l" + off], keys, gcost("v", d - c))
 
-            steps = [(b, None) for b in range(whole)] + [(b, i) for i in range(2) for b in list(range(whole, 4)) + [None]]
-            k = steps.index((None, 0))
-            steps[k:k + 2] = steps[k + 1], steps[k]
+            if whole:
+                take(T[other + "3"][:, 1:2 * C:2], pl(win, 3).indirect(lst(off)), C, both(win + "3") + ["l" + off], [other + "3s"], "s")
+                steps = [(0, None), (2, 0), (3, None), (2, 1), (1, 0), (1, 1), (None, 0), (None, 1)]
+            else:
+                steps = [(0, None), (1, None), (2, None), (3, 0), (3, 1), (None, 0), (None, 1)]
             for n, (b, i) in enumerate(steps):
                 c, d = (0, C) if i is None else RUNS[i]
                 if b is None:
                     quant(q, T[to][:, 4 * c:4 * d], [both("%s%d" % (to, a))[i] for a in range(4)], c, d, both(q)[i])
+                elif b == 3 and whole:
+                    vec(lambda e: e.tensor_tensor_scan(T[to][:, 1:4 * C:2], T.alt[:], T[other + "3"][:], 0.0, MUL, ADD), vcost(2 * C, 0.5),
+                        both(other + "3") + both("alt"), both(to + "3") + both(to + "1"))
                 else:
                     plane(b, c, d, both("%s%d" % (to, b)) if i is None else [both("%s%d" % (to, b))[i]])
                 if n:
                     behind()
 
-        mean("zt", WZ, "tp", "bp%d" % rd, "gv", "z")
+        mean("zt", True, "tp", "bp%d" % rd, "gv", "z")
         for i, (c, d) in enumerate(RUNS):
             mm(1 + 4 * i, "w", 0, "z", ["wq", "wsc", both("z")[i]], c, d)
             unload(pl("hh", 0, c, d), bank(1 + 4 * i, d - c), d - c, ["b%d" % (1 + 4 * i)], [both("hh0")[i]], "vs", 0.015625)
@@ -657,7 +681,8 @@ def rank_program(g, core, T, topo):
             mm(1 + b, "w", 128 * b, "z", ["wq", "wsc"] + both("z"))
             unload(pl("hh", b), bank(1 + b), C, ["b%d" % (1 + b)], both("hh%d" % b), "s", 0.015625)
             sooner(0.1 * (3 - b))
-        mean("xt", WX if rd < 2 else LASTWHOLE, "hh", "ep%d" % rd, "tu", "x%d" % (rd + 1))
+        mean("xt", False, "hh", "ep%d" % rd, "tu", "x%d" % (rd + 1))
+        calls[-1]["ends"] = rd < 2
 
     add([("s", gcost("s", C), lambda e: e.activation(T.uof[:], IOTA.indirect(lst("udo")), COPY, bias=float(MID)))], ["iota", "ludo"], ["uof"])
     dma("y", T.uo[:], T.uof[0:128:16, :], ["uof"], [], LOAD)

from concourse.mybir import dt, AluOpType, ActivationFunctionType

C, KW = 288, 18
STEP = (4, 1, 2)
MID = 145
BIG = 512.0
EVEN, ODD, ODD2 = C, C + 1, C + 3
CE = C + 4
RUNS = ((0, 160), (160, C))
LASTWHOLE, SPLIT = 0, True
LOW, UP = 128, 224
ZONES, HALVES = ((UP, C), (LOW, UP), (0, LOW)), ((LOW, C), (0, LOW))
FILL = ((UP, 256, 272, 272), (UP, 240, 256, 256), (UP, UP, 240, 240), (LOW, 192, UP, UP), (LOW, 160, 192, 192),
        (LOW, LOW, 160, 160), (0, 64, LOW, LOW), (0, 0, 64, 64))
PLAN = ((1, (2, 3, 4)), (4, (8, 12, 16)), (16, (32, 48, 64)))
PLAN0 = ((1, (2,)), (2, (4,)), (4, (8, 12, 16)), (16, (32, 48, 64)))
NEAR = (16, 32, 64)
SKIP0, SKIP = False, True
TAKES = ((UP, C, UP, "s"), (LOW, UP, LOW, "v"), (64, LOW, 0, "s"), (0, 64, 0, "v"))
FIRST = HALVES
WZ, WX = 3, 3

CYCLE, GATHER, DONE, SLACK = 0.00105, 1.65, 0.27, 0.03
HOP, SPARE, CODES, LOAD, LONG = 1.6, 1.0, 4.8, 1.3, 0.7
LEADI, LEADU, LEADR, LEADP = 3.0, 1.0, 1.0, 8.0
PLACE = "sv"
TWO0, TWO = True, True
MOVES = ((170000, 0.3), (70000, 0.2), (70000, 0.2), (30000, 0.05))
SEED = 7
ARRANGED = {}
CUT = {"ring0": 0, "ring": 0, "mates": 8, "h0": 6, "h": 10, "br": 10}

SCRATCH = {}
for _n in ("xin", "xt", "zt", "th", "tp", "tu", "gv", "hh"):
    SCRATCH[_n] = ("sbuf", [128, 4 * C], "bfloat16")
for _n in ("ut", "vt"):
    SCRATCH[_n] = ("sbuf", [128, 512], "bfloat16")
SCRATCH["et"] = ("sbuf", [128, 520], "bfloat16")
for _n, _w in (("x0", C), ("x1", C), ("x2", C), ("x3", C), ("p0", C), ("p1", C), ("p2", C), ("z", C),
               ("u", 128), ("ur", 128), ("v", 128), ("e", 512), ("w", 512)):
    SCRATCH[_n + "q"] = ("sbuf", [128, _w], "float8_e4m3fn_x4")
    SCRATCH[_n + "sc"] = ("sbuf", [128, _w], "uint8")
SCRATCH["ramp"] = ("sbuf", [128, 16 + 304], "bfloat16")
POWERS = sorted({n for m, rows in PLAN + PLAN0 for n in rows})
SCRATCH["pw"] = ("sbuf", [128, 304 * len(POWERS)], "bfloat16")
SCRATCH["fl"] = ("sbuf", [128, C + 48], "bfloat16")
for _n in ("patf", "pp", "r1", "r2", "r3", "nf", "fo", "sb", "br", "uda", "mtr", "mr", "um", "oo"):
    SCRATCH[_n] = ("sbuf", [128, C], "bfloat16")
SCRATCH["pat"] = ("sbuf", [128, C + 64], "bfloat16")
SCRATCH["hpr"] = ("sbuf", [128, 2 * C + 64], "bfloat16")
SCRATCH["win"] = ("sbuf", [128, 2 * C + 16], "bfloat16")
for _n in ("d0", "alt", "gv3"):
    SCRATCH[_n] = ("sbuf", [128, 2 * C], "bfloat16")
SCRATCH["d1"] = ("sbuf", [128, 2 * C], "float16")
SCRATCH["dd"] = ("sbuf", [128, C], "float32")
SCRATCH["pair"] = ("sbuf", [128, 6 * KW], "float32")
SCRATCH["wide"] = ("sbuf", [128, 2 * CE], "float32")
SCANS = ("ch", "co", "cm", "cg", "ce", "cp", "c3", "cw0", "cw1", "cw2", "cx", "cy", "cr")
SCRATCH["cc"] = ("sbuf", [128, len(SCANS) * C + 64], "float16")
for _n in ("pa", "pb"):
    SCRATCH[_n] = ("sbuf", [128, 32], "bfloat16")
for _n in ("ivl", "mtl", "udl", "hpl"):
    SCRATCH[_n] = ("sbuf", [128, KW], "int32")
SCRATCH["i32"] = ("sbuf", [128, 32], "int32")
SCRATCH["qi"] = ("sbuf", [128, 2], "int32")
SCRATCH["col"] = ("sbuf", [128, 16], "float32")
SMALL = ("k16", "kb", "jw", "ivf", "mif", "di", "ga", "ta", "na", "jc", "e0", "df", "sg", "bi", "ti",
         "udf", "umf", "du", "t3", "bj", "tj")
SCRATCH["sm"] = ("sbuf", [128, len(SMALL) * 20], "float32")
LOCAL = ("iv0", "mi", "mto", "udo", "wo", "poso", "fa", "fb", "foff", "ordo", "go")
SCRATCH["lloc"] = ("sbuf", [128, len(LOCAL) * 24], "uint16")
for _n in ("iv1", "iv2", "iv3", "bo0", "bo1", "bo2", "eo0", "eo1", "eo2",
           "ivp0", "ivp1", "ivp2", "bp0", "bp1", "bp2", "ep0", "ep1", "ep2"):
    SCRATCH["l" + _n] = ("sbuf", [128, KW], "uint16")
SCRATCH["lhoff"] = ("sbuf", [128, 6 * KW], "uint16")
SCRATCH["lhp"] = ("sbuf", [128, 2 * KW + 4], "uint16")
SCRATCH["luo"] = ("sbuf", [128, 8], "uint16")
SCRATCH["uoi"] = ("sbuf", [128, 8], "int32")
SCRATCH["uof"] = ("sbuf", [128, C], "float32")
SCRATCH["yf"] = ("sbuf", [128, C], "float32")
SCRATCH["ps"] = ("psum", [128, 4096], "float32")

SEMAPHORES = ["cv", "cs", "ct", "cg", "snt"] + ["d%d" % i for i in range(24)]
SEMAPHORES += ["%s%d" % (a, i) for a in ("rx", "ri", "rb", "re") for i in range(3)]

MUL, ADD, SUB, MAX, MIN = AluOpType.mult, AluOpType.add, AluOpType.subtract, AluOpType.max, AluOpType.min
GT, GE, EQ, NE = AluOpType.is_gt, AluOpType.is_ge, AluOpType.is_equal, AluOpType.not_equal
AND = AluOpType.bitwise_and
COPY = ActivationFunctionType.Copy
IDENT = ActivationFunctionType.Identity


def relays(topo, src, dst):
    if topo.may_write(src, dst):
        return None
    c = [a for a in topo.cores_of(src) if a != src and topo.may_write(a, dst)]
    near = [a for a in c if topo.die(a) == topo.die(src)]
    far = [a for a in c if topo.die(a) != topo.die(src)]
    return (near + far)[:2]


def arrange(calls):
    wr, rd = {}, {}
    for i, c in enumerate(calls):
        after = {wr[k] for k in c["reads"] + c["writes"] if k in wr}
        for k in c["writes"]:
            after |= set(rd.get(k, []))
        for k in c["reads"]:
            rd.setdefault(k, []).append(i)
        for k in c["writes"]:
            wr[k], rd[k] = i, []
        c["after"] = dict({a: 0.0 for a in c["behind"]}, **{})
        c["after"].update({a: calls[a]["late"] for a in after})
        c["before"], c["chain"] = {}, c["late"]
        for a, gap in c["after"].items():
            calls[a]["before"][i] = gap
    for c in reversed(calls):
        c["chain"] += min(w[1] for w in c["ways"]) + c["lead"]
        for a, gap in c["after"].items():
            calls[a]["chain"] = max(calls[a]["chain"], c["chain"] + gap)

    every = range(len(calls))
    shape = tuple(c["late"] for c in calls)
    if shape not in ARRANGED:
        busy, end, way = {}, {}, {}
        for i in sorted(every, key=lambda i: -calls[i]["chain"]):
            ready = max([end[a] + gap for a, gap in calls[i]["after"].items()], default=0.0)
            best = None
            for q, cost, call in calls[i]["ways"]:
                t = ready
                for a, b in busy.setdefault(q, []):
                    if t + cost <= a + SLACK:
                        break
                    t = max(t, b)
                if best is None or t + cost < best[0] + best[2]:
                    best = (t, q, cost)
            way[i], end[i] = best, best[0] + best[2]
            busy[best[1]] = sorted(busy[best[1]] + [(best[0], end[i])])
        ARRANGED[shape] = shorten(calls, sorted(every, key=lambda i: way[i][0]), [way[i][1] for i in every])
    order, queue = ARRANGED[shape]
    for i, c in enumerate(calls):
        c["queue"] = queue[i]
        c["call"] = [w[2] for w in c["ways"] if w[0] == queue[i]][0]
    return [calls[i] for i in order]


def shorten(calls, order, queue):
    n = len(calls)
    after = [list(c["after"].items()) for c in calls]
    cost = [{w[0]: w[1] for w in c["ways"]} for c in calls]

    ends = [i for i in range(n) if not calls[i]["before"]]

    def run(order, queue, bound, same, end, cause, goal, since):
        end, cause, last = end + [], cause + [], {queue[i]: i for i in order[:same]}
        stop = order.index(goal) + 1 if goal < n else n
        for i in order[same:stop]:
            q = queue[i]
            c = last.get(q, n)
            t = end[c]
            for a, gap in after[i]:
                if end[a] + gap > t:
                    t, c = end[a] + gap, a
            cause[i], last[q], end[i] = c, i, t + cost[i][q]
        long, i = (end[goal], goal) if goal < n else max((end[i] + calls[i]["late"], i) for i in ends)
        if long > bound:
            return None
        held = []
        while cause[i] < n and end[i] > since:
            if cause[i] not in calls[i]["after"]:
                held.append((cause[i], i))
            i = cause[i]
        order = sorted(order[:stop], key=lambda i: end[i] - cost[i][queue[i]]) + order[stop:]
        return long, held, order, queue, {i: k for k, i in enumerate(order)}, end, cause

    seed = [SEED]

    def some(k):
        seed[0] = (seed[0] * 1103515245 + 12345) % 2 ** 31
        return (seed[0] >> 8) % k

    since = 0.0
    for goal, (moves, margin) in zip([i for i in range(n) if calls[i]["ends"]] + [n, n], MOVES):
        now = best = run(order, queue, 1e9, 0, [0.0] * (n + 1), [n] * n, goal, since)
        for step in range(moves):
            long, held, order, queue, at = now[:5]
            c, i = held[some(len(held))]
            kind = some(7)
            if kind == 0:
                x = (c, i)[some(2)]
                if len(cost[x]) == 1:
                    continue
                same, queue = at[x], list(queue)
                queue[x] = [q for q in cost[x] if q != queue[x]][0]
            elif kind < 4:
                a, b = at[i], min([at[k] for k in calls[c]["before"]], default=n)
                if b <= a:
                    continue
                same, to = at[c], a + some(b - a) * some(2)
                order = order[:same] + order[same + 1:to + 1] + [c] + order[to + 1:]
            else:
                a, b = max([at[k] for k in calls[i]["after"]], default=-1), at[c]
                if b <= a:
                    continue
                same = b - some(b - a) * some(2)
                order = order[:same] + [i] + order[same:at[i]] + order[at[i] + 1:]
            now = run(order, queue, long + margin * (1 - step / moves) * some(100) / 100, same, now[5], now[6], goal, since) or now
            best = min(best, now, key=lambda r: r[0])
        order, queue = best[2:4]
        since = best[0] - 3.0 if goal < n else 0.0
    return order, queue


def rank_program(g, core, T, topo):
    rank = T.rank_of(core)
    sent = [0]

    def width(a, b):
        return len(topo.engines(a, b))

    def put(dst, out, in_, sem):
        e = topo.engines(core, dst)[:width(core, dst)]
        rid, pid = topo.addr(dst, core)
        m = 0
        for a in e:
            m |= 1 << a
        g.remote_dma(out, in_, T.sem[sem], T.sem.snt, pid, rid, m)
        sent[0] += len(e)

    def u8(ap):
        return ap.bitcast(dt.uint8)

    HALF = C // 2
    if rank is None:
        for rd, step in enumerate(STEP):
            for r, src in enumerate(T.cores):
                dst = T.cores[r ^ step]
                rel = relays(topo, src, dst)
                if not rel or core not in rel:
                    continue
                n = width(src, core)
                if core == rel[0]:
                    g.wait_ge(T.sem["rx%d" % rd], 2 * n)
                    put(dst, u8(T["p%dq" % rd][:, 0:HALF]), u8(T["p%dq" % rd][:, 0:HALF]), "rx%d" % rd)
                    put(dst, T["p%dsc" % rd][:], T["p%dsc" % rd][:], "rx%d" % rd)
                else:
                    g.wait_ge(T.sem["rx%d" % rd], n)
                    put(dst, u8(T["p%dq" % rd][:, HALF:C]), u8(T["p%dq" % rd][:, HALF:C]), "rx%d" % rd)
                    for s, b in (("ri", "livp"), ("rb", "lbp"), ("re", "lep")):
                        g.wait_ge(T.sem["%s%d" % (s, rd)], n)
                        put(dst, T["%s%d" % (b, rd)][:], T["%s%d" % (b, rd)][:], "%s%d" % (s, rd))
        if sent[0]:
            g.wait_ge(T.sem.snt, sent[0])
        return

    calls = []

    def add(ways, reads, writes, late=DONE, kind="op", arrive=None):
        calls.append({"ways": ways, "reads": list(reads), "writes": list(writes), "late": late, "kind": kind, "arrive": arrive,
                      "lead": 0.0, "behind": [], "ends": False})

    def behind():
        calls[-1]["behind"].append(len(calls) - 2)

    def sooner(lead):
        calls[-1]["lead"] = lead

    def vcost(n, rate):
        return max(64, n * rate) * CYCLE

    def gcost(q, n):
        return (0.05 if q == "v" else 0.065) + n * GATHER * CYCLE

    def vec(call, cost, reads, writes):
        add([("v", cost, call)], reads, writes)

    def pool(call, n, reads, writes):
        add([("g", 0.17 + 2 * n * CYCLE, call)], reads, writes, 0.25)

    def dma(q, out, in_, reads, writes, late, kind="dma"):
        add([(q, 0.05, lambda e: e.dma_start(out, in_))], reads, writes, late, kind)

    def send(parts, reads, key, sem, n, late):
        def call(e):
            for dst, out, in_ in parts:
                put(dst, out, in_, sem)
        add([("g", 0.4 * len(parts), call)], reads, [key], late, "send", (sem, n))

    def tt(out, a, b, o, reads, writes, cost=64 * CYCLE):
        vec(lambda e: e.tensor_tensor(out, a, b, o), cost, reads, writes)

    def ts(out, a, s1, o1, reads, writes, s2=None, o2=None, cost=64 * CYCLE):
        if o2 is None:
            vec(lambda e: e.tensor_scalar(out, a, s1, None, o1), cost, reads, writes)
        else:
            vec(lambda e: e.tensor_scalar(out, a, s1, s2, o1, o2), cost, reads, writes)

    def cp(out, in_, reads, writes, cost=64 * CYCLE):
        vec(lambda e: e.tensor_copy(out, in_), cost, reads, writes)

    def take(out, win, n, reads, writes, qs="sv"):
        way = {"v": lambda e: e.tensor_copy(out, win), "s": lambda e: e.activation(out, win, COPY)}
        add([(q, gcost(q, n), way[q]) for q in qs], reads, writes)

    def unload(out, in_, n, reads, writes, qs="sv", scale=None):
        if scale is None:
            way = {"v": lambda e: e.tensor_copy(out, in_), "s": lambda e: e.activation(out, in_, COPY)}
        else:
            way = {"v": lambda e: e.tensor_scalar(out, in_, scale, None, MUL), "s": lambda e: e.activation(out, in_, COPY, scale=scale)}
        add([(q, n * CYCLE + 0.065 if q == "s" else vcost(n, 1), way[q]) for q in qs], reads, writes)

    def fill(ap, c, writes, n=64):
        vec(lambda e: e.memset(ap, c), vcost(n, 0.5), [], writes)

    def count(ap, pattern, base, n, writes, reads=()):
        pool(lambda e: e.iota(ap, pattern, base, 0, allow_small_or_imprecise_dtypes=True), n, reads, writes)

    def quant(name, tile, reads, a=0, b=C, key=None):
        vec(lambda e: e.quantize_mx(T[name + "q"][:, a:b], T[name + "sc"][:, a:b], tile), (15 + 1.05 * (b - a)) * CYCLE, reads, [key or name])

    def mm(bank, l, a, r, reads, c=0, d=C):
        add([("t", 0.07 + 0.0006 * (d - c), lambda e: e.matmul_mx(
            T.ps[:, 512 * bank:512 * bank + d - c], T[l + "q"][:, a:a + 128], T[l + "sc"][:, a:a + 128], T[r + "q"][:, c:d],
            T[r + "sc"][:, c:d], True, True))], reads, ["b%d" % bank])

    def bank(k, n=C):
        return T.ps[:, 512 * k:512 * k + n]

    def pl(name, b, c=0, d=C):
        if b == 3 and name == "gv":
            return T[name + "3"][:, 2 * c:2 * d:2]
        return T[name][:, b * C + c:b * C + d]

    def lst(name, a=0, b=KW):
        if name in LOCAL:
            o = 24 * LOCAL.index(name)
            return T.lloc[:, o + a:o + b]
        return T["l" + name][:, a:b]

    def sm(name, a=0, b=KW):
        o = 20 * SMALL.index(name)
        return T.sm[:, o + a:o + b]

    def small(out, a, b, o):
        tt(sm(out), sm(a), sm(b), o, [a, b], [out])

    def pick(out, win, off, reads, key, k, okey=None):
        take(out[:, 16 * k:C], win.indirect(off(k, KW)), C - 16 * k, reads + (both(okey)[k > 0:] if okey else []),
             both(key)[k > 0:], "s")
        if k:
            take(out[:, 0:16 * k], win.indirect(off(0, k)), 16 * k, reads + ([okey] if okey else []), [key], "v")

    def both(key):
        return [key, key + "s"]

    def scan(row, n, reads, b, pat="pat", c=0, key=None):
        o = C * SCANS.index(b) + c
        vec(lambda e: e.tensor_tensor_scan(T.cc[:, o:o + n], row, T[pat][:, c:c + n], -2 * BIG, MAX, ADD), vcost(n, 0.5), reads + [pat],
            [key or b])
        return key or b, T.cc[:, o + 15:o + n:16]

    Q0, QZ, CORR, THR, QP = [T.col[:, i:i + 1] for i in range(5)]

    def row(n, c, d):
        o = 304 * POWERS.index(n)
        return T.pw[:, o + c:o + d]

    def reach(n):
        return C if n <= NEAR[0] else UP if n <= NEAR[1] else LOW

    def zoned(key, c, d):
        return ["%s.%d" % (key, a) for a, b, z, q in TAKES if a < d and c < b]

    def base(c):
        k = 8 + [a for a, b in ZONES].index(c)
        return T.col[:, k:k + 1]

    def land(job, out, key):
        ts(out, job[1], CORR, ADD, [job[0], "corr"], [key])

    def wrap(row, key, off, okey, k, b):
        land(scan(row[:, 16 * k:C], C - 16 * k, [key + "s"], b, "pat", 16 * k, b + "s"), off(k, KW), okey + "s")
        land(scan(row[:, 0:16 * k], 16 * k, [key], b), off(0, k), okey)

    IOTA = T.ramp[:, 16:16 + CE]

    t = LOAD
    for q, to, src, key, long in (("s", T.hpl[:], T.hp, "hpl", 0.3), ("y", T.mtl[:], T.mt, "mtl", 0.3), ("s", T.ivl[:], T.iv, "ivl", 0.3),
                                  ("y", T.ut[:], T.u, "ut", 0.7), ("y", T.xin[:], T.x, "xin", 1.2), ("y", T.udl[:], T.ud, "udl", 0.3),
                                  ("y", u8(T.wq[:]), T.wc, "wq", 1.2), ("y", T.wsc[:], T.ws, "wsc", 0.5), ("y", T.vt[:], T.v, "vt", 0.7)):
        t += long * LONG
        dma(q, to, src[:], [], [key], t, "load")

    fill(T.et[:], 0.0, ["et"], 520)
    fill(T.alt[:, 0:2 * C:2], 0.0, ["alt"], C)
    unload(T.d0[:, 0:2 * C:2], T.alt[:, 0:2 * C:2], C, ["alt"], ["d0e"], "s")
    add([("s", C * CYCLE + 0.065, lambda e: e.activation(T.alt[:, 1:2 * C:2], T.alt[:, 0:2 * C:2], IDENT, bias=1.0))], ["alt"], ["alts"])
    fill(T.win[:, 2 * C:2 * CE], float(EVEN - MID), ["wine"])
    fill(T.win[:, 2 * EVEN + 1:2 * EVEN + 2], float(ODD - MID), ["wine"])
    fill(T.fl[:, C:C + 48], 0.0, ["fle"])
    fill(T.fl[:, EVEN:EVEN + 1], 1.0, ["fle"])
    fill(T.ramp[:, 15:16], float(C - 1 - MID), ["iom"])
    pool(lambda e: e.iota(T.i32[:], [[1, 32]], 1024, -1), 32, [], ["i32"])
    sooner(1.0)
    pool(lambda e: e.iota(T.qi[:], [[0, 2]], 0, 1), 2, [], ["qi"])
    count(T.ramp[:, 16:320], [[1, 304]], -MID, 304, ["iota"])
    count(T.wide[:], [[1, 2 * CE]], -CE, 2 * CE, ["wide"])
    count(sm("k16"), [[16, KW]], 0, KW, ["k16"])
    pool(lambda e: e.iota(T.uoi[:], [[16, 8]], 0, 0), 8, [], ["uoi"])
    count(sm("kb", 0, 8), [[-64, 2], [0, 4]], -64, 8, ["kb0"])
    count(sm("kb", 8, 14), [[-32, 3], [0, 2]], -160, 6, ["kb1"])
    count(sm("kb", 14, KW), [[-16, 4]], -240, 4, ["kb2"])
    for n in POWERS:
        if n % 2:
            count(row(n, C, CE), [[0, 2], [-1, 2]], ODD - MID, 4, ["h%de" % n])
        else:
            count(row(n, reach(n), CE), [[1, CE - reach(n)]], reach(n) - MID, CE - reach(n), ["h%de" % n])
    ts(QP, T.qi[:, 0:1], float(MID), SUB, ["qi"], ["qp"])
    ts(T.et[:, 3:515:4], IOTA[:, 0:128], QP, EQ, ["iota", "qp", "et"], ["et"], 0.5, MUL)
    ts(T.qi[:], T.qi[:], 15, AND, ["qi"], ["qi"])
    cp(Q0, T.qi[:, 0:1], ["qi"], ["q0"])
    ts(QZ, T.qi[:, 0:1], 0.0, EQ, ["qi"], ["qz"])
    ts(T.i32[:], T.i32[:], 15, AND, ["i32"], ["i32"])
    ts(T.pa[:], T.i32[:], 0.0, EQ, ["i32"], ["pa"], BIG, MUL)
    ts(T.pb[:], T.i32[:], 15.0, EQ, ["i32"], ["pb"], -2 * BIG, MUL)
    tt(T.pat[:, 0:32], T.pa[:], T.pb[:], ADD, ["pa", "pb"], ["pat0"])
    for a in (32, 64, 96):
        unload(T.pat[:, a:a + 32], T.pat[:, 0:32], 32, ["pat0"], ["pat%d" % a])
    unload(T.pat[:, 128:256], T.pat[:, 0:128], 64, ["pat0", "pat32", "pat64", "pat96"], ["pat128"])
    unload(T.pat[:, 256:352], T.pat[:, 0:96], 64, ["pat0", "pat32", "pat64", "pat128"], ["pat"])
    ts(CORR, QZ, 2 * BIG, MUL, ["qz"], ["corr"], MID - BIG, ADD)
    for c, d in ZONES:
        ts(base(c), QZ, 2 * BIG, MUL, ["qz"], ["base%d" % c], MID - BIG - c + 0.5, ADD)
    ts(THR, QZ, -4 * BIG, MUL, ["qz"], ["thr"], 1.5 + 2 * BIG, ADD)
    unload(T.patf[:], T.pat[:, 0:C], C, ["pat"], ["patf"], "s")
    sooner(LEADP)
    tt(T.patf[:, 15:C:16], T.pat[:, 15:C:16], sm("kb"), ADD, ["pat", "kb0", "kb1", "kb2", "patf"], ["patf"])
    ts(sm("jw"), sm("k16"), Q0, ADD, ["k16", "q0"], ["jw"])
    for b in range(4):
        quant("e", T.et[:, 3 - b:515 - b], ["et"], 128 * b, 128 * b + 128, "e%d" % b)

    TOP, END = C + 32, C + 64

    def hrow(k):
        return T.hpr[:, END:END + C] if k else T.hpr[:, 0:C]

    def hoff(k):
        return lambda a, b: T.lhp[:, k * END // 16 + a:k * END // 16 + b]

    def power(k, off, cut):
        pick(hrow(k), hrow(1 - k), hoff(off), both("hpr%d" % (1 - k)) + ["lhp%d" % off], "hpr%d" % k, cut)

    def known(k):
        s0, s1 = (TOP, END + C) if k else (0, END)
        land(scan(T.hpr[:, s0:s1], s1 - s0, both("hpr%d" % k) + ["top", "top1", "top2"], "cr"), T.lhp[:, s0 // 16:s1 // 16], "ltop")
        calls[-1]["writes"].append("lhp%d" % k)

    def places(row, off, keys, s0, s1, k0):
        take(T.oo[:, s0:s1], hrow(row).indirect(off), s1 - s0, both("hpr%d" % row) + keys, ["oo"], PLACE)
        land(scan(T.oo[:, k0:s1], s1 - k0, ["oo"], "co"), lst("ordo", k0 // 16, s1 // 16), "lordo")
        cp(T.r1[:].indirect(lst("ordo", k0 // 16, k0 // 16 + 6)), T.ramp[:, 15 + k0:15 + k0 + 96], ["iota", "iom", "lordo", "lordt"], ["r1"],
           0.05 + 3.5 * 96 * CYCLE)

    fill(T.hpr[:, C:TOP], 0.0, ["top"])
    cp(hoff(0)(0, KW), T.hpl[:], ["hpl"], ["lhp0"])
    pick(hrow(0), IOTA, hoff(0), ["iota", "lhp0"], "hpr0", CUT["ring0"])
    unload(T.hpr[:, END - 1:END], T.hpr[:, C - 1:C], 1, both("hpr0"), ["top1"])
    power(1, 0, CUT["ring0"])
    unload(T.hpr[:, END - 2:END - 1], T.hpr[:, END + C - 1:END + C], 1, both("hpr1"), ["top2"])
    take(T.hpr[:, TOP - 2:END - 2], hrow(1).indirect(hoff(0)(KW - 2, KW)), 32, both("hpr1") + ["lhp0"], ["top"], PLACE)
    power(0, 0, CUT["ring0"])
    known(0)
    for k, n in enumerate((3, 6, 12, 24)):
        power(1 - k % 2, k % 2, CUT["ring"])
        take(T.hpr[:, TOP - n:END - n], hrow(k % 2).indirect(T.lhp[:, TOP // 16:END // 16]), 32, both("hpr%d" % (k % 2)) + ["ltop"],
             ["top"], PLACE)
        known(1 - k % 2)
    power(1, 0, CUT["ring"])
    cp(lst("ordo", 15, KW), T.lhp[:, TOP // 16 - 1:END // 16], ["ltop"], ["lordt"])
    cp(T.oo[:, 240:C], T.hpr[:, TOP - 16:END], ["top"], ["ootop"])
    places(0, T.lhp[:, C // 16:END // 16], ["ltop"], 176, 240, 192)
    places(1, lst("ordo", 12, KW), ["lordo", "lordt"], 96, 192, 96)
    places(1, lst("ordo", 6, 12), ["lordo"], 0, 96, 0)
    land(scan(T.r1[:], C, ["r1"], "cg"), lst("poso"), "lposo")
    sooner(LEADR)

    cp(lst("mto"), T.mtl[:], ["mtl"], ["lmto"])
    cp(lst("iv0"), T.ivl[:], ["ivl"], ["liv0"])
    cp(sm("ivf"), T.ivl[:], ["ivl"], ["ivf"])
    pick(T.mtr, IOTA, lambda a, b: lst("mto", a, b), ["iota", "lmto"], "mtr", CUT["mates"])
    pick(T.mr, T.mtr[:], lambda a, b: lst("iv0", a, b), both("mtr") + ["liv0"], "mr", CUT["mates"])
    job = scan(T.mr[:], C, both("mr"), "cm")
    land(job, lst("mi"), "lmi")
    land(job, sm("mif"), "mif")
    tt(sm("ga"), T.ivl[:], sm("jw"), GT, ["ivl", "jw"], ["ga"])
    ts(sm("ta"), T.ivl[:], float(ODD), SUB, ["ivl"], ["ta"])
    small("na", "ga", "ta", MUL)
    ts(lst("fa"), sm("na"), float(ODD), ADD, ["na"], ["lfa"])
    take(T.win[:, 1:2 * C:2], IOTA.indirect(lst("fa")), C, ["iota", "lfa"], zoned("win", 0, C), "s")
    ts(sm("jc"), sm("jw"), CORR, SUB, ["jw", "corr"], ["jc"])
    fill(T.pair[:, 0:2 * KW:2], 0.0, ["pair0"])
    tt(T.pair[:, 1:2 * KW:2], job[1], sm("jc"), GT, ["cm", "jc"], ["pair1"])
    ts(T.pair[:, 2 * KW:4 * KW:2], job[1], CORR, ADD, ["cm", "corr"], ["pair2"], float(ODD2), SUB)
    ts(T.pair[:, 2 * KW + 1:4 * KW:2], sm("na"), -1.0, MUL, ["na"], ["pair3"], float(ODD2 - ODD), ADD)
    vec(lambda e: e.tensor_tensor_scan(T.pair[:, 4 * KW:6 * KW], T.pair[:, 0:2 * KW], T.pair[:, 2 * KW:4 * KW], 0.0, MUL, ADD), vcost(0, 1),
        ["pair%d" % i for i in range(4)], ["pair"])
    ts(lst("fb"), T.pair[:, 4 * KW + 1:6 * KW:2], float(CE), ADD, ["pair"], ["lfb"])
    cp(sm("df"), T.pair[:, 4 * KW + 1:6 * KW:2], ["pair"], ["df"])
    ts(sm("e0"), sm("na"), float(ODD), ADD, ["na", "corr"], ["e0"], CORR, SUB)
    small("di", "mif", "ivf", SUB)
    cp(lst("udo"), T.udl[:], ["udl"], ["ludo"])
    cp(sm("udf"), T.udl[:], ["udl"], ["udf"])
    take(T.uda[:], IOTA.indirect(lst("udo")), C, ["iota", "ludo"], ["uda"])
    take(T.um[:], T.uda[:].indirect(lst("mto")), C, ["uda", "lmto"], ["um"])
    land(scan(T.um[:], C, ["um"], "ce"), sm("umf"), "umf")
    small("du", "umf", "udf", SUB)

    cp(T.luo[:], T.uoi[:], ["uoi"], ["luo"])
    quant("u", T.ut[:], ["ut"], 0, 128)
    cp(T.urq[:, 0:128].bitcast(dt.uint32), T.uq[:, 0:128].bitcast(dt.uint32).indirect(T.luo[:, 0:8]), ["u", "luo"], ["urq"], gcost("v", 128))
    take(T.ursc[:, 0:128], T.usc[:, 0:128].indirect(T.luo[:, 0:8]), 128, ["u", "luo"], ["ursc"], "s")
    quant("v", T.vt[:], ["vt"], 0, 128)
    for i, (c, d) in enumerate(RUNS):
        quant("x0", T.xin[:, 4 * c:4 * d], ["xin"], c, d, both("x0")[i])

    for rd, step in enumerate(STEP):
        x, p = "x%d" % rd, "p%d" % rd
        dst = T.cores[rank ^ step]
        rel = relays(topo, core, dst)
        back = relays(topo, dst, core)
        hops = 2 if rel else 1
        first = rd == 0

        if rel:
            parts = [(rel[0], u8(T[p + "q"][:, 0:HALF]), u8(T[x + "q"][:, 0:HALF])),
                     (rel[1], u8(T[p + "q"][:, HALF:C]), u8(T[x + "q"][:, HALF:C])), (rel[0], T[p + "sc"][:], T[x + "sc"][:])]
        else:
            parts = [(dst, u8(T[p + "q"][:]), u8(T[x + "q"][:])), (dst, T[p + "sc"][:], T[x + "sc"][:])]
        nx = 2 * width(back[0], core) + width(back[1], core) if back else 2 * width(dst, core)
        send(parts, both(x), p, "rx%d" % rd, nx, CODES + (hops - 1) * (HOP + SPARE))
        if first:
            calls[-1]["behind"] = [i for i, c in enumerate(calls[:-1]) if c["ways"][0][0] == "g"]

        def mail(name, to, sem, spare=SPARE):
            send([(rel[1] if rel else dst, lst(to), lst(name))], ["l" + name], "l" + to, sem, width(back[1] if back else dst, core),
                 hops * (HOP + spare) - 0.4)

        cp(T.d1[:, 1:2 * C:2], T.win[:, 1:2 * C:2], zoned("win", 0, C), ["d1a"], vcost(C, 0.5))
        take(T.dd[:], T.wide[:].indirect(lst("fb")), C, ["wide", "lfb"], ["dd"])
        for i, (c, d) in enumerate(RUNS):
            mm(5 * i, "ur", 0, x, ["urq", "ursc", both(x)[i]], c, d)
            ts(T.pp[:, c:d], bank(5 * i, d - c), 0.0, GT, ["b%d" % (5 * i)], [both("pp")[i]], cost=vcost(d - c, 1))
        apart = TWO0 if first else TWO
        takes, scans = (TAKES, ZONES) if apart else ([h + (0, "sv") for h in HALVES], ((0, C),))
        cw = "cw%d" % rd
        for c, d in FIRST if apart else ((0, C),):
            take(T.d0[:, 2 * c + 1:2 * d:2], T.pp[:].indirect(lst("iv%d" % rd, c // 16, d // 16)), d - c,
                 both("pp") + ["liv%d" % rd, "d0e"], zoned("d0", c, d), "s")
            tt(T.d1[:, 2 * c:2 * d:2], T.pp[:].indirect(lst("mi", c // 16, d // 16)), T.dd[:, c:d], MUL, both("pp") + ["lmi", "dd"],
               zoned("d1", c, d), gcost("v", d - c))
            vec(lambda e, c=c, d=d: e.tensor_tensor_scan(T.win[:, 2 * c:2 * d], T.d0[:, 2 * c:2 * d], T.d1[:, 2 * c:2 * d], 0.0, MUL, ADD),
                vcost(2 * (d - c), 0.5), zoned("d0", c, d) + zoned("d1", c, d) + ["d0e", "d1a"], zoned("win", c, d))
        for c, d in scans:
            job = scan(T.win[:, 2 * c + 1:2 * d:2], d - c, zoned("win", c, d), cw, "pat", c)
            calls[-1]["writes"] = zoned(cw, c, d)
            ts(lst("wo", c // 16, d // 16), job[1], base(c), ADD, zoned(cw, c, d) + ["base%d" % c], zoned("lwo", c, d), 2.0, MUL)
        old = (["e0"], sm("e0")) if first else last
        def led(c, d, cw=cw):
            return T.cc[:, C * SCANS.index(cw) + c + 15:C * SCANS.index(cw) + d:16]

        last = (zoned(cw, 0, C), led(0, C))
        tt(sm("bi"), last[1], old[1], NE, last[0] + old[0], ["bi"])
        small("ti", "bi", "di", MUL)
        small("ivf", "ivf", "ti", ADD)
        cp(lst("iv%d" % (rd + 1)), sm("ivf"), ["ivf"], ["liv%d" % (rd + 1)])
        mail("iv%d" % (rd + 1), "ivp%d" % rd, "ri%d" % rd, 2 * SPARE)
        sooner(LEADI)
        if rd < 2:
            small("mif", "mif", "ti", SUB)
            cp(lst("mi"), sm("mif"), ["mif"], ["lmi"])
            small("di", "mif", "ivf", SUB)
            ts(sm("sg"), sm("bi"), -2.0, MUL, ["bi"], ["sg"], 1.0, ADD)
            small("df", "df", "sg", MUL)
            ts(lst("fb"), sm("df"), float(CE), ADD, ["df"], ["lfb"])
        take(T.r3[:], T.pp[:].indirect(lst("mto")), C, both("pp") + ["lmto"], ["r3"])
        j1 = scan(T.pp[:], C, both("pp"), "cp")
        j2 = scan(T.r3[:], C, ["r3"], "c3")
        tt(sm("t3"), j1[1], j2[1], ADD, [j1[0], j2[0]], ["t3"])
        ts(sm("bj"), sm("t3"), THR, GE, ["t3", "thr"], ["bj"])
        small("tj", "bj", "du", MUL)
        small("udf", "udf", "tj", ADD)
        cp(lst("udo"), sm("udf"), ["udf"], ["ludo"])
        sooner(LEADU)
        if rd < 2:
            small("umf", "umf", "tj", SUB)
            small("du", "umf", "udf", SUB)
        for b in range(4):
            mm(1 + b, "e", 128 * b, x, ["e%d" % b] + both(x))
            unload(pl("th", b), bank(1 + b), C, ["b%d" % (1 + b)], ["th%d" % b])
            take(pl("tu", b), pl("th", b).indirect(lst("udo")), C, ["th%d" % b, "ludo"], ["tu%d" % b])
        for b in range(4):
            k = (5, 6, 7, 0)[b]
            mm(k, "e", 128 * b, p, ["e%d" % b, p])
            unload(pl("tp", b), bank(k), C, ["b%d" % k], both("tp%d" % b))
            take(pl("gv", b), pl("tp", b).indirect(lst("ivp%d" % rd)), C, ["tp%d" % b, "livp%d" % rd], ["gv%d" % b])
        for i, (m, rows) in enumerate(PLAN0 if first else PLAN):
            def off(c, d):
                return T.lhoff[:, i * KW + c // 16:i * KW + d // 16]

            for c, d in scans:
                d = min(d, reach(rows[0]))
                if c < d and m > 1:
                    job = scan(row(m, c, d), d - c, zoned("h%d" % m, c, d), "ch", "pat", c)
                    calls[-1]["writes"] = zoned("ch", c, d)
                    ts(off(c, d), job[1], CORR, ADD, zoned("ch", c, d) + ["corr"], zoned("lh%d" % m, c, d), float(c), SUB)
                elif c < d and len(rows) > 1:
                    ts(off(c, d), led(c, d), CORR, ADD, zoned(cw, c, d) + ["corr"], zoned("lh1", c, d), float(c), SUB)
            for n in rows:
                for c, d, a, qs in takes:
                    d = min(d, reach(n))
                    qs = "sv" if n > NEAR[0] else qs
                    if c < d and n == 2:
                        take(row(n, c, d), T.win[:, 2 * a:2 * CE].indirect(lst("wo", c // 16, d // 16)), d - c,
                             zoned("win", a, C) + ["wine"] + zoned("lwo", c, d), zoned("h2", c, d), qs)
                    elif c < d:
                        take(row(n, c, d), row(n - m, a, CE).indirect(off(c, d)), d - c,
                             zoned("h%d" % (n - m), a, reach(n - m)) + ["h%de" % (n - m)] + zoned("lh%d" % m, c, d), zoned("h%d" % n, c, d), qs)
        ts(T.fl[:, C - 16:C], row(NEAR[0], C - 16, C), float(EVEN - MID), EQ, zoned("h%d" % NEAR[0], UP, C), ["fl"])
        for n, (c, d) in zip(NEAR, ZONES):
            d = min(d, C - 16)
            land(scan(row(n, c, d), d - c, zoned("h%d" % n, c, d), "cy", "patf", c, "cy%d" % n), lst("foff", c // 16, d // 16), "lfoff%d" % c)
        skip = SKIP0 if first else SKIP
        if skip:
            pick(T.r1, row(NEAR[2], 0, CE), lambda a, b: lst("ordo", a, b), zoned("h%d" % NEAR[2], 0, LOW) + ["h%de" % NEAR[2], "lordo"],
                 "r1", CUT["br"])
            wrap(T.r1, "r1", lambda a, b: lst("go", a, b), "lgo", CUT["br"], "cg")
        for z, c, d, e in FILL[:-1 if skip else None]:
            c = c // 32 * 32
            take(T.fl[:, c:d], T.fl[:, e:e + 64 if e > UP else CE].indirect(lst("foff", c // 16, d // 16)), d - c,
                 ["fl", "fle", "lfoff%d" % z], ["fl"], "vs")
        by, keys = ("go", both("lgo")) if skip else ("ordo", ["lordo"])
        add([("s", gcost("s", C), lambda e, by=by: e.activation(T.nf[:], T.fl[:, 0:CE].indirect(lst(by)), IDENT, bias=1.0, scale=-1.0))],
            ["fl", "fle"] + keys, ["nf"])
        tt(T.fo[:], T.fl[:, 0:CE].indirect(lst(by)), T.oo[:], MUL, ["fl", "fle", "oo", "ootop"] + keys, ["fo"], gcost("v", C))
        vec(lambda e: e.tensor_tensor_scan(T.sb[:], T.nf[:], T.fo[:], 0.0, MUL, ADD), vcost(C, 0.5), ["nf", "fo"], ["sb"])
        pick(T.br, T.sb[:], lambda a, b: lst("poso", a, b), ["sb", "lposo"], "br", CUT["br"])
        wrap(T.br, "br", lambda a, b: lst("bo%d" % rd, a, b), "lbo%d" % rd, CUT["br"], "cx")
        mail("bo%d" % rd, "bp%d" % rd, "rb%d" % rd, 0.0)
        calls[-1]["reads"].append("lbo%ds" % rd)
        take(T.r2[:], T.br[:].indirect(lst("ivp%d" % rd)), C, both("br") + ["livp%d" % rd], ["r2"])
        land(scan(T.r2[:], C, ["r2"], "ce"), lst("eo%d" % rd), "leo%d" % rd)
        mail("eo%d" % rd, "ep%d" % rd, "re%d" % rd)
        def mean(to, whole, win, off, other, q):
            def plane(b, c, d, keys):
                tt(T[to][:, 4 * c + b:4 * d:4], pl(win, b).indirect(lst(off, c // 16, d // 16)), pl(other, b, c, d), ADD,
                   both("%s%d" % (win, b)) + ["%s%d" % (other, b), "l" + off], keys, gcost("v", d - c))

            if whole:
                take(T[other + "3"][:, 1:2 * C:2], pl(win, 3).indirect(lst(off)), C, both(win + "3") + ["l" + off], [other + "3s"], "s")
                steps = [(0, None), (2, 0), (3, None), (2, 1), (1, 0), (1, 1), (None, 0), (None, 1)]
            else:
                steps = [(0, None), (1, None), (2, None), (3, 0), (3, 1), (None, 0), (None, 1)]
            for n, (b, i) in enumerate(steps):
                c, d = (0, C) if i is None else RUNS[i]
                if b is None:
                    quant(q, T[to][:, 4 * c:4 * d], [both("%s%d" % (to, a))[i] for a in range(4)], c, d, both(q)[i])
                elif b == 3 and whole:
                    vec(lambda e: e.tensor_tensor_scan(T[to][:, 1:4 * C:2], T.alt[:], T[other + "3"][:], 0.0, MUL, ADD), vcost(2 * C, 0.5),
                        both(other + "3") + both("alt"), both(to + "3") + both(to + "1"))
                else:
                    plane(b, c, d, both("%s%d" % (to, b)) if i is None else [both("%s%d" % (to, b))[i]])
                if n:
                    behind()

        mean("zt", True, "tp", "bp%d" % rd, "gv", "z")
        for i, (c, d) in enumerate(RUNS):
            mm(1 + 4 * i, "w", 0, "z", ["wq", "wsc", both("z")[i]], c, d)
            unload(pl("hh", 0, c, d), bank(1 + 4 * i, d - c), d - c, ["b%d" % (1 + 4 * i)], [both("hh0")[i]], "vs", 0.015625)
            sooner(0.3)
        for b in range(1, 4):
            mm(1 + b, "w", 128 * b, "z", ["wq", "wsc"] + both("z"))
            unload(pl("hh", b), bank(1 + b), C, ["b%d" % (1 + b)], both("hh%d" % b), "s", 0.015625)
            sooner(0.1 * (3 - b))
        mean("xt", False, "hh", "ep%d" % rd, "tu", "x%d" % (rd + 1))
        calls[-1]["ends"] = rd < 2

    add([("s", gcost("s", C), lambda e: e.activation(T.uof[:], IOTA.indirect(lst("udo")), COPY, bias=float(MID)))], ["iota", "ludo"], ["uof"])
    dma("y", T.uo[:], T.uof[0:128:16, :], ["uof"], [], LOAD)
    for i, (c, d) in enumerate(RUNS):
        x = both("x3")[i]
        mm(5 + i, "v", 0, "x3", ["v", x], c, d)
        unload(T.yf[:, c:d], bank(5 + i, d - c), d - c, ["b%d" % (5 + i)], ["yf%d" % i], "vs" if i else "s")
        dma("y", T.oc[:, 4 * c:4 * d], u8(T.x3q[:, c:d]), [x], [], LOAD + 1.5 - i)
        dma("s" if i else "y", T.y[:, c:d], T.yf[:, c:d], ["yf%d" % i], [], LOAD + 1.5 - i)
    for k in range(4):
        dma("ys"[k % 2], T.osc[4 * k:4 * k + 4, :], T.x3sc[32 * k:32 * k + 4, :], both("x3"), [], LOAD)

    order = arrange(calls)
    order = [c for c in calls if c["kind"] == "load"] + [c for c in order if c["kind"] != "load"]
    Q = {"v": g.vector, "s": g.scalar, "t": g.tensor, "g": g, "y": g.sync}
    SEM = {"v": "cv", "s": "cs", "t": "ct", "g": "cg"}
    cnt = {"v": 0, "s": 0, "t": 0, "g": 0}
    clock = {q: {} for q in Q}
    wr, rdr = {}, {}
    dsems = []
    for c in order:
        q = c["queue"]
        need = [wr[k] for k in c["reads"]] + [wr[k] for k in c["writes"] if k in wr]
        for k in c["writes"]:
            need += rdr.get(k, [])
        for sem, val, clk in sorted(need, key=lambda t: -t[1]):
            if clock[q].get(sem, 0) < val:
                Q[q].wait_ge(T.sem[sem], val)
                for a, b in clk.items():
                    clock[q][a] = max(clock[q].get(a, 0), b)
        i = c["call"](Q[q])
        if c["kind"] == "send":
            sem, val = c["arrive"]
            wr[c["writes"][0]] = (sem, val, {sem: val})
            continue
        if c["kind"] == "op":
            cnt[q] += 1
            sem, val = SEM[q], cnt[q]
            i.then_inc(T.sem[sem], 1)
        else:
            sem, val = "d%d" % len(dsems), 16
            dsems.append(sem)
            i.then_inc(T.sem[sem], 16)
        tok = (sem, val, dict(clock[q], **{sem: val}))
        for k in c["reads"]:
            rdr.setdefault(k, []).append(tok)
        for k in c["writes"]:
            wr[k], rdr[k] = tok, []
    for s in dsems:
        Q["y"].wait_ge(T.sem[s], 16)
    for q in ("v", "s", "t", "g"):
        g.wait_ge(T.sem[SEM[q]], cnt[q])
    g.wait_ge(T.sem.snt, sent[0])
